import numpy as np
import ml_dtypes


def mxq(x, axis, fmt="e4m3"):
    dtype, down = {"e4m3": (ml_dtypes.float8_e4m3fn, 7), "e5m2": (ml_dtypes.float8_e5m2, 14)}[fmt]
    v = np.moveaxis(np.asarray(x, np.float32).astype(ml_dtypes.bfloat16).astype(np.float64), axis, -1)
    blocks = v.reshape(v.shape[:-1] + (-1, 32))
    amax = np.abs(blocks).max(-1, keepdims=True)
    byte = np.maximum(np.where(amax > 0, np.frexp(amax)[1] - 1 + 127, 0) - down, 1)
    scale = np.exp2(byte - 127.0)
    codes = (blocks / scale).astype(np.float32).astype(dtype).astype(np.float64)
    return np.moveaxis((codes * scale).reshape(v.shape), -1, axis)


WIDE = False


def mx_kscale(k):
    if not WIDE:
        return np.ones(k)
    levels = np.array([10, -10, 5, -5, 0])
    if k % 512:
        return np.exp2(np.random.permutation(np.resize(levels, k // 32))).repeat(32)
    a = np.empty((k // 512, 16))
    for p in range(k // 512):
        a[p, :8] = np.random.permutation(np.resize(levels, 8))
        for g in range(8):
            far = levels[np.abs(levels - a[p, g]) >= 10]
            a[p, g + 8] = far[np.random.randint(len(far))]
    return np.exp2(a.ravel()).repeat(32)


def f64(x):
    return np.asarray(x).astype(np.float64)


def striped(idx):
    return np.tile(idx.reshape(-1, 16).T, (8, 1)).astype(np.uint16)


def unstriped(offs):
    return offs[:16].T.reshape(-1).astype(np.int64)


E2M1 = np.array([0.0, 0.5, 1.0, 1.5, 2.0, 3.0, 4.0, 6.0, -0.0, -0.5, -1.0, -1.5, -2.0, -3.0, -4.0, -6.0])


def pack_weight(w, fmt):
    k, n = w.shape
    w = f64(np.asarray(w, np.float32).astype(ml_dtypes.bfloat16)).reshape(k // 32, 32, n)
    amax = np.abs(w).max(1)
    if fmt == "e4m3":
        byte = np.frexp(amax)[1] - 1 + 127 - 7
    else:
        mant, ex = np.frexp(amax / 6.0)
        byte = np.where(mant > 0.5, ex, ex - 1) + 127
    byte = np.clip(np.where(amax > 0, byte, 1), 1, 254)
    scaled = (w * np.exp2(127.0 - byte)[:, None, :]).reshape(k, n).astype(np.float32)
    by_word = np.ascontiguousarray(scaled.reshape(k // 512, 128, 4, n).transpose(0, 1, 3, 2))
    if fmt == "e4m3":
        words = by_word.astype(ml_dtypes.float8_e4m3fn).view(np.uint8)
    else:
        c = by_word.astype(ml_dtypes.float4_e2m1fn).view(np.uint8) & 0xF
        words = (c[..., 0::2] | (c[..., 1::2] << 4)).reshape(k // 512, 128, 2 * n)
    return np.ascontiguousarray(words), np.ascontiguousarray(byte.astype(np.uint8).reshape(k // 512, 16, n))


def unpack_weight(words, scales, fmt):
    g, _, n = scales.shape
    words = np.ascontiguousarray(words).reshape(g, 128, n, -1)
    if fmt == "e4m3":
        vals = words.view(ml_dtypes.float8_e4m3fn).astype(np.float64)
    else:
        nib = np.empty((g, 128, n, 4), np.uint8)
        nib[..., 0::2] = words & 0xF
        nib[..., 1::2] = words >> 4
        vals = E2M1[nib]
    vals = vals * np.repeat(np.exp2(scales.astype(np.float64) - 127.0), 8, axis=1)[..., None]
    return vals.transpose(0, 1, 3, 2).reshape(g * 512, n)


def relu(v):
    return np.maximum(v, 0.0)


def d_relu(v):
    return (v > 0).astype(np.float64)


K, T, E, C, H, N = 384, 640, 2, 256, 1024, 2048


def by_expert(wq, xq):
    return np.concatenate([wq[e].T @ xq[:, e * C:(e + 1) * C] for e in range(E)], axis=1)


def setup_inputs():
    n = np.random.standard_normal
    s = mx_kscale(N)[:, None]
    u = mx_kscale(H)
    w2 = [pack_weight(m, "e2m1") for m in n((E, N, H)) / np.sqrt(N) / s[None] * u[None, None, :]]
    w1 = [pack_weight(m, "e2m1") for m in n((E, H, K)) / np.sqrt(H) / u[None, :, None]]
    w3 = [pack_weight(m, "e2m1") for m in n((E, H, K)) / np.sqrt(H) / u[None, :, None]]
    return {
        "dyT": (n((N, T)) * s).astype(np.float32),
        "a1": n((H, E * C)).astype(np.float32),
        "a3": n((H, E * C)).astype(np.float32),
        "w2_words": np.stack([m[0] for m in w2]),
        "w2_scales": np.stack([m[1] for m in w2]),
        "w1_words": np.stack([m[0] for m in w1]),
        "w1_scales": np.stack([m[1] for m in w1]),
        "w3_words": np.stack([m[0] for m in w3]),
        "w3_scales": np.stack([m[1] for m in w3]),
        "gate": np.tile(np.random.uniform(0.2, 1.0, E * C), (N, 1)).astype(np.float32),
        "offs": striped(np.random.permutation(T)[:E * C]),
    }


def reference(dyT, a1, a3, w2_words, w2_scales, w1_words, w1_scales, w3_words, w3_scales, gate, offs):
    idx = unstriped(offs)
    w2 = np.stack([unpack_weight(w2_words[e], w2_scales[e], "e2m1") for e in range(E)])
    w1 = np.stack([unpack_weight(w1_words[e], w1_scales[e], "e2m1") for e in range(E)])
    w3 = np.stack([unpack_weight(w3_words[e], w3_scales[e], "e2m1") for e in range(E)])
    gq = mxq(f64(gate) * f64(dyT)[:, idx], 0, "e4m3")
    dh = by_expert(w2, gq)
    da1 = dh * f64(a3) * d_relu(f64(a1))
    da3 = dh * relu(f64(a1))
    dx = by_expert(w1, mxq(da1, 0, "e4m3")) + by_expert(w3, mxq(da3, 0, "e4m3"))
    out = np.zeros((K, T))
    out[:, idx] = dx
    return out

@@ -1,0 +1,336 @@
+from contextlib import ExitStack
+
+import concourse.mybir as mybir
+from concourse.masks import make_identity
+
+E, C, T, K, H, N = 2, 256, 640, 384, 1024, 2048
+S = E * C
+P = 128
+NP = N // 512
+HP = H // 512
+KT = K // P
+AT = C // P
+
+FLOPS = 2 * S * N * H + 2 * 2 * S * H * K
+BYTES = 4 * (N * T + 2 * H * S + P * S + K * T) + E * (N * H + 2 * H * K) * 17 // 32 + 2 * S * 8
+
+F32 = mybir.dt.float32
+BF16 = mybir.dt.bfloat16
+I32 = mybir.dt.int32
+U32 = mybir.dt.uint32
+U16 = mybir.dt.uint16
+U8 = mybir.dt.uint8
+FP8X4 = mybir.dt.float8_e4m3fn_x4
+FP4X4 = mybir.dt.float4_e2m1fn_x4
+MULT = mybir.AluOpType.mult
+RELU = mybir.ActivationFunctionType.Relu
+SIGN = mybir.ActivationFunctionType.Sign
+
+
+def tile_moe_bdx_glu_relu_kernel(
+    tc, dyT, a1, a3, w2_words, w2_scales, w1_words, w1_scales, w3_words, w3_scales, gate, offs, out
+):
+    nc = tc.nc
+    with ExitStack() as ctx:
+        keep = ctx.enter_context(tc.tile_pool(name="keep", bufs=1))
+        dypool = ctx.enter_context(tc.tile_pool(name="dypool", bufs=4 * NP))
+        gpool = ctx.enter_context(tc.tile_pool(name="gpool", bufs=2))
+        dpool = ctx.enter_context(tc.tile_pool(name="dpool", bufs=3))
+        psum = ctx.enter_context(tc.psum_pool(name="psum", bufs=1))
+
+        offsets = keep.tile([P, S // 16], U16, name="offsets")
+        nc.sync.dma_start(offsets[:], offs)
+        gates = keep.tile([P, S], F32, name="gates")
+        nc.scalar.dma_start(gates[:], gate[0:P, :])
+
+        w2s = keep.tile([P, E * NP, H], U8, name="w2s", align_bytes=64)
+        nc.vector.memset(w2s[:].bitcast(I32), 0)
+        w13s = keep.tile([P, E * HP, 2, K], U8, name="w13s", align_bytes=64)
+        nc.vector.memset(w13s[:].bitcast(I32), 0)
+        ident = keep.tile([P, P], F32, name="ident")
+        make_identity(nc, ident[:])
+        outs = []
+        for kt in range(KT):
+            o = keep.tile([P, T], F32, name=f"out{kt}")
+            nc.gpsimd.memset(o[:], 0.0)
+            outs.append(o)
+
+        dy_rows = dyT.rearrange("(s p t) w -> s t p w", s=NP, p=P, t=4)
+        a1_rows = a1.rearrange("(s p t) j -> s p t j", s=HP, p=P, t=4)
+        a3_rows = a3.rearrange("(s p t) j -> s p t j", s=HP, p=P, t=4)
+        dy = {}
+        w2t = []
+        a1t = {}
+        mr = {}
+
+        def load_dy(s):
+            for t in range(4):
+                d = dypool.tile([P, T], F32, name="dy")
+                nc.sync.dma_start(d[:], dy_rows[s, t])
+                dy[s, t] = d
+
+        def load_w2(s):
+            w = keep.tile([P, E, 2 * H], U8, name=f"w2t{s}", align_bytes=64)
+            nc.sync.dma_start(w[:].bitcast(I32), w2_words.bitcast(I32).rearrange("e s p w -> s p e w")[s])
+            w2t.append(w)
+
+        def load_a1(e, h):
+            t1 = keep.tile([P, 4, C], F32, name=f"a1t{e}{h}")
+            nc.sync.dma_start(t1[:], a1_rows[h][:, :, C * e : C * (e + 1)])
+            a1t[e, h] = t1
+
+        def load_a3(e, h):
+            t3 = keep.tile([P, 2, 4, C], F32, name=f"mr{e}{h}")
+            nc.sync.dma_start(t3[:, 0], a3_rows[h][:, :, C * e : C * (e + 1)])
+            mr[e, h] = t3
+
+        load_dy(0)
+        load_a1(0, 0)
+        load_dy(1)
+        load_a1(0, 1)
+        load_w2(0)
+        load_dy(2)
+        w2s_rows = w2_scales.bitcast(I32).rearrange("e s f i -> f (e s) i")
+        for q in range(4):
+            nc.sync.dma_start(w2s[32 * q : 32 * q + 4].bitcast(I32), w2s_rows[4 * q : 4 * q + 4])
+        load_w2(1)
+        load_dy(3)
+        load_w2(2)
+        load_w2(3)
+        load_a3(0, 0)
+        load_a3(0, 1)
+        load_a1(1, 0)
+        load_a1(1, 1)
+        w13 = keep.tile([P, E * HP, 2, 2 * K], U8, name="w13", align_bytes=64)
+        for w, words in ((0, w1_words), (1, w3_words)):
+            nc.sync.dma_start(
+                w13[:, :, w].bitcast(I32), words.bitcast(I32).rearrange("e s p w -> p (e s) w")
+            )
+        for w, scales in ((0, w1_scales), (1, w3_scales)):
+            rows = scales.bitcast(I32).rearrange("e s f k -> f (e s) k")
+            for q in range(4):
+                nc.sync.dma_start(w13s[32 * q : 32 * q + 4, :, w].bitcast(I32), rows[4 * q : 4 * q + 4])
+
+        load_a3(1, 0)
+        load_a3(1, 1)
+
+        mask = keep.tile([P, HP, S, 4], BF16, name="mask")
+
+        def masks(h, e, half):
+            j = slice(P * half, P * half + P)
+            nc.scalar.activation(mr[e, h][:, 1, :, j], a1t[e, h][:, :, j], RELU)
+            nc.scalar.activation(
+                mask[:, h, C * e + P * half : C * e + P * half + P].rearrange("p (c i) t -> p c t i", i=4),
+                mr[e, h][:, 1, :, j].rearrange("p t (c i) -> p c t i", i=4),
+                SIGN,
+            )
+
+        gc = []
+        gs = []
+        for s in range(NP):
+            c = keep.tile([P, S], U32, name=f"gc{s}", align_bytes=64)
+            z = keep.tile([P, S], U8, name=f"gs{s}", align_bytes=64)
+            gc.append(c)
+            gs.append(z)
+
+        g4 = {}
+
+        def gather(s, t, lo, hi, weights):
+            if (s, lo) not in g4:
+                g = gpool.tile([P, 4, hi - lo], F32, name=f"g4_{hi - lo}")
+                g4[s, lo] = g
+            nc.vector.tensor_tensor(
+                g4[s, lo][:, t, :], dy[s, t][:].indirect(offsets[:, lo // 16 : hi // 16]), weights, MULT
+            )
+
+        def new_gb(width, tag, bufs):
+            return gpool.tile([P, width, 4], BF16, name=tag, bufs=bufs, align_bytes=64)
+
+        def interleave(b, s, base, lo, hi, first):
+            nc.scalar.copy(
+                b[:, lo - first : hi - first].rearrange("p (c i) t -> p c t i", i=4),
+                g4[s, base][:, :, lo - base : hi - base].rearrange("p t (c i) -> p c t i", i=4),
+            )
+
+        def quant_g(b, s, lo, hi, first):
+            nc.vector.quantize_mx(
+                out=gc[s][:, lo:hi].bitcast(FP8X4),
+                scales=gs[s][:, lo:hi],
+                in_=b[:, lo - first : hi - first].rearrange("p j t -> p (j t)"),
+            )
+
+        bank = {}
+
+        def mm1(s, e, some=range(AT)):
+            for a in some:
+                j = slice(C * e + P * a, C * e + P * a + P)
+                for h in range(HP):
+                    if s == 0:
+                        b = psum.tile([P, 512], F32, name=f"bank{e}{a}{h}")
+                        bank[e, a, h] = b
+                    nc.tensor.matmul_mx(
+                        out=bank[e, a, h][:],
+                        lhsT=gc[s][:, j].bitcast(FP8X4),
+                        lhsT_scale=gs[s][:, j],
+                        rhs=w2t[s][:, e, 1024 * h : 1024 * (h + 1)].bitcast(FP4X4),
+                        rhs_scale=w2s[:, e * NP + s, 512 * h : 512 * (h + 1)],
+                        start=(s == 0),
+                        stop=(s == NP - 1),
+                    )
+
+        def turn(e, a, h):
+            d = dpool.tile([P, 4, P], F32, name="dhs")
+            nc.scalar.copy(d[:], bank[e, a, h][:].rearrange("p (m t) -> p t m", t=4))
+            b = psum.tile([P, 4, P], F32, name=f"bank{e}{a}{h}")
+            for t in range(4):
+                nc.tensor.transpose(b[:, t, :], d[:, t, :], ident[:])
+            bank[e, a, h] = b
+
+        dq = {}
+
+        def products(e, a, h):
+            if h == 0:
+                q = dpool.tile([P, HP, 2, P, 4], BF16, name="dq", align_bytes=64)
+                dq[e, a] = q
+            j = slice(P * a, P * a + P)
+            nc.vector.tensor_tensor(
+                dq[e, a][:, h],
+                bank[e, a, h][:].rearrange("p t j -> p j t").unsqueeze(1).to_broadcast([P, 2, P, 4]),
+                mr[e, h][:, :, :, j].rearrange("p w t j -> p w j t"),
+                MULT,
+            )
+
+        def masked(e, a):
+            j = slice(C * e + P * a, C * e + P * a + P)
+            m = dq[e, a][:, :, 0]
+            nc.vector.tensor_tensor(m, m, mask[:, :, j], MULT)
+
+        dc = {}
+
+        def quant_d(e, a):
+            c = dpool.tile([P, HP * 2 * P], U32, name="dc", align_bytes=64)
+            z = dpool.tile([P, HP * 2 * P], U8, name="ds", align_bytes=64)
+            nc.vector.quantize_mx(
+                out=c[:].bitcast(FP8X4), scales=z[:], in_=dq[e, a][:].rearrange("p h w j t -> p (h w j t)")
+            )
+            dc[e, a] = (c, z)
+
+        dxs = []
+        for e in range(E):
+            d = keep.tile([P, KT, C], F32, name=f"dxs{e}")
+            dxs.append(d)
+
+        def mm2(e, a):
+            c, z = dc[e, a]
+            b = psum.tile([P, KT, P], F32, name=f"bank{e}{a}0")
+            for kt in range(KT):
+                for h in range(HP):
+                    for w in range(2):
+                        r = slice(P * (2 * h + w), P * (2 * h + w + 1))
+                        nc.tensor.matmul_mx(
+                            out=b[:, kt],
+                            lhsT=w13[:, e * HP + h, w, 2 * P * kt : 2 * P * (kt + 1)].bitcast(FP4X4),
+                            lhsT_scale=w13s[:, e * HP + h, w, P * kt : P * (kt + 1)],
+                            rhs=c[:, r].bitcast(FP8X4),
+                            rhs_scale=z[:, r],
+                            start=(h == 0 and w == 0),
+                            stop=(h == HP - 1 and w == 1),
+                        )
+            nc.scalar.copy(dxs[e][:, :, P * a : P * (a + 1)], b[:])
+
+        def scatter(e, kt):
+            nc.vector.tensor_copy(
+                outs[kt][:].indirect(offsets[:, C // 16 * e : C // 16 * (e + 1)]), dxs[e][:, kt, :]
+            )
+
+        gx = gpool.tile([P, C], F32, name="gx", bufs=1)
+        nc.scalar.copy(gx[:], gates[:, 0:C])
+        gb = {}
+        gb = {}
+        for s in range(2):
+            for t in range(4):
+                gather(s, t, 0, S, gates[:])
+                if t == 2 and s > 0:
+                    quant_g(gb[s - 1], s - 1, 0, S, 0)
+                    mm1(s - 1, 0)
+                    mm1(s - 1, 1)
+            gb[s] = new_gb(S, "gb", 2)
+            interleave(gb[s], s, 0, 0, S, 0)
+            masks(s, 0, 0)
+            masks(s, 0, 1)
+        for t in range(4):
+            gather(2, t, 0, C, gx[:])
+        quant_g(gb[1], 1, 0, S, 0)
+        mm1(1, 0)
+        mm1(1, 1)
+        b2 = new_gb(C, "gb2", 1)
+        interleave(b2, 2, 0, 0, C, 0)
+        for t in range(4):
+            gather(3, t, 0, C, gx[:])
+            if t == 2:
+                quant_g(b2, 2, 0, C, 0)
+                mm1(2, 0)
+        b3 = new_gb(C, "gb3", 1)
+        for a in range(AT):
+            interleave(b3, 3, 0, P * a, P * (a + 1), 0)
+        gx = gpool.tile([P, C], F32, name="gx", bufs=1)
+        nc.vector.tensor_copy(gx[:], gates[:, C:S])
+        gather(2, 0, C, S, gx[:])
+        gather(2, 1, C, S, gx[:])
+        quant_g(b3, 3, 0, P, 0)
+        mm1(3, 0, (0,))
+        quant_g(b3, 3, P, C, 0)
+        mm1(3, 0, (1,))
+        gather(2, 2, C, S, gx[:])
+        gather(2, 3, C, S, gx[:])
+        turn(0, 0, 0)
+        turn(0, 0, 1)
+        b2 = new_gb(C, "gb3", 1)
+        interleave(b2, 2, C, C, S, C)
+        gather(3, 0, C, S, gx[:])
+        gather(3, 1, C, S, gx[:])
+        turn(0, 1, 0)
+        turn(0, 1, 1)
+        gather(3, 2, C, S, gx[:])
+        quant_g(b2, 2, C, S, C)
+        mm1(2, 1)
+        gather(3, 3, C, S, gx[:])
+        b3 = new_gb(C, "gb3", 1)
+        for a in range(AT):
+            interleave(b3, 3, C, C + P * a, C + P * (a + 1), C)
+        products(0, 0, 0)
+        quant_g(b3, 3, C, C + P, C)
+        mm1(3, 1, (0,))
+        products(0, 0, 1)
+        quant_g(b3, 3, C + P, S, C)
+        mm1(3, 1, (1,))
+        for a in range(AT):
+            for h in range(HP):
+                turn(1, a, h)
+        for a in range(AT):
+            for h in range(HP):
+                masks(h, 1, a)
+        products(0, 1, 0)
+        masked(0, 0)
+        products(0, 1, 1)
+        quant_d(0, 0)
+        mm2(0, 0)
+        products(1, 0, 0)
+        masked(0, 1)
+        products(1, 0, 1)
+        quant_d(0, 1)
+        mm2(0, 1)
+        products(1, 1, 0)
+        masked(1, 0)
+        products(1, 1, 1)
+        quant_d(1, 0)
+        mm2(1, 0)
+        masked(1, 1)
+        scatter(0, 0)
+        quant_d(1, 1)
+        mm2(1, 1)
+        scatter(0, 1)
+        scatter(0, 2)
+        for kt in range(KT):
+            scatter(1, kt)
+            nc.sync.dma_start(out[P * kt : P * (kt + 1), :], outs[kt][:])

@@ -43,8 +43,11 @@ def tile_moe_bdx_glu_relu_kernel(
         gates = keep.tile([P, S], F32, name="gates")
         nc.scalar.dma_start(gates[:], gate[0:P, :])
 
-        w2s = keep.tile([P, E * NP, H], U8, name="w2s", align_bytes=64)
-        nc.vector.memset(w2s[:].bitcast(I32), 0)
+        w2s = []
+        for e in range(E):
+            plane = keep.tile([P, NP, H], U8, name=f"w2s{e}", align_bytes=64)
+            nc.vector.memset(plane[:].bitcast(I32), 0)
+            w2s.append(plane)
         w13s = keep.tile([P, E * HP, 2, K], U8, name="w13s", align_bytes=64)
         nc.vector.memset(w13s[:].bitcast(I32), 0)
         ident = keep.tile([P, P], F32, name="ident")
@@ -59,7 +62,7 @@ def tile_moe_bdx_glu_relu_kernel(
         a1_rows = a1.rearrange("(s p t) j -> s p t j", s=HP, p=P, t=4)
         a3_rows = a3.rearrange("(s p t) j -> s p t j", s=HP, p=P, t=4)
         dy = {}
-        w2t = []
+        w2t = {}
         a1t = {}
         mr = {}
 
@@ -69,10 +72,16 @@ def tile_moe_bdx_glu_relu_kernel(
                 nc.sync.dma_start(d[:], dy_rows[s, t])
                 dy[s, t] = d
 
-        def load_w2(s):
-            w = keep.tile([P, E, 2 * H], U8, name=f"w2t{s}", align_bytes=64)
-            nc.sync.dma_start(w[:].bitcast(I32), w2_words.bitcast(I32).rearrange("e s p w -> s p e w")[s])
-            w2t.append(w)
+        def load_w2(e, s):
+            w = keep.tile([P, 2 * H], U8, name=f"w2t{e}{s}", align_bytes=64)
+            nc.sync.dma_start(w[:].bitcast(I32), w2_words.bitcast(I32)[e, s])
+            w2t[e, s] = w
+
+        w2s_rows = w2_scales.bitcast(I32).rearrange("e s f i -> f e s i")
+
+        def load_w2s(e):
+            for q in range(4):
+                nc.sync.dma_start(w2s[e][32 * q : 32 * q + 4].bitcast(I32), w2s_rows[4 * q : 4 * q + 4, e])
 
         def load_a1(e, h):
             t1 = keep.tile([P, 4, C], F32, name=f"a1t{e}{h}")
@@ -88,19 +97,18 @@ def tile_moe_bdx_glu_relu_kernel(
         load_a1(0, 0)
         load_dy(1)
         load_a1(0, 1)
-        load_w2(0)
         load_dy(2)
-        w2s_rows = w2_scales.bitcast(I32).rearrange("e s f i -> f (e s) i")
-        for q in range(4):
-            nc.sync.dma_start(w2s[32 * q : 32 * q + 4].bitcast(I32), w2s_rows[4 * q : 4 * q + 4])
-        load_w2(1)
+        load_w2s(0)
+        load_w2(0, 0)
+        load_w2(0, 1)
         load_dy(3)
-        load_w2(2)
-        load_w2(3)
+        load_w2(0, 2)
+        load_w2(0, 3)
         load_a3(0, 0)
         load_a3(0, 1)
-        load_a1(1, 0)
-        load_a1(1, 1)
+        load_w2s(1)
+        for s in range(NP):
+            load_w2(1, s)
         w13 = keep.tile([P, E * HP, 2, 2 * K], U8, name="w13", align_bytes=64)
         for w, words in ((0, w1_words), (1, w3_words)):
             nc.sync.dma_start(
@@ -111,8 +119,9 @@ def tile_moe_bdx_glu_relu_kernel(
             for q in range(4):
                 nc.sync.dma_start(w13s[32 * q : 32 * q + 4, :, w].bitcast(I32), rows[4 * q : 4 * q + 4])
 
-        load_a3(1, 0)
-        load_a3(1, 1)
+        for h in range(HP):
+            load_a1(1, h)
+            load_a3(1, h)
 
         mask = keep.tile([P, HP, S, 4], BF16, name="mask")
 
@@ -125,19 +134,16 @@ def tile_moe_bdx_glu_relu_kernel(
                 SIGN,
             )
 
-        gc = []
-        gs = []
-        for s in range(NP):
-            c = keep.tile([P, S], U32, name=f"gc{s}", align_bytes=64)
-            z = keep.tile([P, S], U8, name=f"gs{s}", align_bytes=64)
-            gc.append(c)
-            gs.append(z)
-
+        gc = {}
+        gs = {}
         g4 = {}
 
-        def gather(s, t, lo, hi, weights):
+        def gather(s, t, lo, hi, weights, tag=None):
             if (s, lo) not in g4:
-                g = gpool.tile([P, 4, hi - lo], F32, name=f"g4_{hi - lo}")
+                if tag is None:
+                    g = gpool.tile([P, 4, hi - lo], F32, name=f"g4_{hi - lo}")
+                else:
+                    g = keep.tile([P, 4, hi - lo], F32, name=tag, align_bytes=64)
                 g4[s, lo] = g
             nc.vector.tensor_tensor(
                 g4[s, lo][:, t, :], dy[s, t][:].indirect(offsets[:, lo // 16 : hi // 16]), weights, MULT
@@ -152,10 +158,19 @@ def tile_moe_bdx_glu_relu_kernel(
                 g4[s, base][:, :, lo - base : hi - base].rearrange("p t (c i) -> p c t i", i=4),
             )
 
-        def quant_g(b, s, lo, hi, first):
+        def new_codes(s, lo, hi, tag):
+            c = keep.tile([P, hi - lo], U32, name=f"gc{s}_{lo}", align_bytes=64)
+            z = keep.tile([P, hi - lo], U8, name=tag, align_bytes=64)
+            for a in range(lo // P, hi // P):
+                gc[s, a] = c[:, P * a - lo : P * (a + 1) - lo]
+                gs[s, a] = z[:, P * a - lo : P * (a + 1) - lo]
+            return c, z
+
+        def quant_g(b, s, lo, hi, first, tag=None):
+            c, z = new_codes(s, lo, hi, f"gs{s}_{lo}" if tag is None else tag)
             nc.vector.quantize_mx(
-                out=gc[s][:, lo:hi].bitcast(FP8X4),
-                scales=gs[s][:, lo:hi],
+                out=c[:].bitcast(FP8X4),
+                scales=z[:],
                 in_=b[:, lo - first : hi - first].rearrange("p j t -> p (j t)"),
             )
 
@@ -163,23 +178,25 @@ def tile_moe_bdx_glu_relu_kernel(
 
         def mm1(s, e, some=range(AT)):
             for a in some:
-                j = slice(C * e + P * a, C * e + P * a + P)
                 for h in range(HP):
                     if s == 0:
                         b = psum.tile([P, 512], F32, name=f"bank{e}{a}{h}")
                         bank[e, a, h] = b
                     nc.tensor.matmul_mx(
                         out=bank[e, a, h][:],
-                        lhsT=gc[s][:, j].bitcast(FP8X4),
-                        lhsT_scale=gs[s][:, j],
-                        rhs=w2t[s][:, e, 1024 * h : 1024 * (h + 1)].bitcast(FP4X4),
-                        rhs_scale=w2s[:, e * NP + s, 512 * h : 512 * (h + 1)],
+                        lhsT=gc[s, AT * e + a].bitcast(FP8X4),
+                        lhsT_scale=gs[s, AT * e + a],
+                        rhs=w2t[e, s][:, 1024 * h : 1024 * (h + 1)].bitcast(FP4X4),
+                        rhs_scale=w2s[e][:, s, 512 * h : 512 * (h + 1)],
                         start=(s == 0),
                         stop=(s == NP - 1),
                     )
 
-        def turn(e, a, h):
-            d = dpool.tile([P, 4, P], F32, name="dhs")
+        def turn(e, a, h, tag=None):
+            if tag is None:
+                d = dpool.tile([P, 4, P], F32, name="dhs")
+            else:
+                d = keep.tile([P, 4, P], F32, name=tag, align_bytes=64)
             nc.scalar.copy(d[:], bank[e, a, h][:].rearrange("p (m t) -> p t m", t=4))
             b = psum.tile([P, 4, P], F32, name=f"bank{e}{a}{h}")
             for t in range(4):
@@ -238,72 +255,61 @@ def tile_moe_bdx_glu_relu_kernel(
                         )
             nc.scalar.copy(dxs[e][:, :, P * a : P * (a + 1)], b[:])
 
-        def scatter(e, kt):
+        def scatter(e, a, kt):
+            lo = (C * e + P * a) // 16
             nc.vector.tensor_copy(
-                outs[kt][:].indirect(offsets[:, C // 16 * e : C // 16 * (e + 1)]), dxs[e][:, kt, :]
+                outs[kt][:].indirect(offsets[:, lo : lo + P // 16]), dxs[e][:, kt, P * a : P * (a + 1)]
             )
 
-        gx = gpool.tile([P, C], F32, name="gx", bufs=1)
-        nc.scalar.copy(gx[:], gates[:, 0:C])
+        gxa = keep.tile([P, C], F32, name="slot_a", align_bytes=64)
+        nc.scalar.copy(gxa[:], gates[:, 0:C])
+        gxb = keep.tile([P, C], F32, name="slot_b", align_bytes=64)
+        nc.scalar.copy(gxb[:], gates[:, 0:C])
         gb = {}
-        gb = {}
-        for s in range(2):
+        for s in range(3):
             for t in range(4):
                 gather(s, t, 0, S, gates[:])
                 if t == 2 and s > 0:
                     quant_g(gb[s - 1], s - 1, 0, S, 0)
                     mm1(s - 1, 0)
-                    mm1(s - 1, 1)
-            gb[s] = new_gb(S, "gb", 2)
-            interleave(gb[s], s, 0, 0, S, 0)
-            masks(s, 0, 0)
-            masks(s, 0, 1)
-        for t in range(4):
-            gather(2, t, 0, C, gx[:])
-        quant_g(gb[1], 1, 0, S, 0)
-        mm1(1, 0)
-        mm1(1, 1)
-        b2 = new_gb(C, "gb2", 1)
-        interleave(b2, 2, 0, 0, C, 0)
-        for t in range(4):
-            gather(3, t, 0, C, gx[:])
-            if t == 2:
-                quant_g(b2, 2, 0, C, 0)
-                mm1(2, 0)
+            if s < 2:
+                gb[s] = new_gb(S, "gb", 2)
+                interleave(gb[s], s, 0, 0, S, 0)
+                masks(s, 0, 0)
+                masks(s, 0, 1)
+        b20 = new_gb(C, "gb20", 1)
+        interleave(b20, 2, 0, 0, C, 0)
+        b21 = keep.tile([P, C, 4], BF16, name="slot_c", align_bytes=64)
+        interleave(b21, 2, 0, C, S, C)
+        gather(3, 0, 0, C, gxa[:])
+        gather(3, 1, 0, C, gxa[:])
+        quant_g(b20, 2, 0, C, 0, "slot_a")
+        mm1(2, 0)
+        gather(3, 2, 0, C, gxb[:])
+        gather(3, 3, 0, C, gxb[:])
         b3 = new_gb(C, "gb3", 1)
         for a in range(AT):
             interleave(b3, 3, 0, P * a, P * (a + 1), 0)
-        gx = gpool.tile([P, C], F32, name="gx", bufs=1)
-        nc.vector.tensor_copy(gx[:], gates[:, C:S])
-        gather(2, 0, C, S, gx[:])
-        gather(2, 1, C, S, gx[:])
+        quant_g(b21, 2, C, S, C, "slot_b")
+        gather(3, 0, C, S, gates[:, C:S], "slot_c")
+        gather(3, 1, C, S, gates[:, C:S])
         quant_g(b3, 3, 0, P, 0)
         mm1(3, 0, (0,))
+        gather(3, 2, C, S, gates[:, C:S])
         quant_g(b3, 3, P, C, 0)
         mm1(3, 0, (1,))
-        gather(2, 2, C, S, gx[:])
-        gather(2, 3, C, S, gx[:])
+        gather(3, 3, C, S, gates[:, C:S])
         turn(0, 0, 0)
         turn(0, 0, 1)
-        b2 = new_gb(C, "gb3", 1)
-        interleave(b2, 2, C, C, S, C)
-        gather(3, 0, C, S, gx[:])
-        gather(3, 1, C, S, gx[:])
         turn(0, 1, 0)
-        turn(0, 1, 1)
-        gather(3, 2, C, S, gx[:])
-        quant_g(b2, 2, C, S, C)
-        mm1(2, 1)
-        gather(3, 3, C, S, gx[:])
-        b3 = new_gb(C, "gb3", 1)
-        for a in range(AT):
-            interleave(b3, 3, C, C + P * a, C + P * (a + 1), C)
+        turn(0, 1, 1, "slot_d")
+        b31 = keep.tile([P, C, 4], BF16, name="slot_d", align_bytes=64)
+        interleave(b31, 3, C, C, S, C)
         products(0, 0, 0)
-        quant_g(b3, 3, C, C + P, C)
-        mm1(3, 1, (0,))
         products(0, 0, 1)
-        quant_g(b3, 3, C + P, S, C)
-        mm1(3, 1, (1,))
+        quant_g(b31, 3, C, S, C)
+        for s in range(NP):
+            mm1(s, 1)
         for a in range(AT):
             for h in range(HP):
                 turn(1, a, h)
@@ -315,22 +321,25 @@ def tile_moe_bdx_glu_relu_kernel(
         products(0, 1, 1)
         quant_d(0, 0)
         mm2(0, 0)
-        products(1, 0, 0)
         masked(0, 1)
-        products(1, 0, 1)
         quant_d(0, 1)
         mm2(0, 1)
+        for a in range(AT):
+            for kt in range(KT):
+                scatter(0, a, kt)
+        products(1, 0, 0)
+        products(1, 0, 1)
         products(1, 1, 0)
         masked(1, 0)
         products(1, 1, 1)
         quant_d(1, 0)
         mm2(1, 0)
         masked(1, 1)
-        scatter(0, 0)
+        scatter(1, 0, 0)
         quant_d(1, 1)
         mm2(1, 1)
-        scatter(0, 1)
-        scatter(0, 2)
+        scatter(1, 0, 1)
+        scatter(1, 0, 2)
         for kt in range(KT):
-            scatter(1, kt)
+            scatter(1, 1, kt)
             nc.sync.dma_start(out[P * kt : P * (kt + 1), :], outs[kt][:])

@@ -33,7 +33,6 @@ def tile_moe_bdx_glu_relu_kernel(
     nc = tc.nc
     with ExitStack() as ctx:
         keep = ctx.enter_context(tc.tile_pool(name="keep", bufs=1))
-        dypool = ctx.enter_context(tc.tile_pool(name="dypool", bufs=4 * NP))
         gpool = ctx.enter_context(tc.tile_pool(name="gpool", bufs=2))
         dpool = ctx.enter_context(tc.tile_pool(name="dpool", bufs=3))
         psum = ctx.enter_context(tc.psum_pool(name="psum", bufs=1))
@@ -64,11 +63,11 @@ def tile_moe_bdx_glu_relu_kernel(
         dy = {}
         w2t = {}
         a1t = {}
-        mr = {}
+        a3t = {}
 
         def load_dy(s):
             for t in range(4):
-                d = dypool.tile([P, T], F32, name="dy")
+                d = keep.tile([P, T], F32, name=f"dy{s}{t}", align_bytes=64)
                 nc.sync.dma_start(d[:], dy_rows[s, t])
                 dy[s, t] = d
 
@@ -89,9 +88,9 @@ def tile_moe_bdx_glu_relu_kernel(
             a1t[e, h] = t1
 
         def load_a3(e, h):
-            t3 = keep.tile([P, 2, 4, C], F32, name=f"mr{e}{h}")
-            nc.sync.dma_start(t3[:, 0], a3_rows[h][:, :, C * e : C * (e + 1)])
-            mr[e, h] = t3
+            t3 = keep.tile([P, 4, C], F32, name=f"a3t{e}{h}")
+            nc.sync.dma_start(t3[:], a3_rows[h][:, :, C * e : C * (e + 1)])
+            a3t[e, h] = t3
 
         load_dy(0)
         load_a1(0, 0)
@@ -123,16 +122,22 @@ def tile_moe_bdx_glu_relu_kernel(
             load_a1(1, h)
             load_a3(1, h)
 
-        mask = keep.tile([P, HP, S, 4], BF16, name="mask")
+        mask = {}
+        relu1 = {}
 
-        def masks(h, e, half):
-            j = slice(P * half, P * half + P)
-            nc.scalar.activation(mr[e, h][:, 1, :, j], a1t[e, h][:, :, j], RELU)
+        def masks(h, e, a):
+            j = slice(P * a, P * a + P)
+            if (e, a) not in mask:
+                m = keep.tile([P, HP, P, 4], BF16, name=f"mask{e}{a}", align_bytes=64)
+                mask[e, a] = m
+            r = keep.tile([P, P, 4], F32, name=f"relu{e}{h}{a}")
+            relu1[e, h, a] = r
             nc.scalar.activation(
-                mask[:, h, C * e + P * half : C * e + P * half + P].rearrange("p (c i) t -> p c t i", i=4),
-                mr[e, h][:, 1, :, j].rearrange("p t (c i) -> p c t i", i=4),
-                SIGN,
+                r[:].rearrange("p (c i) t -> p c t i", i=4),
+                a1t[e, h][:, :, j].rearrange("p t (c i) -> p c t i", i=4),
+                RELU,
             )
+            nc.scalar.activation(mask[e, a][:, h], r[:], SIGN)
 
         gc = {}
         gs = {}
@@ -205,22 +210,27 @@ def tile_moe_bdx_glu_relu_kernel(
 
         dq = {}
 
-        def products(e, a, h):
-            if h == 0:
-                q = dpool.tile([P, HP, 2, P, 4], BF16, name="dq", align_bytes=64)
-                dq[e, a] = q
+        def new_dq(e, a, tag):
+            q = keep.tile([P, 2, HP, P, 4], BF16, name=tag, align_bytes=64)
+            dq[e, a] = q
+
+        def prod1(e, a, h):
             j = slice(P * a, P * a + P)
             nc.vector.tensor_tensor(
-                dq[e, a][:, h],
-                bank[e, a, h][:].rearrange("p t j -> p j t").unsqueeze(1).to_broadcast([P, 2, P, 4]),
-                mr[e, h][:, :, :, j].rearrange("p w t j -> p w j t"),
+                dq[e, a][:, 0, h].rearrange("p (c i) t -> p c t i", i=2),
+                bank[e, a, h][:].rearrange("p t (c i) -> p c t i", i=2),
+                a3t[e, h][:, :, j].rearrange("p t (c i) -> p c t i", i=2),
                 MULT,
             )
 
+        def prod3(e, a, h):
+            nc.vector.tensor_tensor(
+                dq[e, a][:, 1, h], bank[e, a, h][:].rearrange("p t j -> p j t"), relu1[e, h, a][:], MULT
+            )
+
         def masked(e, a):
-            j = slice(C * e + P * a, C * e + P * a + P)
-            m = dq[e, a][:, :, 0]
-            nc.vector.tensor_tensor(m, m, mask[:, :, j], MULT)
+            m = dq[e, a][:, 0]
+            nc.vector.tensor_tensor(m, m, mask[e, a][:], MULT)
 
         dc = {}
 
@@ -228,22 +238,19 @@ def tile_moe_bdx_glu_relu_kernel(
             c = dpool.tile([P, HP * 2 * P], U32, name="dc", align_bytes=64)
             z = dpool.tile([P, HP * 2 * P], U8, name="ds", align_bytes=64)
             nc.vector.quantize_mx(
-                out=c[:].bitcast(FP8X4), scales=z[:], in_=dq[e, a][:].rearrange("p h w j t -> p (h w j t)")
+                out=c[:].bitcast(FP8X4), scales=z[:], in_=dq[e, a][:].rearrange("p w h j t -> p (w h j t)")
             )
             dc[e, a] = (c, z)
 
-        dxs = []
-        for e in range(E):
-            d = keep.tile([P, KT, C], F32, name=f"dxs{e}")
-            dxs.append(d)
+        dxs = {}
 
-        def mm2(e, a):
+        def mm2(e, a, tag):
             c, z = dc[e, a]
             b = psum.tile([P, KT, P], F32, name=f"bank{e}{a}0")
             for kt in range(KT):
                 for h in range(HP):
                     for w in range(2):
-                        r = slice(P * (2 * h + w), P * (2 * h + w + 1))
+                        r = slice(P * (HP * w + h), P * (HP * w + h + 1))
                         nc.tensor.matmul_mx(
                             out=b[:, kt],
                             lhsT=w13[:, e * HP + h, w, 2 * P * kt : 2 * P * (kt + 1)].bitcast(FP4X4),
@@ -253,12 +260,14 @@ def tile_moe_bdx_glu_relu_kernel(
                             start=(h == 0 and w == 0),
                             stop=(h == HP - 1 and w == 1),
                         )
-            nc.scalar.copy(dxs[e][:, :, P * a : P * (a + 1)], b[:])
+            d = keep.tile([P, KT, P], F32, name=tag, align_bytes=64)
+            nc.scalar.copy(d[:], b[:])
+            dxs[e, a] = d
 
         def scatter(e, a, kt):
             lo = (C * e + P * a) // 16
             nc.vector.tensor_copy(
-                outs[kt][:].indirect(offsets[:, lo : lo + P // 16]), dxs[e][:, kt, P * a : P * (a + 1)]
+                outs[kt][:].indirect(offsets[:, lo : lo + P // 16]), dxs[e, a][:, kt]
             )
 
         gxa = keep.tile([P, C], F32, name="slot_a", align_bytes=64)
@@ -270,7 +279,7 @@ def tile_moe_bdx_glu_relu_kernel(
             for t in range(4):
                 gather(s, t, 0, S, gates[:])
                 if t == 2 and s > 0:
-                    quant_g(gb[s - 1], s - 1, 0, S, 0)
+                    quant_g(gb[s - 1], s - 1, 0, C, 0)
                     mm1(s - 1, 0)
             if s < 2:
                 gb[s] = new_gb(S, "gb", 2)
@@ -292,21 +301,27 @@ def tile_moe_bdx_glu_relu_kernel(
             interleave(b3, 3, 0, P * a, P * (a + 1), 0)
         quant_g(b21, 2, C, S, C, "slot_b")
         gather(3, 0, C, S, gates[:, C:S], "slot_c")
-        gather(3, 1, C, S, gates[:, C:S])
         quant_g(b3, 3, 0, P, 0)
         mm1(3, 0, (0,))
-        gather(3, 2, C, S, gates[:, C:S])
+        gather(3, 1, C, S, gates[:, C:S])
         quant_g(b3, 3, P, C, 0)
         mm1(3, 0, (1,))
+        gather(3, 2, C, S, gates[:, C:S])
+        quant_g(gb[1], 1, C, S, 0, "dy31")
         gather(3, 3, C, S, gates[:, C:S])
+        quant_g(gb[0], 0, C, S, 0, "dy32")
         turn(0, 0, 0)
         turn(0, 0, 1)
         turn(0, 1, 0)
         turn(0, 1, 1, "slot_d")
         b31 = keep.tile([P, C, 4], BF16, name="slot_d", align_bytes=64)
         interleave(b31, 3, C, C, S, C)
-        products(0, 0, 0)
-        products(0, 0, 1)
+        new_dq(0, 0, "dq00")
+        prod1(0, 0, 0)
+        prod1(0, 0, 1)
+        prod3(0, 0, 0)
+        masked(0, 0)
+        prod3(0, 0, 1)
         quant_g(b31, 3, C, S, C)
         for s in range(NP):
             mm1(s, 1)
@@ -316,30 +331,40 @@ def tile_moe_bdx_glu_relu_kernel(
         for a in range(AT):
             for h in range(HP):
                 masks(h, 1, a)
-        products(0, 1, 0)
-        masked(0, 0)
-        products(0, 1, 1)
+        new_dq(0, 1, "mask00")
+        prod1(0, 1, 0)
         quant_d(0, 0)
-        mm2(0, 0)
+        mm2(0, 0, "dx00")
+        prod1(0, 1, 1)
+        prod3(0, 1, 0)
         masked(0, 1)
+        prod3(0, 1, 1)
+        scatter(0, 0, 0)
         quant_d(0, 1)
-        mm2(0, 1)
-        for a in range(AT):
-            for kt in range(KT):
-                scatter(0, a, kt)
-        products(1, 0, 0)
-        products(1, 0, 1)
-        products(1, 1, 0)
+        mm2(0, 1, "dx01")
+        scatter(0, 0, 1)
+        scatter(0, 0, 2)
+        new_dq(1, 0, "dq10")
+        prod1(1, 0, 0)
+        prod1(1, 0, 1)
+        prod3(1, 0, 0)
         masked(1, 0)
-        products(1, 1, 1)
+        prod3(1, 0, 1)
+        new_dq(1, 1, "mask10")
+        prod1(1, 1, 0)
         quant_d(1, 0)
-        mm2(1, 0)
+        prod1(1, 1, 1)
+        prod3(1, 1, 0)
         masked(1, 1)
-        scatter(1, 0, 0)
+        mm2(1, 0, "mask11")
+        prod3(1, 1, 1)
+        scatter(0, 1, 0)
         quant_d(1, 1)
-        mm2(1, 1)
-        scatter(1, 0, 1)
-        scatter(1, 0, 2)
+        mm2(1, 1, "dx11")
+        scatter(0, 1, 1)
+        scatter(0, 1, 2)
+        for kt in range(KT):
+            scatter(1, 0, kt)
         for kt in range(KT):
             scatter(1, 1, kt)
             nc.sync.dma_start(out[P * kt : P * (kt + 1), :], outs[kt][:])

@@ -78,9 +78,20 @@ def tile_moe_bdx_glu_relu_kernel(
 
         w2s_rows = w2_scales.bitcast(I32).rearrange("e s f i -> f e s i")
 
-        def load_w2s(e):
-            for q in range(4):
-                nc.sync.dma_start(w2s[e][32 * q : 32 * q + 4].bitcast(I32), w2s_rows[4 * q : 4 * q + 4, e])
+        def load_w2s(e, q):
+            nc.sync.dma_start(w2s[e][32 * q : 32 * q + 4].bitcast(I32), w2s_rows[4 * q : 4 * q + 4, e])
+
+        w13 = {}
+
+        def load_w13(e, w):
+            t = keep.tile([P, HP, 2 * K], U8, name=f"w13_{e}{w}", align_bytes=64)
+            words = (w1_words, w3_words)[w]
+            nc.sync.dma_start(t[:].bitcast(I32), words.bitcast(I32).rearrange("e s p w -> e p s w")[e])
+            w13[e, w] = t
+
+        def load_w13s(w, q):
+            rows = (w1_scales, w3_scales)[w].bitcast(I32).rearrange("e s f k -> f (e s) k")
+            nc.sync.dma_start(w13s[32 * q : 32 * q + 4, :, w].bitcast(I32), rows[4 * q : 4 * q + 4])
 
         def load_a1(e, h):
             t1 = keep.tile([P, 4, C], F32, name=f"a1t{e}{h}")
@@ -92,45 +103,46 @@ def tile_moe_bdx_glu_relu_kernel(
             nc.sync.dma_start(t3[:], a3_rows[h][:, :, C * e : C * (e + 1)])
             a3t[e, h] = t3
 
+        late_order = (2, 1, 0, 3)
         load_dy(0)
         load_a1(0, 0)
         load_dy(1)
         load_a1(0, 1)
         load_dy(2)
-        load_w2s(0)
+        for q in range(4):
+            load_w2s(0, q)
         load_w2(0, 0)
         load_w2(0, 1)
         load_dy(3)
-        load_w2(0, 2)
-        load_w2(0, 3)
-        load_a3(0, 0)
-        load_a3(0, 1)
-        load_w2s(1)
-        for s in range(NP):
-            load_w2(1, s)
-        w13 = keep.tile([P, E * HP, 2, 2 * K], U8, name="w13", align_bytes=64)
-        for w, words in ((0, w1_words), (1, w3_words)):
-            nc.sync.dma_start(
-                w13[:, :, w].bitcast(I32), words.bitcast(I32).rearrange("e s p w -> p (e s) w")
-            )
-        for w, scales in ((0, w1_scales), (1, w3_scales)):
-            rows = scales.bitcast(I32).rearrange("e s f k -> f (e s) k")
+        for i in range(2):
+            load_w2(0, 2 + i)
+            load_w2s(1, 2 * i)
+            load_w2s(1, 2 * i + 1)
+        for i in range(2):
+            load_a3(0, i)
             for q in range(4):
-                nc.sync.dma_start(w13s[32 * q : 32 * q + 4, :, w].bitcast(I32), rows[4 * q : 4 * q + 4])
-
+                load_w13s(i, q)
+        load_w2(1, late_order[0])
+        load_w2(1, late_order[1])
+        load_w13(0, 0)
+        load_w13(0, 1)
+        load_w2(1, late_order[2])
+        load_w2(1, late_order[3])
         for h in range(HP):
             load_a1(1, h)
             load_a3(1, h)
+        load_w13(1, 0)
+        load_w13(1, 1)
 
         mask = {}
         relu1 = {}
 
-        def masks(h, e, a):
+        def masks(h, e, a, tag=None):
             j = slice(P * a, P * a + P)
             if (e, a) not in mask:
                 m = keep.tile([P, HP, P, 4], BF16, name=f"mask{e}{a}", align_bytes=64)
                 mask[e, a] = m
-            r = keep.tile([P, P, 4], F32, name=f"relu{e}{h}{a}")
+            r = keep.tile([P, P, 4], F32, name=f"relu{e}{h}{a}" if tag is None else tag, align_bytes=64)
             relu1[e, h, a] = r
             nc.scalar.activation(
                 r[:].rearrange("p (c i) t -> p c t i", i=4),
@@ -181,10 +193,10 @@ def tile_moe_bdx_glu_relu_kernel(
 
         bank = {}
 
-        def mm1(s, e, some=range(AT)):
+        def mm1(s, e, some=range(AT), first=0):
             for a in some:
                 for h in range(HP):
-                    if s == 0:
+                    if s == first:
                         b = psum.tile([P, 512], F32, name=f"bank{e}{a}{h}")
                         bank[e, a, h] = b
                     nc.tensor.matmul_mx(
@@ -193,7 +205,7 @@ def tile_moe_bdx_glu_relu_kernel(
                         lhsT_scale=gs[s, AT * e + a],
                         rhs=w2t[e, s][:, 1024 * h : 1024 * (h + 1)].bitcast(FP4X4),
                         rhs_scale=w2s[e][:, s, 512 * h : 512 * (h + 1)],
-                        start=(s == 0),
+                        start=(s == first),
                         stop=(s == NP - 1),
                     )
 
@@ -253,7 +265,7 @@ def tile_moe_bdx_glu_relu_kernel(
                         r = slice(P * (HP * w + h), P * (HP * w + h + 1))
                         nc.tensor.matmul_mx(
                             out=b[:, kt],
-                            lhsT=w13[:, e * HP + h, w, 2 * P * kt : 2 * P * (kt + 1)].bitcast(FP4X4),
+                            lhsT=w13[e, w][:, h, 2 * P * kt : 2 * P * (kt + 1)].bitcast(FP4X4),
                             lhsT_scale=w13s[:, e * HP + h, w, P * kt : P * (kt + 1)],
                             rhs=c[:, r].bitcast(FP8X4),
                             rhs_scale=z[:, r],
@@ -316,40 +328,46 @@ def tile_moe_bdx_glu_relu_kernel(
         turn(0, 1, 1, "slot_d")
         b31 = keep.tile([P, C, 4], BF16, name="slot_d", align_bytes=64)
         interleave(b31, 3, C, C, S, C)
+        for s in late_order[:2]:
+            mm1(s, 1, first=late_order[0])
         new_dq(0, 0, "dq00")
         prod1(0, 0, 0)
         prod1(0, 0, 1)
         prod3(0, 0, 0)
         masked(0, 0)
         prod3(0, 0, 1)
-        quant_g(b31, 3, C, S, C)
-        for s in range(NP):
-            mm1(s, 1)
-        for a in range(AT):
-            for h in range(HP):
-                turn(1, a, h)
-        for a in range(AT):
-            for h in range(HP):
-                masks(h, 1, a)
         new_dq(0, 1, "mask00")
         prod1(0, 1, 0)
         quant_d(0, 0)
-        mm2(0, 0, "dx00")
         prod1(0, 1, 1)
+        quant_g(b31, 3, C, S, C, "dq00")
         prod3(0, 1, 0)
         masked(0, 1)
+        mm2(0, 0, "mask01")
+        for a in range(AT):
+            for s in late_order[2:]:
+                mm1(s, 1, (a,), first=late_order[0])
         prod3(0, 1, 1)
-        scatter(0, 0, 0)
+        turn(1, 0, 0, "relu011")
         quant_d(0, 1)
+        turn(1, 0, 1, "mask00")
+        masks(0, 1, 0, "relu011")
         mm2(0, 1, "dx01")
-        scatter(0, 0, 1)
-        scatter(0, 0, 2)
+        turn(1, 1, 0, "mask00")
+        for kt in range(KT):
+            scatter(0, 0, kt)
+        masks(1, 1, 0, "mask01")
+        for kt in range(KT):
+            scatter(0, 1, kt)
+        turn(1, 1, 1, "dx01")
         new_dq(1, 0, "dq10")
         prod1(1, 0, 0)
         prod1(1, 0, 1)
         prod3(1, 0, 0)
+        masks(0, 1, 1, "relu011")
         masked(1, 0)
         prod3(1, 0, 1)
+        masks(1, 1, 1, "mask01")
         new_dq(1, 1, "mask10")
         prod1(1, 1, 0)
         quant_d(1, 0)
@@ -358,11 +376,8 @@ def tile_moe_bdx_glu_relu_kernel(
         masked(1, 1)
         mm2(1, 0, "mask11")
         prod3(1, 1, 1)
-        scatter(0, 1, 0)
         quant_d(1, 1)
         mm2(1, 1, "dx11")
-        scatter(0, 1, 1)
-        scatter(0, 1, 2)
         for kt in range(KT):
             scatter(1, 0, kt)
         for kt in range(KT):

@@ -112,8 +112,8 @@ def tile_moe_bdx_glu_relu_kernel(
         for q in range(4):
             load_w2s(0, q)
         load_w2(0, 0)
-        load_w2(0, 1)
         load_dy(3)
+        load_w2(0, 1)
         for i in range(2):
             load_w2(0, 2 + i)
             load_w2s(1, 2 * i)
@@ -137,19 +137,22 @@ def tile_moe_bdx_glu_relu_kernel(
         mask = {}
         relu1 = {}
 
-        def masks(h, e, a, tag=None):
+        def new_relu(e, tag):
+            r = keep.tile([P, AT, HP, P, 4], F32, name=tag, align_bytes=64)
+            relu1[e] = r
+
+        def masks(h, e, a):
             j = slice(P * a, P * a + P)
             if (e, a) not in mask:
                 m = keep.tile([P, HP, P, 4], BF16, name=f"mask{e}{a}", align_bytes=64)
                 mask[e, a] = m
-            r = keep.tile([P, P, 4], F32, name=f"relu{e}{h}{a}" if tag is None else tag, align_bytes=64)
-            relu1[e, h, a] = r
+            r = relu1[e][:, a, h]
             nc.scalar.activation(
-                r[:].rearrange("p (c i) t -> p c t i", i=4),
+                r.rearrange("p (c i) t -> p c t i", i=4),
                 a1t[e, h][:, :, j].rearrange("p t (c i) -> p c t i", i=4),
                 RELU,
             )
-            nc.scalar.activation(mask[e, a][:, h], r[:], SIGN)
+            nc.scalar.activation(mask[e, a][:, h], r, SIGN)
 
         gc = {}
         gs = {}
@@ -209,13 +212,13 @@ def tile_moe_bdx_glu_relu_kernel(
                         stop=(s == NP - 1),
                     )
 
-        def turn(e, a, h, tag=None):
+        def turn(e, a, h, tag=None, into=None):
             if tag is None:
                 d = dpool.tile([P, 4, P], F32, name="dhs")
             else:
                 d = keep.tile([P, 4, P], F32, name=tag, align_bytes=64)
             nc.scalar.copy(d[:], bank[e, a, h][:].rearrange("p (m t) -> p t m", t=4))
-            b = psum.tile([P, 4, P], F32, name=f"bank{e}{a}{h}")
+            b = psum.tile([P, 4, P], F32, name=f"bank{e}{a}{h}" if into is None else into)
             for t in range(4):
                 nc.tensor.transpose(b[:, t, :], d[:, t, :], ident[:])
             bank[e, a, h] = b
@@ -237,7 +240,7 @@ def tile_moe_bdx_glu_relu_kernel(
 
         def prod3(e, a, h):
             nc.vector.tensor_tensor(
-                dq[e, a][:, 1, h], bank[e, a, h][:].rearrange("p t j -> p j t"), relu1[e, h, a][:], MULT
+                dq[e, a][:, 1, h], bank[e, a, h][:].rearrange("p t j -> p j t"), relu1[e][:, a, h], MULT
             )
 
         def masked(e, a):
@@ -256,25 +259,28 @@ def tile_moe_bdx_glu_relu_kernel(
 
         dxs = {}
 
-        def mm2(e, a, tag):
+        def mm2(e, a, tag, banks):
             c, z = dc[e, a]
-            b = psum.tile([P, KT, P], F32, name=f"bank{e}{a}0")
-            for kt in range(KT):
-                for h in range(HP):
-                    for w in range(2):
-                        r = slice(P * (HP * w + h), P * (HP * w + h + 1))
-                        nc.tensor.matmul_mx(
-                            out=b[:, kt],
-                            lhsT=w13[e, w][:, h, 2 * P * kt : 2 * P * (kt + 1)].bitcast(FP4X4),
-                            lhsT_scale=w13s[:, e * HP + h, w, P * kt : P * (kt + 1)],
-                            rhs=c[:, r].bitcast(FP8X4),
-                            rhs_scale=z[:, r],
-                            start=(h == 0 and w == 0),
-                            stop=(h == HP - 1 and w == 1),
-                        )
             d = keep.tile([P, KT, P], F32, name=tag, align_bytes=64)
-            nc.scalar.copy(d[:], b[:])
             dxs[e, a] = d
+            per = KT // len(banks)
+            for i, name in enumerate(banks):
+                b = psum.tile([P, per, P], F32, name=name)
+                for n in range(per):
+                    kt = per * i + n
+                    for h in range(HP):
+                        for w in range(2):
+                            r = slice(P * (HP * w + h), P * (HP * w + h + 1))
+                            nc.tensor.matmul_mx(
+                                out=b[:, n],
+                                lhsT=w13[e, w][:, h, 2 * P * kt : 2 * P * (kt + 1)].bitcast(FP4X4),
+                                lhsT_scale=w13s[:, e * HP + h, w, P * kt : P * (kt + 1)],
+                                rhs=c[:, r].bitcast(FP8X4),
+                                rhs_scale=z[:, r],
+                                start=(h == 0 and w == 0),
+                                stop=(h == HP - 1 and w == 1),
+                            )
+                nc.scalar.copy(d[:, per * i : per * (i + 1)], b[:])
 
         def scatter(e, a, kt):
             lo = (C * e + P * a) // 16
@@ -287,6 +293,7 @@ def tile_moe_bdx_glu_relu_kernel(
         gxb = keep.tile([P, C], F32, name="slot_b", align_bytes=64)
         nc.scalar.copy(gxb[:], gates[:, 0:C])
         gb = {}
+        new_relu(0, "relu0")
         for s in range(3):
             for t in range(4):
                 gather(s, t, 0, S, gates[:])
@@ -343,41 +350,40 @@ def tile_moe_bdx_glu_relu_kernel(
         quant_g(b31, 3, C, S, C, "dq00")
         prod3(0, 1, 0)
         masked(0, 1)
-        mm2(0, 0, "mask01")
+        mm2(0, 0, "mask01", ("bank000",))
         for a in range(AT):
             for s in late_order[2:]:
                 mm1(s, 1, (a,), first=late_order[0])
         prod3(0, 1, 1)
-        turn(1, 0, 0, "relu011")
+        turn(1, 0, 0, "relu0")
         quant_d(0, 1)
         turn(1, 0, 1, "mask00")
-        masks(0, 1, 0, "relu011")
-        mm2(0, 1, "dx01")
-        turn(1, 1, 0, "mask00")
-        for kt in range(KT):
-            scatter(0, 0, kt)
-        masks(1, 1, 0, "mask01")
-        for kt in range(KT):
-            scatter(0, 1, kt)
-        turn(1, 1, 1, "dx01")
-        new_dq(1, 0, "dq10")
+        mm2(0, 1, "dx01", ("bank010", "bank011", "bank001"))
+        turn(1, 1, 0, "relu0", "bank001")
+        turn(1, 1, 1, "mask00")
+        new_relu(1, "relu0")
+        for a in range(AT):
+            for h in range(HP):
+                masks(h, 1, a)
+        for a in range(AT):
+            for kt in range(KT):
+                scatter(0, a, kt)
+        new_dq(1, 0, "dx01")
         prod1(1, 0, 0)
         prod1(1, 0, 1)
         prod3(1, 0, 0)
-        masks(0, 1, 1, "relu011")
         masked(1, 0)
         prod3(1, 0, 1)
-        masks(1, 1, 1, "mask01")
         new_dq(1, 1, "mask10")
         prod1(1, 1, 0)
         quant_d(1, 0)
         prod1(1, 1, 1)
         prod3(1, 1, 0)
         masked(1, 1)
-        mm2(1, 0, "mask11")
+        mm2(1, 0, "mask11", ("bank100",))
         prod3(1, 1, 1)
         quant_d(1, 1)
-        mm2(1, 1, "dx11")
+        mm2(1, 1, "dx11", ("bank110", "bank000", "bank010"))
         for kt in range(KT):
             scatter(1, 0, kt)
         for kt in range(KT):

@@ -141,18 +141,23 @@ def tile_moe_bdx_glu_relu_kernel(
             r = keep.tile([P, AT, HP, P, 4], F32, name=tag, align_bytes=64)
             relu1[e] = r
 
-        def masks(h, e, a):
+        def relus(h, e, a):
             j = slice(P * a, P * a + P)
-            if (e, a) not in mask:
-                m = keep.tile([P, HP, P, 4], BF16, name=f"mask{e}{a}", align_bytes=64)
-                mask[e, a] = m
-            r = relu1[e][:, a, h]
             nc.scalar.activation(
-                r.rearrange("p (c i) t -> p c t i", i=4),
+                relu1[e][:, a, h].rearrange("p (c i) t -> p c t i", i=4),
                 a1t[e, h][:, :, j].rearrange("p t (c i) -> p c t i", i=4),
                 RELU,
             )
-            nc.scalar.activation(mask[e, a][:, h], r, SIGN)
+
+        def sign(e, a, h):
+            if (e, a) not in mask:
+                m = keep.tile([P, HP, P, 4], BF16, name=f"mask{e}{a}", align_bytes=64)
+                mask[e, a] = m
+            nc.scalar.activation(mask[e, a][:, h], relu1[e][:, a, h], SIGN)
+
+        def masks(h, e, a):
+            relus(h, e, a)
+            sign(e, a, h)
 
         gc = {}
         gs = {}
@@ -242,6 +247,22 @@ def tile_moe_bdx_glu_relu_kernel(
             nc.vector.tensor_tensor(
                 dq[e, a][:, 1, h], bank[e, a, h][:].rearrange("p t j -> p j t"), relu1[e][:, a, h], MULT
             )
+
+        dh_sb = {}
+
+        def park(e, a, h, tag):
+            d = keep.tile([P, P, 4], F32, name=tag, align_bytes=64)
+            nc.scalar.copy(d[:], bank[e, a, h][:].rearrange("p t j -> p j t"))
+            dh_sb[e, a, h] = d
+
+        def prod1_g(e, a, h):
+            j = slice(P * a, P * a + P)
+            nc.gpsimd.tensor_tensor(
+                dq[e, a][:, 0, h], dh_sb[e, a, h][:], a3t[e, h][:, :, j].rearrange("p t j -> p j t"), MULT
+            )
+
+        def prod3_g(e, a, h):
+            nc.gpsimd.tensor_tensor(dq[e, a][:, 1, h], dh_sb[e, a, h][:], relu1[e][:, a, h], MULT)
 
         def masked(e, a):
             m = dq[e, a][:, 0]
@@ -351,20 +372,30 @@ def tile_moe_bdx_glu_relu_kernel(
         prod3(0, 1, 0)
         masked(0, 1)
         mm2(0, 0, "mask01", ("bank000",))
-        for a in range(AT):
+        for a in (1, 0):
             for s in late_order[2:]:
                 mm1(s, 1, (a,), first=late_order[0])
         prod3(0, 1, 1)
-        turn(1, 0, 0, "relu0")
+        turn(1, 1, 0, "relu0")
         quant_d(0, 1)
-        turn(1, 0, 1, "mask00")
-        mm2(0, 1, "dx01", ("bank010", "bank011", "bank001"))
-        turn(1, 1, 0, "relu0", "bank001")
         turn(1, 1, 1, "mask00")
+        mm2(0, 1, "dx01", ("bank010", "bank011", "bank001"))
+        park(1, 1, 0, "park0")
+        park(1, 1, 1, "park1")
+        turn(1, 0, 0, "mask00", "bank001")
         new_relu(1, "relu0")
-        for a in range(AT):
-            for h in range(HP):
-                masks(h, 1, a)
+        relus(0, 1, 1)
+        relus(1, 1, 1)
+        turn(1, 0, 1, "mask00")
+        relus(0, 1, 0)
+        relus(1, 1, 0)
+        sign(1, 0, slice(0, HP))
+        sign(1, 1, slice(0, HP))
+        new_dq(1, 1, "dq11")
+        prod1_g(1, 1, 0)
+        prod1_g(1, 1, 1)
+        prod3_g(1, 1, 0)
+        prod3_g(1, 1, 1)
         for a in range(AT):
             for kt in range(KT):
                 scatter(0, a, kt)
@@ -374,16 +405,11 @@ def tile_moe_bdx_glu_relu_kernel(
         prod3(1, 0, 0)
         masked(1, 0)
         prod3(1, 0, 1)
-        new_dq(1, 1, "mask10")
-        prod1(1, 1, 0)
-        quant_d(1, 0)
-        prod1(1, 1, 1)
-        prod3(1, 1, 0)
         masked(1, 1)
-        mm2(1, 0, "mask11", ("bank100",))
-        prod3(1, 1, 1)
+        quant_d(1, 0)
+        mm2(1, 0, "dx10", ("bank000", "bank010", "bank011"))
         quant_d(1, 1)
-        mm2(1, 1, "dx11", ("bank110", "bank000", "bank010"))
+        mm2(1, 1, "dx11", ("bank110",))
         for kt in range(KT):
             scatter(1, 0, kt)
         for kt in range(KT):

@@ -42,15 +42,15 @@ def tile_moe_bdx_glu_relu_kernel(
         gates = keep.tile([P, S], F32, name="gates")
         nc.scalar.dma_start(gates[:], gate[0:P, :])
 
+        ident = keep.tile([P, P], F32, name="ident")
+        make_identity(nc, ident[:])
         w2s = []
         for e in range(E):
             plane = keep.tile([P, NP, H], U8, name=f"w2s{e}", align_bytes=64)
-            nc.vector.memset(plane[:].bitcast(I32), 0)
+            nc.gpsimd.memset(plane[:].bitcast(I32), 0)
             w2s.append(plane)
         w13s = keep.tile([P, E * HP, 2, K], U8, name="w13s", align_bytes=64)
-        nc.vector.memset(w13s[:].bitcast(I32), 0)
-        ident = keep.tile([P, P], F32, name="ident")
-        make_identity(nc, ident[:])
+        nc.gpsimd.memset(w13s[:].bitcast(I32), 0)
         outs = []
         for kt in range(KT):
             o = keep.tile([P, T], F32, name=f"out{kt}")
@@ -96,7 +96,13 @@ def tile_moe_bdx_glu_relu_kernel(
         def load_a1(e, h):
             t1 = keep.tile([P, 4, C], F32, name=f"a1t{e}{h}")
             nc.sync.dma_start(t1[:], a1_rows[h][:, :, C * e : C * (e + 1)])
-            a1t[e, h] = t1
+            a1t[e, h] = t1[:]
+
+        def load_a1_both(h):
+            t1 = keep.tile([P, 4, S], F32, name=f"a1t{h}")
+            nc.sync.dma_start(t1[:], a1_rows[h])
+            for e in range(E):
+                a1t[e, h] = t1[:, :, C * e : C * (e + 1)]
 
         def load_a3(e, h):
             t3 = keep.tile([P, 4, C], F32, name=f"a3t{e}{h}")
@@ -107,7 +113,7 @@ def tile_moe_bdx_glu_relu_kernel(
         load_dy(0)
         load_a1(0, 0)
         load_dy(1)
-        load_a1(0, 1)
+        load_a1_both(1)
         load_dy(2)
         for q in range(4):
             load_w2s(0, q)
@@ -128,23 +134,23 @@ def tile_moe_bdx_glu_relu_kernel(
         load_w13(0, 1)
         load_w2(1, late_order[2])
         load_w2(1, late_order[3])
-        for h in range(HP):
-            load_a1(1, h)
-            load_a3(1, h)
+        load_a1(1, 0)
+        load_a3(1, 0)
+        load_a3(1, 1)
         load_w13(1, 0)
         load_w13(1, 1)
 
         mask = {}
         relu1 = {}
 
-        def new_relu(e, tag):
-            r = keep.tile([P, AT, HP, P, 4], F32, name=tag, align_bytes=64)
-            relu1[e] = r
+        def new_relu(e, h, tag):
+            r = keep.tile([P, AT, P, 4], F32, name=tag, align_bytes=64)
+            relu1[e, h] = r
 
         def relus(h, e, a):
             j = slice(P * a, P * a + P)
             nc.scalar.activation(
-                relu1[e][:, a, h].rearrange("p (c i) t -> p c t i", i=4),
+                relu1[e, h][:, a].rearrange("p (c i) t -> p c t i", i=4),
                 a1t[e, h][:, :, j].rearrange("p t (c i) -> p c t i", i=4),
                 RELU,
             )
@@ -153,7 +159,7 @@ def tile_moe_bdx_glu_relu_kernel(
             if (e, a) not in mask:
                 m = keep.tile([P, HP, P, 4], BF16, name=f"mask{e}{a}", align_bytes=64)
                 mask[e, a] = m
-            nc.scalar.activation(mask[e, a][:, h], relu1[e][:, a, h], SIGN)
+            nc.scalar.activation(mask[e, a][:, h], relu1[e, h][:, a], SIGN)
 
         def masks(h, e, a):
             relus(h, e, a)
@@ -245,7 +251,7 @@ def tile_moe_bdx_glu_relu_kernel(
 
         def prod3(e, a, h):
             nc.vector.tensor_tensor(
-                dq[e, a][:, 1, h], bank[e, a, h][:].rearrange("p t j -> p j t"), relu1[e][:, a, h], MULT
+                dq[e, a][:, 1, h], bank[e, a, h][:].rearrange("p t j -> p j t"), relu1[e, h][:, a], MULT
             )
 
         dh_sb = {}
@@ -262,7 +268,7 @@ def tile_moe_bdx_glu_relu_kernel(
             )
 
         def prod3_g(e, a, h):
-            nc.gpsimd.tensor_tensor(dq[e, a][:, 1, h], dh_sb[e, a, h][:], relu1[e][:, a, h], MULT)
+            nc.gpsimd.tensor_tensor(dq[e, a][:, 1, h], dh_sb[e, a, h][:], relu1[e, h][:, a], MULT)
 
         def masked(e, a):
             m = dq[e, a][:, 0]
@@ -280,13 +286,14 @@ def tile_moe_bdx_glu_relu_kernel(
 
         dxs = {}
 
-        def mm2(e, a, tag, banks):
+        dxb = {}
+
+        def mm2(e, a, banks):
             c, z = dc[e, a]
-            d = keep.tile([P, KT, P], F32, name=tag, align_bytes=64)
-            dxs[e, a] = d
             per = KT // len(banks)
             for i, name in enumerate(banks):
                 b = psum.tile([P, per, P], F32, name=name)
+                dxb[e, a, i] = b
                 for n in range(per):
                     kt = per * i + n
                     for h in range(HP):
@@ -301,12 +308,19 @@ def tile_moe_bdx_glu_relu_kernel(
                                 start=(h == 0 and w == 0),
                                 stop=(h == HP - 1 and w == 1),
                             )
-                nc.scalar.copy(d[:, per * i : per * (i + 1)], b[:])
+
+        def dx_out(e, a, i, tag):
+            b = dxb[e, a, i]
+            per = b.shape[1]
+            d = keep.tile([P, per, P], F32, name=tag, align_bytes=64)
+            nc.scalar.copy(d[:], b[:])
+            for n in range(per):
+                dxs[e, a, per * i + n] = d[:, n]
 
         def scatter(e, a, kt):
             lo = (C * e + P * a) // 16
             nc.vector.tensor_copy(
-                outs[kt][:].indirect(offsets[:, lo : lo + P // 16]), dxs[e, a][:, kt]
+                outs[kt][:].indirect(offsets[:, lo : lo + P // 16]), dxs[e, a, kt]
             )
 
         gxa = keep.tile([P, C], F32, name="slot_a", align_bytes=64)
@@ -314,12 +328,13 @@ def tile_moe_bdx_glu_relu_kernel(
         gxb = keep.tile([P, C], F32, name="slot_b", align_bytes=64)
         nc.scalar.copy(gxb[:], gates[:, 0:C])
         gb = {}
-        new_relu(0, "relu0")
+        new_relu(0, 0, "relu00")
+        new_relu(0, 1, "relu01")
         for s in range(3):
             for t in range(4):
                 gather(s, t, 0, S, gates[:])
                 if t == 2 and s > 0:
-                    quant_g(gb[s - 1], s - 1, 0, C, 0)
+                    quant_g(gb[s - 1], s - 1, 0, C, 0, f"dy{s}1")
                     mm1(s - 1, 0)
             if s < 2:
                 gb[s] = new_gb(S, "gb", 2)
@@ -356,6 +371,9 @@ def tile_moe_bdx_glu_relu_kernel(
         turn(0, 1, 1, "slot_d")
         b31 = keep.tile([P, C, 4], BF16, name="slot_d", align_bytes=64)
         interleave(b31, 3, C, C, S, C)
+        new_relu(1, 1, "slot_c")
+        masks(1, 1, 1)
+        masks(1, 1, 0)
         for s in late_order[:2]:
             mm1(s, 1, first=late_order[0])
         new_dq(0, 0, "dq00")
@@ -371,45 +389,52 @@ def tile_moe_bdx_glu_relu_kernel(
         quant_g(b31, 3, C, S, C, "dq00")
         prod3(0, 1, 0)
         masked(0, 1)
-        mm2(0, 0, "mask01", ("bank000",))
+        mm2(0, 0, ("bank000",))
+        dx_out(0, 0, 0, "mask01")
         for a in (1, 0):
             for s in late_order[2:]:
                 mm1(s, 1, (a,), first=late_order[0])
         prod3(0, 1, 1)
-        turn(1, 1, 0, "relu0")
+        turn(1, 1, 0, "relu01")
         quant_d(0, 1)
         turn(1, 1, 1, "mask00")
-        mm2(0, 1, "dx01", ("bank010", "bank011", "bank001"))
+        mm2(0, 1, ("bank010", "bank001", "bank011"))
         park(1, 1, 0, "park0")
         park(1, 1, 1, "park1")
-        turn(1, 0, 0, "mask00", "bank001")
-        new_relu(1, "relu0")
-        relus(0, 1, 1)
-        relus(1, 1, 1)
+        dx_out(0, 1, 0, "dx010")
+        dx_out(0, 1, 1, "dx011")
+        turn(1, 0, 0, "relu01", "bank001")
         turn(1, 0, 1, "mask00")
+        new_relu(1, 0, "relu01")
         relus(0, 1, 0)
-        relus(1, 1, 0)
-        sign(1, 0, slice(0, HP))
-        sign(1, 1, slice(0, HP))
+        relus(0, 1, 1)
+        sign(1, 0, 0)
+        sign(1, 1, 0)
         new_dq(1, 1, "dq11")
         prod1_g(1, 1, 0)
         prod1_g(1, 1, 1)
-        prod3_g(1, 1, 0)
         prod3_g(1, 1, 1)
-        for a in range(AT):
-            for kt in range(KT):
-                scatter(0, a, kt)
-        new_dq(1, 0, "dx01")
+        prod3_g(1, 1, 0)
+        for kt in range(KT):
+            scatter(0, 0, kt)
+        scatter(0, 1, 0)
+        scatter(0, 1, 1)
+        new_dq(1, 0, "dx011")
         prod1(1, 0, 0)
         prod1(1, 0, 1)
+        prod3(1, 0, 1)
         prod3(1, 0, 0)
         masked(1, 0)
-        prod3(1, 0, 1)
         masked(1, 1)
+        dx_out(0, 1, 2, "mask11")
         quant_d(1, 0)
-        mm2(1, 0, "dx10", ("bank000", "bank010", "bank011"))
+        mm2(1, 0, ("bank000", "bank010", "bank100"))
         quant_d(1, 1)
-        mm2(1, 1, "dx11", ("bank110",))
+        for kt in range(KT):
+            dx_out(1, 0, kt, f"dx10{kt}")
+        mm2(1, 1, ("bank110",))
+        dx_out(1, 1, 0, "dx11")
+        scatter(0, 1, 2)
         for kt in range(KT):
             scatter(1, 0, kt)
         for kt in range(KT):

@@ -27,6 +27,14 @@ RELU = mybir.ActivationFunctionType.Relu
 SIGN = mybir.ActivationFunctionType.Sign
 
 
+def walk_rows(rows, run):
+    return rows.rearrange("p t (c r) -> p c t r", r=run)
+
+
+def walk_packed(packed, run):
+    return packed.rearrange("p (c r) t -> p c t r", r=run)
+
+
 def tile_moe_bdx_glu_relu_kernel(
     tc, dyT, a1, a3, w2_words, w2_scales, w1_words, w1_scales, w3_words, w3_scales, gate, offs, out
 ):
@@ -57,11 +65,13 @@ def tile_moe_bdx_glu_relu_kernel(
             nc.gpsimd.memset(o[:], 0.0)
             outs.append(o)
 
-        dy_rows = dyT.rearrange("(s p t) w -> s t p w", s=NP, p=P, t=4)
+        dy_rows = dyT.rearrange("(s p t) u -> s t p u", s=NP, p=P, t=4)
         a1_rows = a1.rearrange("(s p t) j -> s p t j", s=HP, p=P, t=4)
         a3_rows = a3.rearrange("(s p t) j -> s p t j", s=HP, p=P, t=4)
+        w2s_rows = w2_scales.bitcast(I32).rearrange("e s f i -> f e s i")
         dy = {}
         w2t = {}
+        w13 = {}
         a1t = {}
         a3t = {}
 
@@ -72,44 +82,39 @@ def tile_moe_bdx_glu_relu_kernel(
                 dy[s, t] = d
 
         def load_w2(e, s):
-            w = keep.tile([P, 2 * H], U8, name=f"w2t{e}{s}", align_bytes=64)
-            nc.sync.dma_start(w[:].bitcast(I32), w2_words.bitcast(I32)[e, s])
-            w2t[e, s] = w
-
-        w2s_rows = w2_scales.bitcast(I32).rearrange("e s f i -> f e s i")
+            words = keep.tile([P, 2 * H], U8, name=f"w2t{e}{s}", align_bytes=64)
+            nc.sync.dma_start(words[:].bitcast(I32), w2_words.bitcast(I32)[e, s])
+            w2t[e, s] = words
 
         def load_w2s(e, q):
             nc.sync.dma_start(w2s[e][32 * q : 32 * q + 4].bitcast(I32), w2s_rows[4 * q : 4 * q + 4, e])
 
-        w13 = {}
-
         def load_w13(e, w):
-            t = keep.tile([P, HP, 2 * K], U8, name=f"w13_{e}{w}", align_bytes=64)
-            words = (w1_words, w3_words)[w]
-            nc.sync.dma_start(t[:].bitcast(I32), words.bitcast(I32).rearrange("e s p w -> e p s w")[e])
-            w13[e, w] = t
+            words = keep.tile([P, HP, 2 * K], U8, name=f"w13_{e}{w}", align_bytes=64)
+            source = (w1_words, w3_words)[w].bitcast(I32).rearrange("e s p x -> e p s x")
+            nc.sync.dma_start(words[:].bitcast(I32), source[e])
+            w13[e, w] = words
 
         def load_w13s(w, q):
-            rows = (w1_scales, w3_scales)[w].bitcast(I32).rearrange("e s f k -> f (e s) k")
-            nc.sync.dma_start(w13s[32 * q : 32 * q + 4, :, w].bitcast(I32), rows[4 * q : 4 * q + 4])
+            scale_rows = (w1_scales, w3_scales)[w].bitcast(I32).rearrange("e s f k -> f (e s) k")
+            nc.sync.dma_start(w13s[32 * q : 32 * q + 4, :, w].bitcast(I32), scale_rows[4 * q : 4 * q + 4])
 
         def load_a1(e, h):
-            t1 = keep.tile([P, 4, C], F32, name=f"a1t{e}{h}")
-            nc.sync.dma_start(t1[:], a1_rows[h][:, :, C * e : C * (e + 1)])
-            a1t[e, h] = t1[:]
+            rows = keep.tile([P, 4, C], F32, name=f"a1t{e}{h}")
+            nc.sync.dma_start(rows[:], a1_rows[h][:, :, C * e : C * (e + 1)])
+            a1t[e, h] = rows[:]
 
         def load_a1_both(h):
-            t1 = keep.tile([P, 4, S], F32, name=f"a1t{h}")
-            nc.sync.dma_start(t1[:], a1_rows[h])
+            rows = keep.tile([P, 4, S], F32, name=f"a1t{h}")
+            nc.sync.dma_start(rows[:], a1_rows[h])
             for e in range(E):
-                a1t[e, h] = t1[:, :, C * e : C * (e + 1)]
+                a1t[e, h] = rows[:, :, C * e : C * (e + 1)]
 
         def load_a3(e, h):
-            t3 = keep.tile([P, 4, C], F32, name=f"a3t{e}{h}")
-            nc.sync.dma_start(t3[:], a3_rows[h][:, :, C * e : C * (e + 1)])
-            a3t[e, h] = t3
+            rows = keep.tile([P, 4, C], F32, name=f"a3t{e}{h}")
+            nc.sync.dma_start(rows[:], a3_rows[h][:, :, C * e : C * (e + 1)])
+            a3t[e, h] = rows
 
-        late_order = (2, 1, 0, 3)
         load_dy(0)
         load_a1(0, 0)
         load_dy(1)
@@ -120,321 +125,310 @@ def tile_moe_bdx_glu_relu_kernel(
         load_w2(0, 0)
         load_dy(3)
         load_w2(0, 1)
-        for i in range(2):
-            load_w2(0, 2 + i)
-            load_w2s(1, 2 * i)
-            load_w2s(1, 2 * i + 1)
-        for i in range(2):
-            load_a3(0, i)
+        for step in range(2):
+            load_w2(0, 2 + step)
+            load_w2s(1, 2 * step)
+            load_w2s(1, 2 * step + 1)
+        for step in range(2):
+            load_a3(0, step)
             for q in range(4):
-                load_w13s(i, q)
-        load_w2(1, late_order[0])
-        load_w2(1, late_order[1])
+                load_w13s(step, q)
+        load_w2(1, 2)
+        load_w2(1, 1)
         load_w13(0, 0)
         load_w13(0, 1)
-        load_w2(1, late_order[2])
-        load_w2(1, late_order[3])
+        load_w2(1, 0)
+        load_w2(1, 3)
         load_a1(1, 0)
         load_a3(1, 0)
         load_a3(1, 1)
         load_w13(1, 0)
         load_w13(1, 1)
 
-        mask = {}
         relu1 = {}
+        mask = {}
 
-        def new_relu(e, h, tag):
-            r = keep.tile([P, AT, P, 4], F32, name=tag, align_bytes=64)
+        def new_relu(e, h, buffer):
+            r = keep.tile([P, AT, P, 4], F32, name=buffer, align_bytes=64)
             relu1[e, h] = r
 
-        def relus(h, e, a):
-            j = slice(P * a, P * a + P)
+        def make_relu(e, a, h):
             nc.scalar.activation(
-                relu1[e, h][:, a].rearrange("p (c i) t -> p c t i", i=4),
-                a1t[e, h][:, :, j].rearrange("p t (c i) -> p c t i", i=4),
-                RELU,
+                walk_packed(relu1[e, h][:, a], 4), walk_rows(a1t[e, h][:, :, P * a : P * (a + 1)], 4), RELU
             )
 
-        def sign(e, a, h):
+        def make_mask(e, a, h):
             if (e, a) not in mask:
                 m = keep.tile([P, HP, P, 4], BF16, name=f"mask{e}{a}", align_bytes=64)
                 mask[e, a] = m
             nc.scalar.activation(mask[e, a][:, h], relu1[e, h][:, a], SIGN)
 
-        def masks(h, e, a):
-            relus(h, e, a)
-            sign(e, a, h)
+        def relu_and_mask(e, a, h):
+            make_relu(e, a, h)
+            make_mask(e, a, h)
 
-        gc = {}
-        gs = {}
-        g4 = {}
-
-        def gather(s, t, lo, hi, weights, tag=None):
-            if (s, lo) not in g4:
-                if tag is None:
-                    g = gpool.tile([P, 4, hi - lo], F32, name=f"g4_{hi - lo}")
-                else:
-                    g = keep.tile([P, 4, hi - lo], F32, name=tag, align_bytes=64)
-                g4[s, lo] = g
+        def gather(rows, s, t, lo, hi, weights):
             nc.vector.tensor_tensor(
-                g4[s, lo][:, t, :], dy[s, t][:].indirect(offsets[:, lo // 16 : hi // 16]), weights, MULT
+                rows[:, t, :], dy[s, t][:].indirect(offsets[:, lo // 16 : hi // 16]), weights, MULT
             )
 
-        def new_gb(width, tag, bufs):
-            return gpool.tile([P, width, 4], BF16, name=tag, bufs=bufs, align_bytes=64)
+        def new_packed(width, name, bufs):
+            return gpool.tile([P, width, 4], BF16, name=name, bufs=bufs, align_bytes=64)
 
-        def interleave(b, s, base, lo, hi, first):
-            nc.scalar.copy(
-                b[:, lo - first : hi - first].rearrange("p (c i) t -> p c t i", i=4),
-                g4[s, base][:, :, lo - base : hi - base].rearrange("p t (c i) -> p c t i", i=4),
-            )
+        def pack(packed, rows):
+            nc.scalar.copy(walk_packed(packed, 4), walk_rows(rows, 4))
 
-        def new_codes(s, lo, hi, tag):
-            c = keep.tile([P, hi - lo], U32, name=f"gc{s}_{lo}", align_bytes=64)
-            z = keep.tile([P, hi - lo], U8, name=tag, align_bytes=64)
-            for a in range(lo // P, hi // P):
-                gc[s, a] = c[:, P * a - lo : P * (a + 1) - lo]
-                gs[s, a] = z[:, P * a - lo : P * (a + 1) - lo]
-            return c, z
+        g_codes = {}
+        g_scales = {}
 
-        def quant_g(b, s, lo, hi, first, tag=None):
-            c, z = new_codes(s, lo, hi, f"gs{s}_{lo}" if tag is None else tag)
+        def quantise_g(packed, s, lo, hi, buffer=None):
+            codes = keep.tile([P, hi - lo], U32, name=f"gc{s}_{lo}", align_bytes=64)
+            scales = keep.tile([P, hi - lo], U8, name=buffer or f"gs{s}_{lo}", align_bytes=64)
             nc.vector.quantize_mx(
-                out=c[:].bitcast(FP8X4),
-                scales=z[:],
-                in_=b[:, lo - first : hi - first].rearrange("p j t -> p (j t)"),
+                out=codes[:].bitcast(FP8X4), scales=scales[:], in_=packed.rearrange("p j t -> p (j t)")
             )
+            for first in range(lo, hi, P):
+                g_codes[s, first] = codes[:, first - lo : first - lo + P]
+                g_scales[s, first] = scales[:, first - lo : first - lo + P]
 
         bank = {}
 
-        def mm1(s, e, some=range(AT), first=0):
-            for a in some:
-                for h in range(HP):
-                    if s == first:
-                        b = psum.tile([P, 512], F32, name=f"bank{e}{a}{h}")
-                        bank[e, a, h] = b
-                    nc.tensor.matmul_mx(
-                        out=bank[e, a, h][:],
-                        lhsT=gc[s, AT * e + a].bitcast(FP8X4),
-                        lhsT_scale=gs[s, AT * e + a],
-                        rhs=w2t[e, s][:, 1024 * h : 1024 * (h + 1)].bitcast(FP4X4),
-                        rhs_scale=w2s[e][:, s, 512 * h : 512 * (h + 1)],
-                        start=(s == first),
-                        stop=(s == NP - 1),
-                    )
+        def first_product(s, e, a, opens, closes):
+            for h in range(HP):
+                if s == opens:
+                    b = psum.tile([P, 512], F32, name=f"bank{e}{a}{h}")
+                    bank[e, a, h] = b
+                nc.tensor.matmul_mx(
+                    out=bank[e, a, h][:],
+                    lhsT=g_codes[s, C * e + P * a].bitcast(FP8X4),
+                    lhsT_scale=g_scales[s, C * e + P * a],
+                    rhs=w2t[e, s][:, 1024 * h : 1024 * (h + 1)].bitcast(FP4X4),
+                    rhs_scale=w2s[e][:, s, 512 * h : 512 * (h + 1)],
+                    start=(s == opens),
+                    stop=(s == closes),
+                )
 
-        def turn(e, a, h, tag=None, into=None):
-            if tag is None:
-                d = dpool.tile([P, 4, P], F32, name="dhs")
+        def turn(e, a, h, buffer=None, into=None):
+            if buffer is None:
+                sorted_dh = dpool.tile([P, 4, P], F32, name="sorted_dh")
             else:
-                d = keep.tile([P, 4, P], F32, name=tag, align_bytes=64)
-            nc.scalar.copy(d[:], bank[e, a, h][:].rearrange("p (m t) -> p t m", t=4))
-            b = psum.tile([P, 4, P], F32, name=f"bank{e}{a}{h}" if into is None else into)
+                sorted_dh = keep.tile([P, 4, P], F32, name=buffer, align_bytes=64)
+            nc.scalar.copy(sorted_dh[:], bank[e, a, h][:].rearrange("p (m t) -> p t m", t=4))
+            b = psum.tile([P, 4, P], F32, name=into or f"bank{e}{a}{h}")
             for t in range(4):
-                nc.tensor.transpose(b[:, t, :], d[:, t, :], ident[:])
+                nc.tensor.transpose(b[:, t, :], sorted_dh[:, t, :], ident[:])
             bank[e, a, h] = b
 
-        dq = {}
+        da = {}
 
-        def new_dq(e, a, tag):
-            q = keep.tile([P, 2, HP, P, 4], BF16, name=tag, align_bytes=64)
-            dq[e, a] = q
+        def new_da(e, a, buffer):
+            packed = keep.tile([P, 2, HP, P, 4], BF16, name=buffer, align_bytes=64)
+            da[e, a] = packed
 
-        def prod1(e, a, h):
-            j = slice(P * a, P * a + P)
+        def make_da1(e, a, h):
             nc.vector.tensor_tensor(
-                dq[e, a][:, 0, h].rearrange("p (c i) t -> p c t i", i=2),
-                bank[e, a, h][:].rearrange("p t (c i) -> p c t i", i=2),
-                a3t[e, h][:, :, j].rearrange("p t (c i) -> p c t i", i=2),
+                walk_packed(da[e, a][:, 0, h], 2),
+                walk_rows(bank[e, a, h][:], 2),
+                walk_rows(a3t[e, h][:, :, P * a : P * (a + 1)], 2),
                 MULT,
             )
 
-        def prod3(e, a, h):
+        def make_da3(e, a, h):
             nc.vector.tensor_tensor(
-                dq[e, a][:, 1, h], bank[e, a, h][:].rearrange("p t j -> p j t"), relu1[e, h][:, a], MULT
+                da[e, a][:, 1, h], bank[e, a, h][:].rearrange("p t j -> p j t"), relu1[e, h][:, a], MULT
             )
 
-        dh_sb = {}
+        parked = {}
 
-        def park(e, a, h, tag):
-            d = keep.tile([P, P, 4], F32, name=tag, align_bytes=64)
-            nc.scalar.copy(d[:], bank[e, a, h][:].rearrange("p t j -> p j t"))
-            dh_sb[e, a, h] = d
+        def park(e, a, h):
+            dh = keep.tile([P, P, 4], F32, name=f"park{h}", align_bytes=64)
+            nc.scalar.copy(dh[:], bank[e, a, h][:].rearrange("p t j -> p j t"))
+            parked[h] = dh
 
-        def prod1_g(e, a, h):
-            j = slice(P * a, P * a + P)
-            nc.gpsimd.tensor_tensor(
-                dq[e, a][:, 0, h], dh_sb[e, a, h][:], a3t[e, h][:, :, j].rearrange("p t j -> p j t"), MULT
-            )
+        def make_da1_gpsimd(e, a, h):
+            a3_packed = a3t[e, h][:, :, P * a : P * (a + 1)].rearrange("p t j -> p j t")
+            nc.gpsimd.tensor_tensor(da[e, a][:, 0, h], parked[h][:], a3_packed, MULT)
 
-        def prod3_g(e, a, h):
-            nc.gpsimd.tensor_tensor(dq[e, a][:, 1, h], dh_sb[e, a, h][:], relu1[e, h][:, a], MULT)
+        def make_da3_gpsimd(e, a, h):
+            nc.gpsimd.tensor_tensor(da[e, a][:, 1, h], parked[h][:], relu1[e, h][:, a], MULT)
 
-        def masked(e, a):
-            m = dq[e, a][:, 0]
-            nc.vector.tensor_tensor(m, m, mask[e, a][:], MULT)
+        def apply_mask(e, a):
+            da1 = da[e, a][:, 0]
+            nc.vector.tensor_tensor(da1, da1, mask[e, a][:], MULT)
 
-        dc = {}
+        da_codes = {}
 
-        def quant_d(e, a):
-            c = dpool.tile([P, HP * 2 * P], U32, name="dc", align_bytes=64)
-            z = dpool.tile([P, HP * 2 * P], U8, name="ds", align_bytes=64)
+        def quantise_da(e, a):
+            codes = dpool.tile([P, 2 * HP * P], U32, name="dc", align_bytes=64)
+            scales = dpool.tile([P, 2 * HP * P], U8, name="ds", align_bytes=64)
             nc.vector.quantize_mx(
-                out=c[:].bitcast(FP8X4), scales=z[:], in_=dq[e, a][:].rearrange("p w h j t -> p (w h j t)")
+                out=codes[:].bitcast(FP8X4),
+                scales=scales[:],
+                in_=da[e, a][:].rearrange("p w h j t -> p (w h j t)"),
             )
-            dc[e, a] = (c, z)
+            da_codes[e, a] = (codes, scales)
 
-        dxs = {}
-
-        dxb = {}
-
-        def mm2(e, a, banks):
-            c, z = dc[e, a]
-            per = KT // len(banks)
-            for i, name in enumerate(banks):
-                b = psum.tile([P, per, P], F32, name=name)
-                dxb[e, a, i] = b
-                for n in range(per):
-                    kt = per * i + n
+        def second_product(e, a, banks):
+            codes, scales = da_codes[e, a]
+            per_bank = KT // len(banks)
+            sums = []
+            for number, name in enumerate(banks):
+                b = psum.tile([P, per_bank, P], F32, name=name)
+                sums.append(b)
+                for within in range(per_bank):
+                    kt = per_bank * number + within
                     for h in range(HP):
                         for w in range(2):
-                            r = slice(P * (HP * w + h), P * (HP * w + h + 1))
+                            cols = slice(P * (HP * w + h), P * (HP * w + h + 1))
                             nc.tensor.matmul_mx(
-                                out=b[:, n],
+                                out=b[:, within],
                                 lhsT=w13[e, w][:, h, 2 * P * kt : 2 * P * (kt + 1)].bitcast(FP4X4),
                                 lhsT_scale=w13s[:, e * HP + h, w, P * kt : P * (kt + 1)],
-                                rhs=c[:, r].bitcast(FP8X4),
-                                rhs_scale=z[:, r],
+                                rhs=codes[:, cols].bitcast(FP8X4),
+                                rhs_scale=scales[:, cols],
                                 start=(h == 0 and w == 0),
                                 stop=(h == HP - 1 and w == 1),
                             )
+            return sums
 
-        def dx_out(e, a, i, tag):
-            b = dxb[e, a, i]
-            per = b.shape[1]
-            d = keep.tile([P, per, P], F32, name=tag, align_bytes=64)
-            nc.scalar.copy(d[:], b[:])
-            for n in range(per):
-                dxs[e, a, per * i + n] = d[:, n]
+        dx = {}
+
+        def copy_dx(e, a, first_kt, bank_tile, buffer):
+            count = bank_tile.shape[1]
+            d = keep.tile([P, count, P], F32, name=buffer, align_bytes=64)
+            nc.scalar.copy(d[:], bank_tile[:])
+            for within in range(count):
+                dx[e, a, first_kt + within] = d[:, within]
 
         def scatter(e, a, kt):
             lo = (C * e + P * a) // 16
-            nc.vector.tensor_copy(
-                outs[kt][:].indirect(offsets[:, lo : lo + P // 16]), dxs[e, a, kt]
-            )
+            nc.vector.tensor_copy(outs[kt][:].indirect(offsets[:, lo : lo + P // 16]), dx[e, a, kt])
 
-        gxa = keep.tile([P, C], F32, name="slot_a", align_bytes=64)
-        nc.scalar.copy(gxa[:], gates[:, 0:C])
-        gxb = keep.tile([P, C], F32, name="slot_b", align_bytes=64)
-        nc.scalar.copy(gxb[:], gates[:, 0:C])
-        gb = {}
+        last = NP - 1
+
+        gates_early = keep.tile([P, C], F32, name="gates_early", align_bytes=64)
+        nc.scalar.copy(gates_early[:], gates[:, 0:C])
+        gates_late = keep.tile([P, C], F32, name="gates_late", align_bytes=64)
+        nc.scalar.copy(gates_late[:], gates[:, 0:C])
         new_relu(0, 0, "relu00")
         new_relu(0, 1, "relu01")
-        for s in range(3):
+        g_packed = {}
+        for s in range(last):
+            rows = gpool.tile([P, 4, S], F32, name="g_rows")
             for t in range(4):
-                gather(s, t, 0, S, gates[:])
+                gather(rows, s, t, 0, S, gates[:])
                 if t == 2 and s > 0:
-                    quant_g(gb[s - 1], s - 1, 0, C, 0, f"dy{s}1")
-                    mm1(s - 1, 0)
+                    quantise_g(g_packed[s - 1][:, 0:C], s - 1, 0, C, "dy21" if s == 2 else None)
+                    for a in range(AT):
+                        first_product(s - 1, 0, a, 0, last)
             if s < 2:
-                gb[s] = new_gb(S, "gb", 2)
-                interleave(gb[s], s, 0, 0, S, 0)
-                masks(s, 0, 0)
-                masks(s, 0, 1)
-        b20 = new_gb(C, "gb20", 1)
-        interleave(b20, 2, 0, 0, C, 0)
-        b21 = keep.tile([P, C, 4], BF16, name="slot_c", align_bytes=64)
-        interleave(b21, 2, 0, C, S, C)
-        gather(3, 0, 0, C, gxa[:])
-        gather(3, 1, 0, C, gxa[:])
-        quant_g(b20, 2, 0, C, 0, "slot_a")
-        mm1(2, 0)
-        gather(3, 2, 0, C, gxb[:])
-        gather(3, 3, 0, C, gxb[:])
-        b3 = new_gb(C, "gb3", 1)
+                g_packed[s] = new_packed(S, "g_packed", 2)
+                pack(g_packed[s][:], rows[:])
+                for a in range(AT):
+                    relu_and_mask(0, a, s)
+        packed20 = new_packed(C, "packed20", 1)
+        pack(packed20[:], rows[:, :, 0:C])
+        packed21 = new_packed(C, "packed21", 1)
+        pack(packed21[:], rows[:, :, C:S])
+
+        rows30 = gpool.tile([P, 4, C], F32, name="g_rows30")
+        gather(rows30, last, 0, 0, C, gates_early[:])
+        gather(rows30, last, 1, 0, C, gates_early[:])
+        quantise_g(packed20[:], 2, 0, C, "gates_early")
         for a in range(AT):
-            interleave(b3, 3, 0, P * a, P * (a + 1), 0)
-        quant_g(b21, 2, C, S, C, "slot_b")
-        gather(3, 0, C, S, gates[:, C:S], "slot_c")
-        quant_g(b3, 3, 0, P, 0)
-        mm1(3, 0, (0,))
-        gather(3, 1, C, S, gates[:, C:S])
-        quant_g(b3, 3, P, C, 0)
-        mm1(3, 0, (1,))
-        gather(3, 2, C, S, gates[:, C:S])
-        quant_g(gb[1], 1, C, S, 0, "dy31")
-        gather(3, 3, C, S, gates[:, C:S])
-        quant_g(gb[0], 0, C, S, 0, "dy32")
+            first_product(2, 0, a, 0, last)
+        gather(rows30, last, 2, 0, C, gates_late[:])
+        gather(rows30, last, 3, 0, C, gates_late[:])
+        packed30 = new_packed(C, "packed30", 1)
+        for a in range(AT):
+            pack(packed30[:, P * a : P * (a + 1)], rows30[:, :, P * a : P * (a + 1)])
+        rows31 = keep.tile([P, 4, C], F32, name="gates_late", align_bytes=64)
+        gather(rows31, last, 0, C, S, gates[:, C:S])
+        gather(rows31, last, 1, C, S, gates[:, C:S])
+        quantise_g(packed30[:, 0:P], last, 0, P)
+        first_product(last, 0, 0, 0, last)
+        quantise_g(packed21[:], 2, C, S, "dy30")
+        quantise_g(packed30[:, P:C], last, P, C)
+        first_product(last, 0, 1, 0, last)
+        gather(rows31, last, 2, C, S, gates[:, C:S])
+        quantise_g(g_packed[1][:, C:S], 1, C, S, "dy31")
+        gather(rows31, last, 3, C, S, gates[:, C:S])
+        quantise_g(g_packed[0][:, C:S], 0, C, S, "dy32")
         turn(0, 0, 0)
         turn(0, 0, 1)
         turn(0, 1, 0)
-        turn(0, 1, 1, "slot_d")
-        b31 = keep.tile([P, C, 4], BF16, name="slot_d", align_bytes=64)
-        interleave(b31, 3, C, C, S, C)
-        new_relu(1, 1, "slot_c")
-        masks(1, 1, 1)
-        masks(1, 1, 0)
-        for s in late_order[:2]:
-            mm1(s, 1, first=late_order[0])
-        new_dq(0, 0, "dq00")
-        prod1(0, 0, 0)
-        prod1(0, 0, 1)
-        prod3(0, 0, 0)
-        masked(0, 0)
-        prod3(0, 0, 1)
-        new_dq(0, 1, "mask00")
-        prod1(0, 1, 0)
-        quant_d(0, 0)
-        prod1(0, 1, 1)
-        quant_g(b31, 3, C, S, C, "dq00")
-        prod3(0, 1, 0)
-        masked(0, 1)
-        mm2(0, 0, ("bank000",))
-        dx_out(0, 0, 0, "mask01")
-        for a in (1, 0):
-            for s in late_order[2:]:
-                mm1(s, 1, (a,), first=late_order[0])
-        prod3(0, 1, 1)
+        turn(0, 1, 1, "last_turn0")
+        packed31 = keep.tile([P, C, 4], BF16, name="last_turn0", align_bytes=64)
+        pack(packed31[:], rows31[:])
+        new_relu(1, 1, "gates_late")
+        relu_and_mask(1, 1, 1)
+        relu_and_mask(1, 0, 1)
+        for s in (2, 1):
+            for a in range(AT):
+                first_product(s, 1, a, 2, last)
+
+        new_da(0, 0, "da00")
+        make_da1(0, 0, 0)
+        make_da1(0, 0, 1)
+        make_da3(0, 0, 0)
+        apply_mask(0, 0)
+        make_da3(0, 0, 1)
+        new_da(0, 1, "mask00")
+        make_da1(0, 1, 0)
+        quantise_da(0, 0)
+        make_da1(0, 1, 1)
+        quantise_g(packed31[:, P:C], last, C + P, S, "da00")
+        make_da3(0, 1, 0)
+        apply_mask(0, 1)
+        sums00 = second_product(0, 0, ("bank000",))
+        copy_dx(0, 0, 0, sums00[0], "mask01")
+        for s in (0, last):
+            first_product(s, 1, 1, 2, last)
+        make_da3(0, 1, 1)
         turn(1, 1, 0, "relu01")
-        quant_d(0, 1)
-        turn(1, 1, 1, "mask00")
-        mm2(0, 1, ("bank010", "bank001", "bank011"))
-        park(1, 1, 0, "park0")
-        park(1, 1, 1, "park1")
-        dx_out(0, 1, 0, "dx010")
-        dx_out(0, 1, 1, "dx011")
+        quantise_da(0, 1)
+        turn(1, 1, 1, "relu00")
+        quantise_g(packed31[:, 0:P], last, C, C + P, "mask00")
+        sums01 = second_product(0, 1, ("bank010", "bank001", "bank011"))
+        for h in range(HP):
+            park(1, 1, h)
+        for kt in range(KT - 1):
+            copy_dx(0, 1, kt, sums01[kt], f"dx01{kt}")
+        for s in (last, 0):
+            first_product(s, 1, 0, 2, 0)
         turn(1, 0, 0, "relu01", "bank001")
-        turn(1, 0, 1, "mask00")
+        turn(1, 0, 1, "relu00")
         new_relu(1, 0, "relu01")
-        relus(0, 1, 0)
-        relus(0, 1, 1)
-        sign(1, 0, 0)
-        sign(1, 1, 0)
-        new_dq(1, 1, "dq11")
-        prod1_g(1, 1, 0)
-        prod1_g(1, 1, 1)
-        prod3_g(1, 1, 1)
-        prod3_g(1, 1, 0)
+        for a in range(AT):
+            make_relu(1, a, 0)
+        for a in range(AT):
+            make_mask(1, a, 0)
+
+        new_da(1, 1, "da11")
+        make_da1_gpsimd(1, 1, 0)
+        make_da1_gpsimd(1, 1, 1)
+        make_da3_gpsimd(1, 1, 1)
+        make_da3_gpsimd(1, 1, 0)
         for kt in range(KT):
             scatter(0, 0, kt)
-        scatter(0, 1, 0)
-        scatter(0, 1, 1)
-        new_dq(1, 0, "dx011")
-        prod1(1, 0, 0)
-        prod1(1, 0, 1)
-        prod3(1, 0, 1)
-        prod3(1, 0, 0)
-        masked(1, 0)
-        masked(1, 1)
-        dx_out(0, 1, 2, "mask11")
-        quant_d(1, 0)
-        mm2(1, 0, ("bank000", "bank010", "bank100"))
-        quant_d(1, 1)
+        for kt in range(KT - 1):
+            scatter(0, 1, kt)
+        new_da(1, 0, "da10")
+        make_da1(1, 0, 0)
+        make_da1(1, 0, 1)
+        make_da3(1, 0, 1)
+        make_da3(1, 0, 0)
+        apply_mask(1, 0)
+        apply_mask(1, 1)
+        copy_dx(0, 1, KT - 1, sums01[KT - 1], "mask11")
+        quantise_da(1, 0)
+        sums10 = second_product(1, 0, ("bank000", "bank010", "bank100"))
+        quantise_da(1, 1)
         for kt in range(KT):
-            dx_out(1, 0, kt, f"dx10{kt}")
-        mm2(1, 1, ("bank110",))
-        dx_out(1, 1, 0, "dx11")
-        scatter(0, 1, 2)
+            copy_dx(1, 0, kt, sums10[kt], f"dx10{kt}")
+        sums11 = second_product(1, 1, ("bank110",))
+        copy_dx(1, 1, 0, sums11[0], "dx11")
+        scatter(0, 1, KT - 1)
         for kt in range(KT):
             scatter(1, 0, kt)
         for kt in range(KT):

@@ -68,7 +68,7 @@ def tile_moe_bdx_glu_relu_kernel(
         dy_rows = dyT.rearrange("(s p t) u -> s t p u", s=NP, p=P, t=4)
         a1_rows = a1.rearrange("(s p t) j -> s p t j", s=HP, p=P, t=4)
         a3_rows = a3.rearrange("(s p t) j -> s p t j", s=HP, p=P, t=4)
-        w2s_rows = w2_scales.bitcast(I32).rearrange("e s f i -> f e s i")
+        w2s_rows = w2_scales.bitcast(I32).rearrange("e s (q r) i -> r q e s i", r=4)
         dy = {}
         w2t = {}
         w13 = {}
@@ -87,7 +87,7 @@ def tile_moe_bdx_glu_relu_kernel(
             w2t[e, s] = words
 
         def load_w2s(e, q):
-            nc.sync.dma_start(w2s[e][32 * q : 32 * q + 4].bitcast(I32), w2s_rows[4 * q : 4 * q + 4, e])
+            nc.sync.dma_start(w2s[e][q:P:32].bitcast(I32), w2s_rows[q, :, e])
 
         def load_w13(e, w):
             words = keep.tile([P, HP, 2 * K], U8, name=f"w13_{e}{w}", align_bytes=64)
@@ -96,8 +96,8 @@ def tile_moe_bdx_glu_relu_kernel(
             w13[e, w] = words
 
         def load_w13s(w, q):
-            scale_rows = (w1_scales, w3_scales)[w].bitcast(I32).rearrange("e s f k -> f (e s) k")
-            nc.sync.dma_start(w13s[32 * q : 32 * q + 4, :, w].bitcast(I32), scale_rows[4 * q : 4 * q + 4])
+            scale_rows = (w1_scales, w3_scales)[w].bitcast(I32).rearrange("e s (q r) k -> r q (e s) k", r=4)
+            nc.sync.dma_start(w13s[q:P:32, :, w].bitcast(I32), scale_rows[q])
 
         def load_a1(e, h):
             rows = keep.tile([P, 4, C], F32, name=f"a1t{e}{h}")

@@ -43,6 +43,7 @@ def tile_moe_bdx_glu_relu_kernel(
         keep = ctx.enter_context(tc.tile_pool(name="keep", bufs=1))
         gpool = ctx.enter_context(tc.tile_pool(name="gpool", bufs=2))
         dpool = ctx.enter_context(tc.tile_pool(name="dpool", bufs=3))
+        placed = ctx.enter_context(tc.tile_pool(name="placed", bufs=1))
         psum = ctx.enter_context(tc.psum_pool(name="psum", bufs=1))
 
         offsets = keep.tile([P, S // 16], U16, name="offsets")
@@ -135,36 +136,38 @@ def tile_moe_bdx_glu_relu_kernel(
                 load_w13s(step, q)
         load_w2(1, 2)
         load_w2(1, 1)
+        load_w2(1, 0)
         load_w13(0, 0)
         load_w13(0, 1)
-        load_w2(1, 0)
         load_w2(1, 3)
         load_a1(1, 0)
-        load_a3(1, 0)
         load_a3(1, 1)
+        load_a3(1, 0)
         load_w13(1, 0)
         load_w13(1, 1)
 
         relu1 = {}
         mask = {}
 
-        def new_relu(e, h, buffer):
-            r = keep.tile([P, AT, P, 4], F32, name=buffer, align_bytes=64)
-            relu1[e, h] = r
-
-        def make_relu(e, a, h):
-            nc.scalar.activation(
-                walk_packed(relu1[e, h][:, a], 4), walk_rows(a1t[e, h][:, :, P * a : P * (a + 1)], 4), RELU
-            )
+        def make_relu(e, a, h, into=None):
+            if into is None:
+                own = keep.tile([P, P, 4], F32, name=f"relu{e}{a}{h}", align_bytes=64)
+                into = own[:]
+            r = into
+            relu1[e, a, h] = r
+            nc.scalar.activation(walk_packed(r, 4), walk_rows(a1t[e, h][:, :, P * a : P * (a + 1)], 4), RELU)
 
         def make_mask(e, a, h):
             if (e, a) not in mask:
-                m = keep.tile([P, HP, P, 4], BF16, name=f"mask{e}{a}", align_bytes=64)
+                if (e, a) == (0, 0):
+                    m = placed.tile([P, HP, P, 4], BF16, name="mask00", align_bytes=64, offset=0)
+                else:
+                    m = keep.tile([P, HP, P, 4], BF16, name=f"mask{e}{a}", align_bytes=64)
                 mask[e, a] = m
-            nc.scalar.activation(mask[e, a][:, h], relu1[e, h][:, a], SIGN)
+            nc.scalar.activation(mask[e, a][:, h], relu1[e, a, h], SIGN)
 
-        def relu_and_mask(e, a, h):
-            make_relu(e, a, h)
+        def relu_and_mask(e, a, h, buffer=None):
+            make_relu(e, a, h, buffer)
             make_mask(e, a, h)
 
         def gather(rows, s, t, lo, hi, weights):
@@ -183,7 +186,10 @@ def tile_moe_bdx_glu_relu_kernel(
 
         def quantise_g(packed, s, lo, hi, buffer=None):
             codes = keep.tile([P, hi - lo], U32, name=f"gc{s}_{lo}", align_bytes=64)
-            scales = keep.tile([P, hi - lo], U8, name=buffer or f"gs{s}_{lo}", align_bytes=64)
+            if buffer == "mask00":
+                scales = placed.tile([P, hi - lo], U8, name="gs_last", align_bytes=64, offset=0)
+            else:
+                scales = keep.tile([P, hi - lo], U8, name=buffer or f"gs{s}_{lo}", align_bytes=64)
             nc.vector.quantize_mx(
                 out=codes[:].bitcast(FP8X4), scales=scales[:], in_=packed.rearrange("p j t -> p (j t)")
             )
@@ -193,8 +199,8 @@ def tile_moe_bdx_glu_relu_kernel(
 
         bank = {}
 
-        def first_product(s, e, a, opens, closes):
-            for h in range(HP):
+        def first_product(s, e, a, opens, closes, halves=(0, 1)):
+            for h in halves:
                 if s == opens:
                     b = psum.tile([P, 512], F32, name=f"bank{e}{a}{h}")
                     bank[e, a, h] = b
@@ -222,7 +228,10 @@ def tile_moe_bdx_glu_relu_kernel(
         da = {}
 
         def new_da(e, a, buffer):
-            packed = keep.tile([P, 2, HP, P, 4], BF16, name=buffer, align_bytes=64)
+            if buffer == "mask00":
+                packed = placed.tile([P, 2, HP, P, 4], BF16, name=f"da{e}{a}", align_bytes=64, offset=P)
+            else:
+                packed = keep.tile([P, 2, HP, P, 4], BF16, name=buffer, align_bytes=64)
             da[e, a] = packed
 
         def make_da1(e, a, h):
@@ -235,7 +244,7 @@ def tile_moe_bdx_glu_relu_kernel(
 
         def make_da3(e, a, h):
             nc.vector.tensor_tensor(
-                da[e, a][:, 1, h], bank[e, a, h][:].rearrange("p t j -> p j t"), relu1[e, h][:, a], MULT
+                da[e, a][:, 1, h], bank[e, a, h][:].rearrange("p t j -> p j t"), relu1[e, a, h], MULT
             )
 
         parked = {}
@@ -250,7 +259,7 @@ def tile_moe_bdx_glu_relu_kernel(
             nc.gpsimd.tensor_tensor(da[e, a][:, 0, h], parked[h][:], a3_packed, MULT)
 
         def make_da3_gpsimd(e, a, h):
-            nc.gpsimd.tensor_tensor(da[e, a][:, 1, h], parked[h][:], relu1[e, h][:, a], MULT)
+            nc.gpsimd.tensor_tensor(da[e, a][:, 1, h], parked[h][:], relu1[e, a, h], MULT)
 
         def apply_mask(e, a):
             da1 = da[e, a][:, 0]
@@ -310,8 +319,6 @@ def tile_moe_bdx_glu_relu_kernel(
         nc.scalar.copy(gates_early[:], gates[:, 0:C])
         gates_late = keep.tile([P, C], F32, name="gates_late", align_bytes=64)
         nc.scalar.copy(gates_late[:], gates[:, 0:C])
-        new_relu(0, 0, "relu00")
-        new_relu(0, 1, "relu01")
         g_packed = {}
         for s in range(last):
             rows = gpool.tile([P, 4, S], F32, name="g_rows")
@@ -359,12 +366,13 @@ def tile_moe_bdx_glu_relu_kernel(
         turn(0, 1, 0)
         turn(0, 1, 1, "last_turn0")
         packed31 = keep.tile([P, C, 4], BF16, name="last_turn0", align_bytes=64)
-        pack(packed31[:], rows31[:])
-        new_relu(1, 1, "gates_late")
-        relu_and_mask(1, 1, 1)
-        relu_and_mask(1, 0, 1)
-        for s in (2, 1):
-            for a in range(AT):
+        pack(packed31[:, P:C], rows31[:, :, P:C])
+        pack(packed31[:, 0:P], rows31[:, :, 0:P])
+        relu_late = keep.tile([P, AT, P, 4], F32, name="gates_late", align_bytes=64)
+        relu_and_mask(1, 1, 1, relu_late[:, 1])
+        relu_and_mask(1, 0, 1, relu_late[:, 0])
+        for s in (2, 1, 0):
+            for a in (1, 0):
                 first_product(s, 1, a, 2, last)
 
         new_da(0, 0, "da00")
@@ -373,60 +381,57 @@ def tile_moe_bdx_glu_relu_kernel(
         make_da3(0, 0, 0)
         apply_mask(0, 0)
         make_da3(0, 0, 1)
+        quantise_g(packed31[:, P:C], last, C + P, S, "mask00")
         new_da(0, 1, "mask00")
         make_da1(0, 1, 0)
         quantise_da(0, 0)
         make_da1(0, 1, 1)
-        quantise_g(packed31[:, P:C], last, C + P, S, "da00")
         make_da3(0, 1, 0)
         apply_mask(0, 1)
-        sums00 = second_product(0, 0, ("bank000",))
-        copy_dx(0, 0, 0, sums00[0], "mask01")
-        for s in (0, last):
-            first_product(s, 1, 1, 2, last)
+        first_product(last, 1, 1, 2, last, (1, 0))
+        turn(1, 1, 1, None, "bank000")
+        turn(1, 1, 0, "turn110", "bank111")
+        park(1, 1, 1)
+        sums00 = second_product(0, 0, ("bank001",))
+        copy_dx(0, 0, 0, sums00[0], "dx00")
+        park(1, 1, 0)
         make_da3(0, 1, 1)
-        turn(1, 1, 0, "relu01")
         quantise_da(0, 1)
-        turn(1, 1, 1, "relu00")
-        quantise_g(packed31[:, 0:P], last, C, C + P, "mask00")
-        sums01 = second_product(0, 1, ("bank010", "bank001", "bank011"))
-        for h in range(HP):
-            park(1, 1, h)
+        quantise_g(packed31[:, 0:P], last, C, C + P, "turn110")
+        make_relu(1, 1, 0)
+        sums01 = second_product(0, 1, ("bank110",))
         for kt in range(KT - 1):
-            copy_dx(0, 1, kt, sums01[kt], f"dx01{kt}")
-        for s in (last, 0):
-            first_product(s, 1, 0, 2, 0)
-        turn(1, 0, 0, "relu01", "bank001")
-        turn(1, 0, 1, "relu00")
-        new_relu(1, 0, "relu01")
-        for a in range(AT):
-            make_relu(1, a, 0)
+            copy_dx(0, 1, kt, sums01[0][:, kt : kt + 1], f"dx01{kt}")
+        first_product(last, 1, 0, 2, last, (1, 0))
+        turn(1, 0, 1)
+        turn(1, 0, 0)
+        make_relu(1, 0, 0)
         for a in range(AT):
             make_mask(1, a, 0)
 
-        new_da(1, 1, "da11")
-        make_da1_gpsimd(1, 1, 0)
-        make_da1_gpsimd(1, 1, 1)
+        new_da(1, 1, "mask00")
         make_da3_gpsimd(1, 1, 1)
         make_da3_gpsimd(1, 1, 0)
+        make_da1_gpsimd(1, 1, 1)
+        make_da1_gpsimd(1, 1, 0)
         for kt in range(KT):
             scatter(0, 0, kt)
         for kt in range(KT - 1):
             scatter(0, 1, kt)
-        new_da(1, 0, "da10")
-        make_da1(1, 0, 0)
+        new_da(1, 0, "dx010")
         make_da1(1, 0, 1)
         make_da3(1, 0, 1)
+        make_da1(1, 0, 0)
         make_da3(1, 0, 0)
         apply_mask(1, 0)
         apply_mask(1, 1)
-        copy_dx(0, 1, KT - 1, sums01[KT - 1], "mask11")
+        copy_dx(0, 1, KT - 1, sums01[0][:, KT - 1 : KT], "mask11")
         quantise_da(1, 0)
-        sums10 = second_product(1, 0, ("bank000", "bank010", "bank100"))
+        sums10 = second_product(1, 0, ("bank001", "bank010", "bank011"))
         quantise_da(1, 1)
         for kt in range(KT):
             copy_dx(1, 0, kt, sums10[kt], f"dx10{kt}")
-        sums11 = second_product(1, 1, ("bank110",))
+        sums11 = second_product(1, 1, ("bank000",))
         copy_dx(1, 1, 0, sums11[0], "dx11")
         scatter(0, 1, KT - 1)
         for kt in range(KT):

@@ -140,8 +140,8 @@ def tile_moe_bdx_glu_relu_kernel(
         load_w13(0, 0)
         load_w13(0, 1)
         load_w2(1, 3)
-        load_a1(1, 0)
         load_a3(1, 1)
+        load_a1(1, 0)
         load_a3(1, 0)
         load_w13(1, 0)
         load_w13(1, 1)
@@ -170,9 +170,17 @@ def tile_moe_bdx_glu_relu_kernel(
             make_relu(e, a, h, buffer)
             make_mask(e, a, h)
 
+        def relu_and_mask_rows(e, a, h):
+            r = keep.tile([P, 4, P], F32, name=f"relu{e}{a}{h}", align_bytes=64)
+            nc.scalar.activation(r[:], a1t[e, h][:, :, P * a : P * (a + 1)], RELU)
+            relu1[e, a, h] = r[:]
+            m = keep.tile([P, 4, P], BF16, name=f"mask{e}{a}{h}", align_bytes=64)
+            nc.scalar.activation(m[:], r[:], SIGN)
+            mask[e, a, h] = m
+
         def gather(rows, s, t, lo, hi, weights):
             nc.vector.tensor_tensor(
-                rows[:, t, :], dy[s, t][:].indirect(offsets[:, lo // 16 : hi // 16]), weights, MULT
+                rows, dy[s, t][:].indirect(offsets[:, lo // 16 : hi // 16]), weights, MULT
             )
 
         def new_packed(width, name, bufs):
@@ -216,10 +224,14 @@ def tile_moe_bdx_glu_relu_kernel(
 
         def turn(e, a, h, buffer=None, into=None):
             if buffer is None:
-                sorted_dh = dpool.tile([P, 4, P], F32, name="sorted_dh")
+                own = dpool.tile([P, 4, P], F32, name="sorted_dh")
+                sorted_dh = own[:]
+            elif isinstance(buffer, str):
+                own = keep.tile([P, 4, P], F32, name=buffer, align_bytes=64)
+                sorted_dh = own[:]
             else:
-                sorted_dh = keep.tile([P, 4, P], F32, name=buffer, align_bytes=64)
-            nc.scalar.copy(sorted_dh[:], bank[e, a, h][:].rearrange("p (m t) -> p t m", t=4))
+                sorted_dh = buffer
+            nc.scalar.copy(sorted_dh, bank[e, a, h][:].rearrange("p (m t) -> p t m", t=4))
             b = psum.tile([P, 4, P], F32, name=into or f"bank{e}{a}{h}")
             for t in range(4):
                 nc.tensor.transpose(b[:, t, :], sorted_dh[:, t, :], ident[:])
@@ -229,7 +241,7 @@ def tile_moe_bdx_glu_relu_kernel(
 
         def new_da(e, a, buffer):
             if buffer == "mask00":
-                packed = placed.tile([P, 2, HP, P, 4], BF16, name=f"da{e}{a}", align_bytes=64, offset=P)
+                packed = placed.tile([P, 2, HP, P, 4], BF16, name=f"da{e}{a}", align_bytes=64, offset=C)
             else:
                 packed = keep.tile([P, 2, HP, P, 4], BF16, name=buffer, align_bytes=64)
             da[e, a] = packed
@@ -247,10 +259,13 @@ def tile_moe_bdx_glu_relu_kernel(
                 da[e, a][:, 1, h], bank[e, a, h][:].rearrange("p t j -> p j t"), relu1[e, a, h], MULT
             )
 
+        def product_rows(into, e, a, h, rows):
+            nc.vector.tensor_tensor(walk_packed(into, 2), walk_rows(bank[e, a, h][:], 2), walk_rows(rows, 2), MULT)
+
         parked = {}
 
-        def park(e, a, h):
-            dh = keep.tile([P, P, 4], F32, name=f"park{h}", align_bytes=64)
+        def park(e, a, h, buffer):
+            dh = keep.tile([P, P, 4], F32, name=buffer, align_bytes=64)
             nc.scalar.copy(dh[:], bank[e, a, h][:].rearrange("p t j -> p j t"))
             parked[h] = dh
 
@@ -268,33 +283,44 @@ def tile_moe_bdx_glu_relu_kernel(
         da_codes = {}
 
         def quantise_da(e, a):
-            codes = dpool.tile([P, 2 * HP * P], U32, name="dc", align_bytes=64)
+            codes = keep.tile([P, 2 * HP * P], U32, name=f"dc{e}{a}", align_bytes=64)
             scales = dpool.tile([P, 2 * HP * P], U8, name="ds", align_bytes=64)
             nc.vector.quantize_mx(
                 out=codes[:].bitcast(FP8X4),
                 scales=scales[:],
                 in_=da[e, a][:].rearrange("p w h j t -> p (w h j t)"),
             )
-            da_codes[e, a] = (codes, scales)
+            for w in range(2):
+                for h in range(HP):
+                    cols = slice(P * (HP * w + h), P * (HP * w + h + 1))
+                    da_codes[e, a, w, h] = (codes[:, cols], scales[:, cols])
 
-        def second_product(e, a, banks):
-            codes, scales = da_codes[e, a]
-            per_bank = KT // len(banks)
+        def quantise_da_half(e, a, h, half, codes, scales):
+            both = slice(2 * P * h, 2 * P * (h + 1))
+            nc.vector.quantize_mx(
+                out=codes[:, both].bitcast(FP8X4), scales=scales[:, both], in_=half[:].rearrange("p w j t -> p (w j t)")
+            )
+            for w in range(2):
+                cols = slice(P * (2 * h + w), P * (2 * h + w + 1))
+                da_codes[e, a, w, h] = (codes[:, cols], scales[:, cols])
+
+        def second_product(e, a, banks, first_kt=0, count=KT):
+            per_bank = count // len(banks)
             sums = []
             for number, name in enumerate(banks):
                 b = psum.tile([P, per_bank, P], F32, name=name)
                 sums.append(b)
                 for within in range(per_bank):
-                    kt = per_bank * number + within
+                    kt = first_kt + per_bank * number + within
                     for h in range(HP):
                         for w in range(2):
-                            cols = slice(P * (HP * w + h), P * (HP * w + h + 1))
+                            codes, scales = da_codes[e, a, w, h]
                             nc.tensor.matmul_mx(
                                 out=b[:, within],
                                 lhsT=w13[e, w][:, h, 2 * P * kt : 2 * P * (kt + 1)].bitcast(FP4X4),
                                 lhsT_scale=w13s[:, e * HP + h, w, P * kt : P * (kt + 1)],
-                                rhs=codes[:, cols].bitcast(FP8X4),
-                                rhs_scale=scales[:, cols],
+                                rhs=codes.bitcast(FP8X4),
+                                rhs_scale=scales,
                                 start=(h == 0 and w == 0),
                                 stop=(h == HP - 1 and w == 1),
                             )
@@ -315,15 +341,15 @@ def tile_moe_bdx_glu_relu_kernel(
 
         last = NP - 1
 
-        gates_early = keep.tile([P, C], F32, name="gates_early", align_bytes=64)
-        nc.scalar.copy(gates_early[:], gates[:, 0:C])
-        gates_late = keep.tile([P, C], F32, name="gates_late", align_bytes=64)
-        nc.scalar.copy(gates_late[:], gates[:, 0:C])
+        gates_early = keep.tile([P, P], F32, name="gates_early", align_bytes=64)
+        nc.scalar.copy(gates_early[:], gates[:, 0:P])
+        gates_late = keep.tile([P, P], F32, name="gates_late", align_bytes=64)
+        nc.scalar.copy(gates_late[:], gates[:, 0:P])
         g_packed = {}
         for s in range(last):
             rows = gpool.tile([P, 4, S], F32, name="g_rows")
             for t in range(4):
-                gather(rows, s, t, 0, S, gates[:])
+                gather(rows[:, t], s, t, 0, S, gates[:])
                 if t == 2 and s > 0:
                     quantise_g(g_packed[s - 1][:, 0:C], s - 1, 0, C, "dy21" if s == 2 else None)
                     for a in range(AT):
@@ -331,43 +357,47 @@ def tile_moe_bdx_glu_relu_kernel(
             if s < 2:
                 g_packed[s] = new_packed(S, "g_packed", 2)
                 pack(g_packed[s][:], rows[:])
-                for a in range(AT):
-                    relu_and_mask(0, a, s)
+                relu_and_mask(0, 0, s)
+                relu_and_mask_rows(0, 1, s)
         packed20 = new_packed(C, "packed20", 1)
         pack(packed20[:], rows[:, :, 0:C])
         packed21 = new_packed(C, "packed21", 1)
         pack(packed21[:], rows[:, :, C:S])
 
         rows30 = gpool.tile([P, 4, C], F32, name="g_rows30")
-        gather(rows30, last, 0, 0, C, gates_early[:])
-        gather(rows30, last, 1, 0, C, gates_early[:])
+        gather(rows30[:, 0], last, 0, 0, C, gates[:, 0:C])
+        gather(rows30[:, 1], last, 1, 0, C, gates[:, 0:C])
+        gather(rows30[:, 2, 0:P], last, 2, 0, P, gates_early[:])
+        gather(rows30[:, 2, P:C], last, 2, P, C, gates[:, P:C])
         quantise_g(packed20[:], 2, 0, C, "gates_early")
         for a in range(AT):
             first_product(2, 0, a, 0, last)
-        gather(rows30, last, 2, 0, C, gates_late[:])
-        gather(rows30, last, 3, 0, C, gates_late[:])
+        gather(rows30[:, 3, 0:P], last, 3, 0, P, gates_late[:])
+        gather(rows30[:, 3, P:C], last, 3, P, C, gates[:, P:C])
         packed30 = new_packed(C, "packed30", 1)
         for a in range(AT):
             pack(packed30[:, P * a : P * (a + 1)], rows30[:, :, P * a : P * (a + 1)])
         rows31 = keep.tile([P, 4, C], F32, name="gates_late", align_bytes=64)
-        gather(rows31, last, 0, C, S, gates[:, C:S])
-        gather(rows31, last, 1, C, S, gates[:, C:S])
+        gather(rows31[:, 0], last, 0, C, S, gates[:, C:S])
+        gather(rows31[:, 1], last, 1, C, S, gates[:, C:S])
         quantise_g(packed30[:, 0:P], last, 0, P)
         first_product(last, 0, 0, 0, last)
         quantise_g(packed21[:], 2, C, S, "dy30")
         quantise_g(packed30[:, P:C], last, P, C)
         first_product(last, 0, 1, 0, last)
-        gather(rows31, last, 2, C, S, gates[:, C:S])
+        gather(rows31[:, 2], last, 2, C, S, gates[:, C:S])
         quantise_g(g_packed[1][:, C:S], 1, C, S, "dy31")
-        gather(rows31, last, 3, C, S, gates[:, C:S])
+        gather(rows31[:, 3], last, 3, C, S, gates[:, C:S])
         quantise_g(g_packed[0][:, C:S], 0, C, S, "dy32")
+        masked_a3 = keep.tile([P, HP, 4, P], F32, name="dy33", align_bytes=64)
+        for h in range(HP):
+            nc.gpsimd.tensor_tensor(masked_a3[:, h], a3t[0, h][:, :, P:C], mask[0, 1, h][:], MULT)
         turn(0, 0, 0)
         turn(0, 0, 1)
         turn(0, 1, 0)
         turn(0, 1, 1, "last_turn0")
         packed31 = keep.tile([P, C, 4], BF16, name="last_turn0", align_bytes=64)
-        pack(packed31[:, P:C], rows31[:, :, P:C])
-        pack(packed31[:, 0:P], rows31[:, :, 0:P])
+        pack(packed31[:], rows31[:])
         relu_late = keep.tile([P, AT, P, 4], F32, name="gates_late", align_bytes=64)
         relu_and_mask(1, 1, 1, relu_late[:, 1])
         relu_and_mask(1, 0, 1, relu_late[:, 0])
@@ -376,46 +406,54 @@ def tile_moe_bdx_glu_relu_kernel(
                 first_product(s, 1, a, 2, last)
 
         new_da(0, 0, "da00")
-        make_da1(0, 0, 0)
-        make_da1(0, 0, 1)
         make_da3(0, 0, 0)
-        apply_mask(0, 0)
+        make_da1(0, 0, 0)
         make_da3(0, 0, 1)
-        quantise_g(packed31[:, P:C], last, C + P, S, "mask00")
-        new_da(0, 1, "mask00")
-        make_da1(0, 1, 0)
+        make_da1(0, 0, 1)
+        half0 = keep.tile([P, 2, P, 4], BF16, name="relu001", align_bytes=64)
+        product_rows(half0[:, 1], 0, 1, 0, relu1[0, 1, 0])
+        apply_mask(0, 0)
+        product_rows(half0[:, 0], 0, 1, 0, masked_a3[:, 0])
+        quantise_g(packed31[:], last, C, S, "mask00")
+        half1 = placed.tile([P, 2, P, 4], BF16, name="half1", align_bytes=64, offset=C)
         quantise_da(0, 0)
-        make_da1(0, 1, 1)
-        make_da3(0, 1, 0)
-        apply_mask(0, 1)
+        product_rows(half1[:, 0], 0, 1, 1, masked_a3[:, 1])
+        product_rows(half1[:, 1], 0, 1, 1, relu1[0, 1, 1])
+        codes01 = keep.tile([P, 2 * HP * P], U32, name="dc01", align_bytes=64)
+        scales01 = dpool.tile([P, 2 * HP * P], U8, name="ds", align_bytes=64)
+        quantise_da_half(0, 1, 0, half0, codes01, scales01)
+        quantise_da_half(0, 1, 1, half1, codes01, scales01)
+
         first_product(last, 1, 1, 2, last, (1, 0))
+        sums000 = second_product(0, 0, ("bank001",), 0, 1)
+        copy_dx(0, 0, 0, sums000[0], "dx000")
         turn(1, 1, 1, None, "bank000")
+        sums001 = second_product(0, 0, ("bank010",), 1, KT - 1)
         turn(1, 1, 0, "turn110", "bank111")
-        park(1, 1, 1)
-        sums00 = second_product(0, 0, ("bank001",))
-        copy_dx(0, 0, 0, sums00[0], "dx00")
-        park(1, 1, 0)
-        make_da3(0, 1, 1)
-        quantise_da(0, 1)
-        quantise_g(packed31[:, 0:P], last, C, C + P, "turn110")
-        make_relu(1, 1, 0)
+        park(1, 1, 1, "park1")
+        copy_dx(0, 0, 1, sums001[0], "dx001")
+        park(1, 1, 0, "dc00")
+        scatter(0, 0, 0)
+        scatter(0, 0, 1)
         sums01 = second_product(0, 1, ("bank110",))
         for kt in range(KT - 1):
             copy_dx(0, 1, kt, sums01[0][:, kt : kt + 1], f"dx01{kt}")
+        relu_last = keep.tile([P, AT, P, 4], F32, name="dc01", align_bytes=64)
+        make_relu(1, 1, 0, relu_last[:, 1])
         first_product(last, 1, 0, 2, last, (1, 0))
-        turn(1, 0, 1)
-        turn(1, 0, 0)
-        make_relu(1, 0, 0)
+        sorted10 = keep.tile([P, HP, 4, P], F32, name="turn110", align_bytes=64)
+        turn(1, 0, 1, sorted10[:, 1])
+        turn(1, 0, 0, sorted10[:, 0])
+        make_relu(1, 0, 0, relu_last[:, 0])
         for a in range(AT):
             make_mask(1, a, 0)
 
         new_da(1, 1, "mask00")
         make_da3_gpsimd(1, 1, 1)
-        make_da3_gpsimd(1, 1, 0)
         make_da1_gpsimd(1, 1, 1)
         make_da1_gpsimd(1, 1, 0)
-        for kt in range(KT):
-            scatter(0, 0, kt)
+        make_da3_gpsimd(1, 1, 0)
+        scatter(0, 0, 2)
         for kt in range(KT - 1):
             scatter(0, 1, kt)
         new_da(1, 0, "dx010")

@@ -11,6 +11,8 @@ HP = H // 512
 KT = K // P
 AT = C // P
 
+LATE = 4608
+
 FLOPS = 2 * S * N * H + 2 * 2 * S * H * K
 BYTES = 4 * (N * T + 2 * H * S + P * S + K * T) + E * (N * H + 2 * H * K) * 17 // 32 + 2 * S * 8
 
@@ -49,7 +51,7 @@ def tile_moe_bdx_glu_relu_kernel(
         offsets = keep.tile([P, S // 16], U16, name="offsets")
         nc.sync.dma_start(offsets[:], offs)
         gates = keep.tile([P, S], F32, name="gates")
-        nc.scalar.dma_start(gates[:], gate[0:P, :])
+        nc.scalar.dma_start(gates[:, 0:P], gate[0:P, 0:P])
 
         ident = keep.tile([P, P], F32, name="ident")
         make_identity(nc, ident[:])
@@ -80,6 +82,8 @@ def tile_moe_bdx_glu_relu_kernel(
             for t in range(4):
                 d = keep.tile([P, T], F32, name=f"dy{s}{t}", align_bytes=64)
                 nc.sync.dma_start(d[:], dy_rows[s, t])
+                if (s, t) == (0, 0):
+                    nc.sync.dma_start(gates[:, P:S], gate[0:P, P:S])
                 dy[s, t] = d
 
         def load_w2(e, s):
@@ -112,7 +116,10 @@ def tile_moe_bdx_glu_relu_kernel(
                 a1t[e, h] = rows[:, :, C * e : C * (e + 1)]
 
         def load_a3(e, h):
-            rows = keep.tile([P, 4, C], F32, name=f"a3t{e}{h}")
+            if (e, h) == (0, 1):
+                rows = placed.tile([P, 4, C], F32, name="a3t01", align_bytes=64, offset=0)
+            else:
+                rows = keep.tile([P, 4, C], F32, name=f"a3t{e}{h}")
             nc.sync.dma_start(rows[:], a3_rows[h][:, :, C * e : C * (e + 1)])
             a3t[e, h] = rows
 
@@ -157,12 +164,9 @@ def tile_moe_bdx_glu_relu_kernel(
             relu1[e, a, h] = r
             nc.scalar.activation(walk_packed(r, 4), walk_rows(a1t[e, h][:, :, P * a : P * (a + 1)], 4), RELU)
 
-        def make_mask(e, a, h):
+        def make_mask(e, a, h, buffer=None):
             if (e, a) not in mask:
-                if (e, a) == (0, 0):
-                    m = placed.tile([P, HP, P, 4], BF16, name="mask00", align_bytes=64, offset=0)
-                else:
-                    m = keep.tile([P, HP, P, 4], BF16, name=f"mask{e}{a}", align_bytes=64)
+                m = keep.tile([P, HP, P, 4], BF16, name=buffer or f"mask{e}{a}", align_bytes=64)
                 mask[e, a] = m
             nc.scalar.activation(mask[e, a][:, h], relu1[e, a, h], SIGN)
 
@@ -196,6 +200,8 @@ def tile_moe_bdx_glu_relu_kernel(
             codes = keep.tile([P, hi - lo], U32, name=f"gc{s}_{lo}", align_bytes=64)
             if buffer == "mask00":
                 scales = placed.tile([P, hi - lo], U8, name="gs_last", align_bytes=64, offset=0)
+            elif buffer == "gates_late":
+                scales = placed.tile([P, hi - lo], U8, name=f"gs{s}_{lo}", align_bytes=64, offset=LATE - 192 + C * s)
             else:
                 scales = keep.tile([P, hi - lo], U8, name=buffer or f"gs{s}_{lo}", align_bytes=64)
             nc.vector.quantize_mx(
@@ -343,13 +349,17 @@ def tile_moe_bdx_glu_relu_kernel(
 
         gates_early = keep.tile([P, P], F32, name="gates_early", align_bytes=64)
         nc.scalar.copy(gates_early[:], gates[:, 0:P])
-        gates_late = keep.tile([P, P], F32, name="gates_late", align_bytes=64)
+        gates_late = placed.tile([P, P], F32, name="gates_late", align_bytes=64, offset=LATE)
         nc.scalar.copy(gates_late[:], gates[:, 0:P])
         g_packed = {}
         for s in range(last):
             rows = gpool.tile([P, 4, S], F32, name="g_rows")
             for t in range(4):
-                gather(rows[:, t], s, t, 0, S, gates[:])
+                if (s, t) == (0, 0):
+                    gather(rows[:, t, 0:P], s, t, 0, P, gates[:, 0:P])
+                    gather(rows[:, t, P:S], s, t, P, S, gates[:, P:S])
+                else:
+                    gather(rows[:, t], s, t, 0, S, gates[:])
                 if t == 2 and s > 0:
                     quantise_g(g_packed[s - 1][:, 0:C], s - 1, 0, C, "dy21" if s == 2 else None)
                     for a in range(AT):
@@ -364,7 +374,7 @@ def tile_moe_bdx_glu_relu_kernel(
         packed21 = new_packed(C, "packed21", 1)
         pack(packed21[:], rows[:, :, C:S])
 
-        rows30 = gpool.tile([P, 4, C], F32, name="g_rows30")
+        rows30 = keep.tile([P, 4, C], F32, name="rows3", align_bytes=64)
         gather(rows30[:, 0], last, 0, 0, C, gates[:, 0:C])
         gather(rows30[:, 1], last, 1, 0, C, gates[:, 0:C])
         gather(rows30[:, 2, 0:P], last, 2, 0, P, gates_early[:])
@@ -377,29 +387,27 @@ def tile_moe_bdx_glu_relu_kernel(
         packed30 = new_packed(C, "packed30", 1)
         for a in range(AT):
             pack(packed30[:, P * a : P * (a + 1)], rows30[:, :, P * a : P * (a + 1)])
-        rows31 = keep.tile([P, 4, C], F32, name="gates_late", align_bytes=64)
-        gather(rows31[:, 0], last, 0, C, S, gates[:, C:S])
-        gather(rows31[:, 1], last, 1, C, S, gates[:, C:S])
         quantise_g(packed30[:, 0:P], last, 0, P)
         first_product(last, 0, 0, 0, last)
-        quantise_g(packed21[:], 2, C, S, "dy30")
         quantise_g(packed30[:, P:C], last, P, C)
         first_product(last, 0, 1, 0, last)
-        gather(rows31[:, 2], last, 2, C, S, gates[:, C:S])
-        quantise_g(g_packed[1][:, C:S], 1, C, S, "dy31")
-        gather(rows31[:, 3], last, 3, C, S, gates[:, C:S])
-        quantise_g(g_packed[0][:, C:S], 0, C, S, "dy32")
+        quantise_g(g_packed[0][:, C:S], 0, C, S, "gates_late")
+        quantise_g(g_packed[1][:, C:S], 1, C, S, "gates_late")
+        quantise_g(packed21[:], 2, C, S, "gates_late")
+        rows31 = keep.tile([P, 4, C], F32, name="rows3", align_bytes=64)
+        for t in range(4):
+            gather(rows31[:, t], last, t, C, S, gates[:, C:S])
         masked_a3 = keep.tile([P, HP, 4, P], F32, name="dy33", align_bytes=64)
         for h in range(HP):
             nc.gpsimd.tensor_tensor(masked_a3[:, h], a3t[0, h][:, :, P:C], mask[0, 1, h][:], MULT)
         turn(0, 0, 0)
         turn(0, 0, 1)
-        turn(0, 1, 0)
-        turn(0, 1, 1, "last_turn0")
+        turn(0, 1, 0, "last_turn0")
+        turn(0, 1, 1)
         packed31 = keep.tile([P, C, 4], BF16, name="last_turn0", align_bytes=64)
         pack(packed31[:], rows31[:])
-        relu_late = keep.tile([P, AT, P, 4], F32, name="gates_late", align_bytes=64)
-        relu_and_mask(1, 1, 1, relu_late[:, 1])
+        relu_late = keep.tile([P, AT, P, 4], F32, name="rows3", align_bytes=64)
+        make_relu(1, 1, 1, relu_late[:, 1])
         relu_and_mask(1, 0, 1, relu_late[:, 0])
         for s in (2, 1, 0):
             for a in (1, 0):
@@ -412,13 +420,13 @@ def tile_moe_bdx_glu_relu_kernel(
         make_da1(0, 0, 1)
         half0 = keep.tile([P, 2, P, 4], BF16, name="relu001", align_bytes=64)
         product_rows(half0[:, 1], 0, 1, 0, relu1[0, 1, 0])
-        apply_mask(0, 0)
         product_rows(half0[:, 0], 0, 1, 0, masked_a3[:, 0])
+        apply_mask(0, 0)
         quantise_g(packed31[:], last, C, S, "mask00")
         half1 = placed.tile([P, 2, P, 4], BF16, name="half1", align_bytes=64, offset=C)
         quantise_da(0, 0)
-        product_rows(half1[:, 0], 0, 1, 1, masked_a3[:, 1])
         product_rows(half1[:, 1], 0, 1, 1, relu1[0, 1, 1])
+        product_rows(half1[:, 0], 0, 1, 1, masked_a3[:, 1])
         codes01 = keep.tile([P, 2 * HP * P], U32, name="dc01", align_bytes=64)
         scales01 = dpool.tile([P, 2 * HP * P], U8, name="ds", align_bytes=64)
         quantise_da_half(0, 1, 0, half0, codes01, scales01)
@@ -445,8 +453,9 @@ def tile_moe_bdx_glu_relu_kernel(
         turn(1, 0, 1, sorted10[:, 1])
         turn(1, 0, 0, sorted10[:, 0])
         make_relu(1, 0, 0, relu_last[:, 0])
-        for a in range(AT):
-            make_mask(1, a, 0)
+        make_mask(1, 0, 0)
+        for h in range(HP):
+            make_mask(1, 1, h, "turn110")
 
         new_da(1, 1, "mask00")
         make_da3_gpsimd(1, 1, 1)
@@ -463,7 +472,7 @@ def tile_moe_bdx_glu_relu_kernel(
         make_da3(1, 0, 0)
         apply_mask(1, 0)
         apply_mask(1, 1)
-        copy_dx(0, 1, KT - 1, sums01[0][:, KT - 1 : KT], "mask11")
+        copy_dx(0, 1, KT - 1, sums01[0][:, KT - 1 : KT], "turn110")
         quantise_da(1, 0)
         sums10 = second_product(1, 0, ("bank001", "bank010", "bank011"))
         quantise_da(1, 1)

@@ -141,9 +141,9 @@ def tile_moe_bdx_glu_relu_kernel(
             load_a3(0, step)
             for q in range(4):
                 load_w13s(step, q)
-        load_w2(1, 2)
-        load_w2(1, 1)
         load_w2(1, 0)
+        load_w2(1, 1)
+        load_w2(1, 2)
         load_w13(0, 0)
         load_w13(0, 1)
         load_w2(1, 3)
@@ -371,32 +371,34 @@ def tile_moe_bdx_glu_relu_kernel(
                 relu_and_mask_rows(0, 1, s)
         packed20 = new_packed(C, "packed20", 1)
         pack(packed20[:], rows[:, :, 0:C])
-        packed21 = new_packed(C, "packed21", 1)
-        pack(packed21[:], rows[:, :, C:S])
 
-        rows30 = keep.tile([P, 4, C], F32, name="rows3", align_bytes=64)
-        gather(rows30[:, 0], last, 0, 0, C, gates[:, 0:C])
-        gather(rows30[:, 1], last, 1, 0, C, gates[:, 0:C])
-        gather(rows30[:, 2, 0:P], last, 2, 0, P, gates_early[:])
-        gather(rows30[:, 2, P:C], last, 2, P, C, gates[:, P:C])
+        rows300 = keep.tile([P, 4, P], F32, name="rows3", align_bytes=64)
+        rows301 = keep.tile([P, 4, P], F32, name="rows301", align_bytes=64)
+        for t in range(2):
+            gather(rows300[:, t], last, t, 0, P, gates[:, 0:P])
+            gather(rows301[:, t], last, t, P, C, gates[:, P:C])
+        gather(rows300[:, 2], last, 2, 0, P, gates_early[:])
+        gather(rows301[:, 2], last, 2, P, C, gates[:, P:C])
         quantise_g(packed20[:], 2, 0, C, "gates_early")
         for a in range(AT):
             first_product(2, 0, a, 0, last)
-        gather(rows30[:, 3, 0:P], last, 3, 0, P, gates_late[:])
-        gather(rows30[:, 3, P:C], last, 3, P, C, gates[:, P:C])
+        gather(rows300[:, 3], last, 3, 0, P, gates_late[:])
+        gather(rows301[:, 3], last, 3, P, C, gates[:, P:C])
         packed30 = new_packed(C, "packed30", 1)
-        for a in range(AT):
-            pack(packed30[:, P * a : P * (a + 1)], rows30[:, :, P * a : P * (a + 1)])
+        pack(packed30[:, 0:P], rows300[:])
+        pack(packed30[:, P:C], rows301[:])
+        packed21 = keep.tile([P, C, 4], BF16, name="rows301", align_bytes=64)
+        pack(packed21[:], rows[:, :, C:S])
         quantise_g(packed30[:, 0:P], last, 0, P)
         first_product(last, 0, 0, 0, last)
         quantise_g(packed30[:, P:C], last, P, C)
         first_product(last, 0, 1, 0, last)
         quantise_g(g_packed[0][:, C:S], 0, C, S, "gates_late")
         quantise_g(g_packed[1][:, C:S], 1, C, S, "gates_late")
-        quantise_g(packed21[:], 2, C, S, "gates_late")
         rows31 = keep.tile([P, 4, C], F32, name="rows3", align_bytes=64)
         for t in range(4):
             gather(rows31[:, t], last, t, C, S, gates[:, C:S])
+        quantise_g(packed21[:], 2, C, S, "dy32")
         masked_a3 = keep.tile([P, HP, 4, P], F32, name="dy33", align_bytes=64)
         for h in range(HP):
             nc.gpsimd.tensor_tensor(masked_a3[:, h], a3t[0, h][:, :, P:C], mask[0, 1, h][:], MULT)
@@ -407,11 +409,11 @@ def tile_moe_bdx_glu_relu_kernel(
         packed31 = keep.tile([P, C, 4], BF16, name="last_turn0", align_bytes=64)
         pack(packed31[:], rows31[:])
         relu_late = keep.tile([P, AT, P, 4], F32, name="rows3", align_bytes=64)
-        make_relu(1, 1, 1, relu_late[:, 1])
+        relu_and_mask(1, 1, 1, relu_late[:, 1])
         relu_and_mask(1, 0, 1, relu_late[:, 0])
-        for s in (2, 1, 0):
+        for s in range(last):
             for a in (1, 0):
-                first_product(s, 1, a, 2, last)
+                first_product(s, 1, a, 0, last)
 
         new_da(0, 0, "da00")
         make_da3(0, 0, 0)
@@ -432,7 +434,7 @@ def tile_moe_bdx_glu_relu_kernel(
         quantise_da_half(0, 1, 0, half0, codes01, scales01)
         quantise_da_half(0, 1, 1, half1, codes01, scales01)
 
-        first_product(last, 1, 1, 2, last, (1, 0))
+        first_product(last, 1, 1, 0, last, (1, 0))
         sums000 = second_product(0, 0, ("bank001",), 0, 1)
         copy_dx(0, 0, 0, sums000[0], "dx000")
         turn(1, 1, 1, None, "bank000")
@@ -448,14 +450,13 @@ def tile_moe_bdx_glu_relu_kernel(
             copy_dx(0, 1, kt, sums01[0][:, kt : kt + 1], f"dx01{kt}")
         relu_last = keep.tile([P, AT, P, 4], F32, name="dc01", align_bytes=64)
         make_relu(1, 1, 0, relu_last[:, 1])
-        first_product(last, 1, 0, 2, last, (1, 0))
+        first_product(last, 1, 0, 0, last, (1, 0))
         sorted10 = keep.tile([P, HP, 4, P], F32, name="turn110", align_bytes=64)
         turn(1, 0, 1, sorted10[:, 1])
         turn(1, 0, 0, sorted10[:, 0])
         make_relu(1, 0, 0, relu_last[:, 0])
-        make_mask(1, 0, 0)
-        for h in range(HP):
-            make_mask(1, 1, h, "turn110")
+        for a in range(AT):
+            make_mask(1, a, 0)
 
         new_da(1, 1, "mask00")
         make_da3_gpsimd(1, 1, 1)
@@ -472,14 +473,15 @@ def tile_moe_bdx_glu_relu_kernel(
         make_da3(1, 0, 0)
         apply_mask(1, 0)
         apply_mask(1, 1)
-        copy_dx(0, 1, KT - 1, sums01[0][:, KT - 1 : KT], "turn110")
+        copy_dx(0, 1, KT - 1, sums01[0][:, KT - 1 : KT], "mask11")
         quantise_da(1, 0)
         sums10 = second_product(1, 0, ("bank001", "bank010", "bank011"))
         quantise_da(1, 1)
         for kt in range(KT):
             copy_dx(1, 0, kt, sums10[kt], f"dx10{kt}")
-        sums11 = second_product(1, 1, ("bank000",))
-        copy_dx(1, 1, 0, sums11[0], "dx11")
+        sums11 = second_product(1, 1, ("bank000", "bank111", "bank101"))
+        for kt in range(KT):
+            copy_dx(1, 1, kt, sums11[kt], f"dx11{kt}")
         scatter(0, 1, KT - 1)
         for kt in range(KT):
             scatter(1, 0, kt)

@@ -80,6 +80,8 @@ def tile_moe_bdx_glu_relu_kernel(
 
         def load_dy(s):
             for t in range(4):
+                if (s, t) == (0, 3):
+                    load_a1(0, 0)
                 d = keep.tile([P, T], F32, name=f"dy{s}{t}", align_bytes=64)
                 nc.sync.dma_start(d[:], dy_rows[s, t])
                 if (s, t) == (0, 0):
@@ -124,7 +126,6 @@ def tile_moe_bdx_glu_relu_kernel(
             a3t[e, h] = rows
 
         load_dy(0)
-        load_a1(0, 0)
         load_dy(1)
         load_a1_both(1)
         load_dy(2)
@@ -288,6 +289,20 @@ def tile_moe_bdx_glu_relu_kernel(
 
         da_codes = {}
 
+        def quantise_da_by_w(e, a):
+            codes = keep.tile([P, 2 * HP * P], U32, name=f"dc{e}{a}", align_bytes=64)
+            scales = dpool.tile([P, 2 * HP * P], U8, name="ds", align_bytes=64)
+            for w in (1, 0):
+                both = slice(HP * P * w, HP * P * (w + 1))
+                nc.vector.quantize_mx(
+                    out=codes[:, both].bitcast(FP8X4),
+                    scales=scales[:, both],
+                    in_=da[e, a][:, w].rearrange("p h j t -> p (h j t)"),
+                )
+                for h in range(HP):
+                    cols = slice(P * (HP * w + h), P * (HP * w + h + 1))
+                    da_codes[e, a, w, h] = (codes[:, cols], scales[:, cols])
+
         def quantise_da(e, a):
             codes = keep.tile([P, 2 * HP * P], U32, name=f"dc{e}{a}", align_bytes=64)
             scales = dpool.tile([P, 2 * HP * P], U8, name="ds", align_bytes=64)
@@ -318,8 +333,11 @@ def tile_moe_bdx_glu_relu_kernel(
                 sums.append(b)
                 for within in range(per_bank):
                     kt = first_kt + per_bank * number + within
-                    for h in range(HP):
-                        for w in range(2):
+                    passes = [(w, h) for w in (1, 0) for h in range(HP)]
+                    if e == 0:
+                        passes = [(w, h) for h in range(HP) for w in range(2)]
+                    for w, h in passes:
+                        if True:
                             codes, scales = da_codes[e, a, w, h]
                             nc.tensor.matmul_mx(
                                 out=b[:, within],
@@ -327,8 +345,8 @@ def tile_moe_bdx_glu_relu_kernel(
                                 lhsT_scale=w13s[:, e * HP + h, w, P * kt : P * (kt + 1)],
                                 rhs=codes.bitcast(FP8X4),
                                 rhs_scale=scales,
-                                start=(h == 0 and w == 0),
-                                stop=(h == HP - 1 and w == 1),
+                                start=((w, h) == passes[0]),
+                                stop=((w, h) == passes[-1]),
                             )
             return sums
 
@@ -351,6 +369,8 @@ def tile_moe_bdx_glu_relu_kernel(
         nc.scalar.copy(gates_early[:], gates[:, 0:P])
         gates_late = placed.tile([P, P], F32, name="gates_late", align_bytes=64, offset=LATE)
         nc.scalar.copy(gates_late[:], gates[:, 0:P])
+        relu_and_mask(0, 0, 0)
+        relu_and_mask_rows(0, 1, 0)
         g_packed = {}
         for s in range(last):
             rows = gpool.tile([P, 4, S], F32, name="g_rows")
@@ -367,6 +387,7 @@ def tile_moe_bdx_glu_relu_kernel(
             if s < 2:
                 g_packed[s] = new_packed(S, "g_packed", 2)
                 pack(g_packed[s][:], rows[:])
+            if s == 1:
                 relu_and_mask(0, 0, s)
                 relu_and_mask_rows(0, 1, s)
         packed20 = new_packed(C, "packed20", 1)
@@ -446,7 +467,7 @@ def tile_moe_bdx_glu_relu_kernel(
         scatter(0, 0, 0)
         scatter(0, 0, 1)
         sums01 = second_product(0, 1, ("bank110",))
-        for kt in range(KT - 1):
+        for kt in range(KT):
             copy_dx(0, 1, kt, sums01[0][:, kt : kt + 1], f"dx01{kt}")
         relu_last = keep.tile([P, AT, P, 4], F32, name="dc01", align_bytes=64)
         make_relu(1, 1, 0, relu_last[:, 1])
@@ -464,7 +485,7 @@ def tile_moe_bdx_glu_relu_kernel(
         make_da1_gpsimd(1, 1, 0)
         make_da3_gpsimd(1, 1, 0)
         scatter(0, 0, 2)
-        for kt in range(KT - 1):
+        for kt in range(KT):
             scatter(0, 1, kt)
         new_da(1, 0, "dx010")
         make_da1(1, 0, 1)
@@ -472,17 +493,15 @@ def tile_moe_bdx_glu_relu_kernel(
         make_da1(1, 0, 0)
         make_da3(1, 0, 0)
         apply_mask(1, 0)
-        apply_mask(1, 1)
-        copy_dx(0, 1, KT - 1, sums01[0][:, KT - 1 : KT], "mask11")
-        quantise_da(1, 0)
+        quantise_da_by_w(1, 0)
         sums10 = second_product(1, 0, ("bank001", "bank010", "bank011"))
-        quantise_da(1, 1)
+        apply_mask(1, 1)
+        quantise_da_by_w(1, 1)
         for kt in range(KT):
             copy_dx(1, 0, kt, sums10[kt], f"dx10{kt}")
         sums11 = second_product(1, 1, ("bank000", "bank111", "bank101"))
         for kt in range(KT):
             copy_dx(1, 1, kt, sums11[kt], f"dx11{kt}")
-        scatter(0, 1, KT - 1)
         for kt in range(KT):
             scatter(1, 0, kt)
         for kt in range(KT):

@@ -11,7 +11,10 @@ HP = H // 512
 KT = K // P
 AT = C // P
 
-LATE = 4608
+A3_AT = 0
+DA_AT = A3_AT + C
+GATES_AT = 4608
+LATE_SCALES_AT = GATES_AT - 192
 
 FLOPS = 2 * S * N * H + 2 * 2 * S * H * K
 BYTES = 4 * (N * T + 2 * H * S + P * S + K * T) + E * (N * H + 2 * H * K) * 17 // 32 + 2 * S * 8
@@ -80,8 +83,8 @@ def tile_moe_bdx_glu_relu_kernel(
 
         def load_dy(s):
             for t in range(4):
-                if (s, t) == (0, 3):
-                    load_a1(0, 0)
+                if s < HP and t == 3:
+                    load_a1(0, s)
                 d = keep.tile([P, T], F32, name=f"dy{s}{t}", align_bytes=64)
                 nc.sync.dma_start(d[:], dy_rows[s, t])
                 if (s, t) == (0, 0):
@@ -111,15 +114,9 @@ def tile_moe_bdx_glu_relu_kernel(
             nc.sync.dma_start(rows[:], a1_rows[h][:, :, C * e : C * (e + 1)])
             a1t[e, h] = rows[:]
 
-        def load_a1_both(h):
-            rows = keep.tile([P, 4, S], F32, name=f"a1t{h}")
-            nc.sync.dma_start(rows[:], a1_rows[h])
-            for e in range(E):
-                a1t[e, h] = rows[:, :, C * e : C * (e + 1)]
-
         def load_a3(e, h):
             if (e, h) == (0, 1):
-                rows = placed.tile([P, 4, C], F32, name="a3t01", align_bytes=64, offset=0)
+                rows = placed.tile([P, 4, C], F32, name="a3t01", align_bytes=64, offset=A3_AT)
             else:
                 rows = keep.tile([P, 4, C], F32, name=f"a3t{e}{h}")
             nc.sync.dma_start(rows[:], a3_rows[h][:, :, C * e : C * (e + 1)])
@@ -127,7 +124,6 @@ def tile_moe_bdx_glu_relu_kernel(
 
         load_dy(0)
         load_dy(1)
-        load_a1_both(1)
         load_dy(2)
         for q in range(4):
             load_w2s(0, q)
@@ -143,6 +139,7 @@ def tile_moe_bdx_glu_relu_kernel(
             for q in range(4):
                 load_w13s(step, q)
         load_w2(1, 0)
+        load_a1(1, 1)
         load_w2(1, 1)
         load_w2(1, 2)
         load_w13(0, 0)
@@ -161,18 +158,17 @@ def tile_moe_bdx_glu_relu_kernel(
             if into is None:
                 own = keep.tile([P, P, 4], F32, name=f"relu{e}{a}{h}", align_bytes=64)
                 into = own[:]
-            r = into
-            relu1[e, a, h] = r
-            nc.scalar.activation(walk_packed(r, 4), walk_rows(a1t[e, h][:, :, P * a : P * (a + 1)], 4), RELU)
+            relu1[e, a, h] = into
+            nc.scalar.activation(walk_packed(into, 4), walk_rows(a1t[e, h][:, :, P * a : P * (a + 1)], 4), RELU)
 
-        def make_mask(e, a, h, buffer=None):
+        def make_mask(e, a, h):
             if (e, a) not in mask:
-                m = keep.tile([P, HP, P, 4], BF16, name=buffer or f"mask{e}{a}", align_bytes=64)
+                m = keep.tile([P, HP, P, 4], BF16, name=f"mask{e}{a}", align_bytes=64)
                 mask[e, a] = m
             nc.scalar.activation(mask[e, a][:, h], relu1[e, a, h], SIGN)
 
-        def relu_and_mask(e, a, h, buffer=None):
-            make_relu(e, a, h, buffer)
+        def relu_and_mask(e, a, h, into=None):
+            make_relu(e, a, h, into)
             make_mask(e, a, h)
 
         def relu_and_mask_rows(e, a, h):
@@ -199,10 +195,11 @@ def tile_moe_bdx_glu_relu_kernel(
 
         def quantise_g(packed, s, lo, hi, buffer=None):
             codes = keep.tile([P, hi - lo], U32, name=f"gc{s}_{lo}", align_bytes=64)
-            if buffer == "mask00":
-                scales = placed.tile([P, hi - lo], U8, name="gs_last", align_bytes=64, offset=0)
+            if buffer == "a3t01":
+                scales = placed.tile([P, hi - lo], U8, name="gs_last", align_bytes=64, offset=A3_AT)
             elif buffer == "gates_late":
-                scales = placed.tile([P, hi - lo], U8, name=f"gs{s}_{lo}", align_bytes=64, offset=LATE - 192 + C * s)
+                at = LATE_SCALES_AT + C * s
+                scales = placed.tile([P, hi - lo], U8, name=f"gs{s}_{lo}", align_bytes=64, offset=at)
             else:
                 scales = keep.tile([P, hi - lo], U8, name=buffer or f"gs{s}_{lo}", align_bytes=64)
             nc.vector.quantize_mx(
@@ -213,10 +210,11 @@ def tile_moe_bdx_glu_relu_kernel(
                 g_scales[s, first] = scales[:, first - lo : first - lo + P]
 
         bank = {}
+        last = NP - 1
 
-        def first_product(s, e, a, opens, closes, halves=(0, 1)):
+        def first_product(s, e, a, halves=(0, 1)):
             for h in halves:
-                if s == opens:
+                if s == 0:
                     b = psum.tile([P, 512], F32, name=f"bank{e}{a}{h}")
                     bank[e, a, h] = b
                 nc.tensor.matmul_mx(
@@ -225,8 +223,8 @@ def tile_moe_bdx_glu_relu_kernel(
                     lhsT_scale=g_scales[s, C * e + P * a],
                     rhs=w2t[e, s][:, 1024 * h : 1024 * (h + 1)].bitcast(FP4X4),
                     rhs_scale=w2s[e][:, s, 512 * h : 512 * (h + 1)],
-                    start=(s == opens),
-                    stop=(s == closes),
+                    start=(s == 0),
+                    stop=(s == last),
                 )
 
         def turn(e, a, h, buffer=None, into=None):
@@ -247,8 +245,8 @@ def tile_moe_bdx_glu_relu_kernel(
         da = {}
 
         def new_da(e, a, buffer):
-            if buffer == "mask00":
-                packed = placed.tile([P, 2, HP, P, 4], BF16, name=f"da{e}{a}", align_bytes=64, offset=C)
+            if buffer == "half1":
+                packed = placed.tile([P, 2, HP, P, 4], BF16, name=f"da{e}{a}", align_bytes=64, offset=DA_AT)
             else:
                 packed = keep.tile([P, 2, HP, P, 4], BF16, name=buffer, align_bytes=64)
             da[e, a] = packed
@@ -327,27 +325,27 @@ def tile_moe_bdx_glu_relu_kernel(
 
         def second_product(e, a, banks, first_kt=0, count=KT):
             per_bank = count // len(banks)
+            if e == 0:
+                passes = [(w, h) for h in range(HP) for w in range(2)]
+            else:
+                passes = [(w, h) for w in (1, 0) for h in range(HP)]
             sums = []
             for number, name in enumerate(banks):
                 b = psum.tile([P, per_bank, P], F32, name=name)
                 sums.append(b)
                 for within in range(per_bank):
                     kt = first_kt + per_bank * number + within
-                    passes = [(w, h) for w in (1, 0) for h in range(HP)]
-                    if e == 0:
-                        passes = [(w, h) for h in range(HP) for w in range(2)]
                     for w, h in passes:
-                        if True:
-                            codes, scales = da_codes[e, a, w, h]
-                            nc.tensor.matmul_mx(
-                                out=b[:, within],
-                                lhsT=w13[e, w][:, h, 2 * P * kt : 2 * P * (kt + 1)].bitcast(FP4X4),
-                                lhsT_scale=w13s[:, e * HP + h, w, P * kt : P * (kt + 1)],
-                                rhs=codes.bitcast(FP8X4),
-                                rhs_scale=scales,
-                                start=((w, h) == passes[0]),
-                                stop=((w, h) == passes[-1]),
-                            )
+                        codes, scales = da_codes[e, a, w, h]
+                        nc.tensor.matmul_mx(
+                            out=b[:, within],
+                            lhsT=w13[e, w][:, h, 2 * P * kt : 2 * P * (kt + 1)].bitcast(FP4X4),
+                            lhsT_scale=w13s[:, e * HP + h, w, P * kt : P * (kt + 1)],
+                            rhs=codes.bitcast(FP8X4),
+                            rhs_scale=scales,
+                            start=((w, h) == passes[0]),
+                            stop=((w, h) == passes[-1]),
+                        )
             return sums
 
         dx = {}
@@ -363,11 +361,9 @@ def tile_moe_bdx_glu_relu_kernel(
             lo = (C * e + P * a) // 16
             nc.vector.tensor_copy(outs[kt][:].indirect(offsets[:, lo : lo + P // 16]), dx[e, a, kt])
 
-        last = NP - 1
-
         gates_early = keep.tile([P, P], F32, name="gates_early", align_bytes=64)
         nc.scalar.copy(gates_early[:], gates[:, 0:P])
-        gates_late = placed.tile([P, P], F32, name="gates_late", align_bytes=64, offset=LATE)
+        gates_late = placed.tile([P, P], F32, name="gates_late", align_bytes=64, offset=GATES_AT)
         nc.scalar.copy(gates_late[:], gates[:, 0:P])
         relu_and_mask(0, 0, 0)
         relu_and_mask_rows(0, 1, 0)
@@ -383,13 +379,13 @@ def tile_moe_bdx_glu_relu_kernel(
                 if t == 2 and s > 0:
                     quantise_g(g_packed[s - 1][:, 0:C], s - 1, 0, C, "dy21" if s == 2 else None)
                     for a in range(AT):
-                        first_product(s - 1, 0, a, 0, last)
+                        first_product(s - 1, 0, a)
             if s < 2:
                 g_packed[s] = new_packed(S, "g_packed", 2)
                 pack(g_packed[s][:], rows[:])
-            if s == 1:
-                relu_and_mask(0, 0, s)
-                relu_and_mask_rows(0, 1, s)
+            if s == 0:
+                relu_and_mask(0, 0, 1)
+                relu_and_mask_rows(0, 1, 1)
         packed20 = new_packed(C, "packed20", 1)
         pack(packed20[:], rows[:, :, 0:C])
 
@@ -402,7 +398,7 @@ def tile_moe_bdx_glu_relu_kernel(
         gather(rows301[:, 2], last, 2, P, C, gates[:, P:C])
         quantise_g(packed20[:], 2, 0, C, "gates_early")
         for a in range(AT):
-            first_product(2, 0, a, 0, last)
+            first_product(2, 0, a)
         gather(rows300[:, 3], last, 3, 0, P, gates_late[:])
         gather(rows301[:, 3], last, 3, P, C, gates[:, P:C])
         packed30 = new_packed(C, "packed30", 1)
@@ -411,9 +407,9 @@ def tile_moe_bdx_glu_relu_kernel(
         packed21 = keep.tile([P, C, 4], BF16, name="rows301", align_bytes=64)
         pack(packed21[:], rows[:, :, C:S])
         quantise_g(packed30[:, 0:P], last, 0, P)
-        first_product(last, 0, 0, 0, last)
+        first_product(last, 0, 0)
         quantise_g(packed30[:, P:C], last, P, C)
-        first_product(last, 0, 1, 0, last)
+        first_product(last, 0, 1)
         quantise_g(g_packed[0][:, C:S], 0, C, S, "gates_late")
         quantise_g(g_packed[1][:, C:S], 1, C, S, "gates_late")
         rows31 = keep.tile([P, 4, C], F32, name="rows3", align_bytes=64)
@@ -434,7 +430,7 @@ def tile_moe_bdx_glu_relu_kernel(
         relu_and_mask(1, 0, 1, relu_late[:, 0])
         for s in range(last):
             for a in (1, 0):
-                first_product(s, 1, a, 0, last)
+                first_product(s, 1, a)
 
         new_da(0, 0, "da00")
         make_da3(0, 0, 0)
@@ -445,8 +441,8 @@ def tile_moe_bdx_glu_relu_kernel(
         product_rows(half0[:, 1], 0, 1, 0, relu1[0, 1, 0])
         product_rows(half0[:, 0], 0, 1, 0, masked_a3[:, 0])
         apply_mask(0, 0)
-        quantise_g(packed31[:], last, C, S, "mask00")
-        half1 = placed.tile([P, 2, P, 4], BF16, name="half1", align_bytes=64, offset=C)
+        quantise_g(packed31[:], last, C, S, "a3t01")
+        half1 = placed.tile([P, 2, P, 4], BF16, name="half1", align_bytes=64, offset=DA_AT)
         quantise_da(0, 0)
         product_rows(half1[:, 1], 0, 1, 1, relu1[0, 1, 1])
         product_rows(half1[:, 0], 0, 1, 1, masked_a3[:, 1])
@@ -455,7 +451,7 @@ def tile_moe_bdx_glu_relu_kernel(
         quantise_da_half(0, 1, 0, half0, codes01, scales01)
         quantise_da_half(0, 1, 1, half1, codes01, scales01)
 
-        first_product(last, 1, 1, 0, last, (1, 0))
+        first_product(last, 1, 1, (1, 0))
         sums000 = second_product(0, 0, ("bank001",), 0, 1)
         copy_dx(0, 0, 0, sums000[0], "dx000")
         turn(1, 1, 1, None, "bank000")
@@ -471,7 +467,7 @@ def tile_moe_bdx_glu_relu_kernel(
             copy_dx(0, 1, kt, sums01[0][:, kt : kt + 1], f"dx01{kt}")
         relu_last = keep.tile([P, AT, P, 4], F32, name="dc01", align_bytes=64)
         make_relu(1, 1, 0, relu_last[:, 1])
-        first_product(last, 1, 0, 0, last, (1, 0))
+        first_product(last, 1, 0, (1, 0))
         sorted10 = keep.tile([P, HP, 4, P], F32, name="turn110", align_bytes=64)
         turn(1, 0, 1, sorted10[:, 1])
         turn(1, 0, 0, sorted10[:, 0])
@@ -479,7 +475,7 @@ def tile_moe_bdx_glu_relu_kernel(
         for a in range(AT):
             make_mask(1, a, 0)
 
-        new_da(1, 1, "mask00")
+        new_da(1, 1, "half1")
         make_da3_gpsimd(1, 1, 1)
         make_da1_gpsimd(1, 1, 1)
         make_da1_gpsimd(1, 1, 0)

@@ -11,11 +11,6 @@ HP = H // 512
 KT = K // P
 AT = C // P
 
-A3_AT = 0
-DA_AT = A3_AT + C
-GATES_AT = 4608
-LATE_SCALES_AT = GATES_AT - 192
-
 FLOPS = 2 * S * N * H + 2 * 2 * S * H * K
 BYTES = 4 * (N * T + 2 * H * S + P * S + K * T) + E * (N * H + 2 * H * K) * 17 // 32 + 2 * S * 8
 
@@ -28,8 +23,8 @@ U8 = mybir.dt.uint8
 FP8X4 = mybir.dt.float8_e4m3fn_x4
 FP4X4 = mybir.dt.float4_e2m1fn_x4
 MULT = mybir.AluOpType.mult
-RELU = mybir.ActivationFunctionType.Relu
-SIGN = mybir.ActivationFunctionType.Sign
+IS_GT = mybir.AluOpType.is_gt
+COPY = mybir.ActivationFunctionType.Copy
 
 
 def walk_rows(rows, run):
@@ -46,15 +41,10 @@ def tile_moe_bdx_glu_relu_kernel(
     nc = tc.nc
     with ExitStack() as ctx:
         keep = ctx.enter_context(tc.tile_pool(name="keep", bufs=1))
-        gpool = ctx.enter_context(tc.tile_pool(name="gpool", bufs=2))
-        dpool = ctx.enter_context(tc.tile_pool(name="dpool", bufs=3))
-        placed = ctx.enter_context(tc.tile_pool(name="placed", bufs=1))
         psum = ctx.enter_context(tc.psum_pool(name="psum", bufs=1))
 
         offsets = keep.tile([P, S // 16], U16, name="offsets")
         nc.sync.dma_start(offsets[:], offs)
-        gates = keep.tile([P, S], F32, name="gates")
-        nc.scalar.dma_start(gates[:, 0:P], gate[0:P, 0:P])
 
         ident = keep.tile([P, P], F32, name="ident")
         make_identity(nc, ident[:])
@@ -68,36 +58,44 @@ def tile_moe_bdx_glu_relu_kernel(
         outs = []
         for kt in range(KT):
             o = keep.tile([P, T], F32, name=f"out{kt}")
-            nc.gpsimd.memset(o[:], 0.0)
+            if kt == 0:
+                nc.vector.memset(o[:], 0.0)
+            elif kt == 1:
+                nc.scalar.activation(o[:], outs[0][:], COPY)
+            else:
+                nc.gpsimd.memset(o[:], 0.0)
             outs.append(o)
 
         dy_rows = dyT.rearrange("(s p t) u -> s t p u", s=NP, p=P, t=4)
-        a1_rows = a1.rearrange("(s p t) j -> s p t j", s=HP, p=P, t=4)
-        a3_rows = a3.rearrange("(s p t) j -> s p t j", s=HP, p=P, t=4)
+        a_rows = [x.rearrange("(s p t) j -> s p t j", s=HP, p=P, t=4) for x in (a1, a3)]
         w2s_rows = w2_scales.bitcast(I32).rearrange("e s (q r) i -> r q e s i", r=4)
+        w2_rows = w2_words.bitcast(I32).rearrange("e s p x -> e p s x")
         dy = {}
         w2t = {}
         w13 = {}
-        a1t = {}
-        a3t = {}
+        at = {}
+        gates = keep.tile([P, S], F32, name="gates", align_bytes=64)
 
-        def load_dy(s):
+        def load_dy(s, t):
+            d = keep.tile([P, T], F32, name=f"dy{s}{t}", align_bytes=64)
+            nc.sync.dma_start(d[:], dy_rows[s, t])
+            dy[s, t] = d[:]
+
+        def load_dy_pass(s):
+            d = keep.tile([P, 4, T], F32, name=f"dy{s}", align_bytes=64)
+            nc.sync.dma_start(d[:], dyT.rearrange("(s p t) u -> s p t u", s=NP, p=P, t=4)[s])
             for t in range(4):
-                if s < HP and t == 3:
-                    load_a1(0, s)
-                d = keep.tile([P, T], F32, name=f"dy{s}{t}", align_bytes=64)
-                nc.sync.dma_start(d[:], dy_rows[s, t])
-                if (s, t) == (0, 0):
-                    nc.sync.dma_start(gates[:, P:S], gate[0:P, P:S])
-                dy[s, t] = d
+                dy[s, t] = d[:, t]
 
-        def load_w2(e, s):
-            words = keep.tile([P, 2 * H], U8, name=f"w2t{e}{s}", align_bytes=64)
-            nc.sync.dma_start(words[:].bitcast(I32), w2_words.bitcast(I32)[e, s])
-            w2t[e, s] = words
+        def load_w2(e, pair):
+            words = keep.tile([P, 2, 2 * H], U8, name=f"w2t{e}{pair}", align_bytes=64)
+            nc.sync.dma_start(words[:].bitcast(I32), w2_rows[e][:, 2 * pair : 2 * pair + 2])
+            for u in range(2):
+                w2t[e, 2 * pair + u] = words[:, u]
 
-        def load_w2s(e, q):
-            nc.sync.dma_start(w2s[e][q:P:32].bitcast(I32), w2s_rows[q, :, e])
+        def load_w2s(e):
+            for q in range(4):
+                nc.sync.dma_start(w2s[e][q:P:32].bitcast(I32), w2s_rows[q, :, e])
 
         def load_w13(e, w):
             words = keep.tile([P, HP, 2 * K], U8, name=f"w13_{e}{w}", align_bytes=64)
@@ -105,401 +103,228 @@ def tile_moe_bdx_glu_relu_kernel(
             nc.sync.dma_start(words[:].bitcast(I32), source[e])
             w13[e, w] = words
 
-        def load_w13s(w, q):
+        def load_w13s(w):
             scale_rows = (w1_scales, w3_scales)[w].bitcast(I32).rearrange("e s (q r) k -> r q (e s) k", r=4)
-            nc.sync.dma_start(w13s[q:P:32, :, w].bitcast(I32), scale_rows[q])
-
-        def load_a1(e, h):
-            rows = keep.tile([P, 4, C], F32, name=f"a1t{e}{h}")
-            nc.sync.dma_start(rows[:], a1_rows[h][:, :, C * e : C * (e + 1)])
-            a1t[e, h] = rows[:]
-
-        def load_a3(e, h):
-            if (e, h) == (0, 1):
-                rows = placed.tile([P, 4, C], F32, name="a3t01", align_bytes=64, offset=A3_AT)
-            else:
-                rows = keep.tile([P, 4, C], F32, name=f"a3t{e}{h}")
-            nc.sync.dma_start(rows[:], a3_rows[h][:, :, C * e : C * (e + 1)])
-            a3t[e, h] = rows
-
-        load_dy(0)
-        load_dy(1)
-        load_dy(2)
-        for q in range(4):
-            load_w2s(0, q)
-        load_w2(0, 0)
-        load_dy(3)
-        load_w2(0, 1)
-        for step in range(2):
-            load_w2(0, 2 + step)
-            load_w2s(1, 2 * step)
-            load_w2s(1, 2 * step + 1)
-        for step in range(2):
-            load_a3(0, step)
             for q in range(4):
-                load_w13s(step, q)
+                nc.sync.dma_start(w13s[q:P:32, :, w].bitcast(I32), scale_rows[q])
+
+        def load_a(w, e, h):
+            rows = keep.tile([P, 4, C], F32, name=f"a{w}{e}{h}", align_bytes=64)
+            nc.sync.dma_start(rows[:], a_rows[w][h][:, :, C * e : C * (e + 1)])
+            at[w, e, h] = rows
+
+        for s in range(NP - 1):
+            for t in range(4):
+                load_dy(s, t)
+                if (s, t) == (0, 2):
+                    nc.sync.dma_start(gates[:], gate[0:P, :])
+        load_dy_pass(NP - 1)
+        load_w2s(0)
+        load_w2(0, 0)
+        load_w2(0, 1)
+        load_a(0, 0, 0)
+        load_a(0, 0, 1)
+        load_w2s(1)
         load_w2(1, 0)
-        load_a1(1, 1)
         load_w2(1, 1)
-        load_w2(1, 2)
-        load_w13(0, 0)
+        load_a(1, 0, 0)
+        load_a(1, 0, 1)
+        load_a(0, 1, 0)
+        load_a(0, 1, 1)
+        load_w13s(0)
+        load_w13s(1)
         load_w13(0, 1)
-        load_w2(1, 3)
-        load_a3(1, 1)
-        load_a1(1, 0)
-        load_a3(1, 0)
-        load_w13(1, 0)
+        load_w13(0, 0)
+        load_a(1, 1, 0)
+        load_a(1, 1, 1)
         load_w13(1, 1)
+        load_w13(1, 0)
 
-        relu1 = {}
-        mask = {}
-
-        def make_relu(e, a, h, into=None):
-            if into is None:
-                own = keep.tile([P, P, 4], F32, name=f"relu{e}{a}{h}", align_bytes=64)
-                into = own[:]
-            relu1[e, a, h] = into
-            nc.scalar.activation(walk_packed(into, 4), walk_rows(a1t[e, h][:, :, P * a : P * (a + 1)], 4), RELU)
-
-        def make_mask(e, a, h):
-            if (e, a) not in mask:
-                m = keep.tile([P, HP, P, 4], BF16, name=f"mask{e}{a}", align_bytes=64)
-                mask[e, a] = m
-            nc.scalar.activation(mask[e, a][:, h], relu1[e, a, h], SIGN)
-
-        def relu_and_mask(e, a, h, into=None):
-            make_relu(e, a, h, into)
-            make_mask(e, a, h)
-
-        def relu_and_mask_rows(e, a, h):
-            r = keep.tile([P, 4, P], F32, name=f"relu{e}{a}{h}", align_bytes=64)
-            nc.scalar.activation(r[:], a1t[e, h][:, :, P * a : P * (a + 1)], RELU)
-            relu1[e, a, h] = r[:]
-            m = keep.tile([P, 4, P], BF16, name=f"mask{e}{a}{h}", align_bytes=64)
-            nc.scalar.activation(m[:], r[:], SIGN)
-            mask[e, a, h] = m
-
-        def gather(rows, s, t, lo, hi, weights):
-            nc.vector.tensor_tensor(
-                rows, dy[s, t][:].indirect(offsets[:, lo // 16 : hi // 16]), weights, MULT
-            )
-
-        def new_packed(width, name, bufs):
-            return gpool.tile([P, width, 4], BF16, name=name, bufs=bufs, align_bytes=64)
-
-        def pack(packed, rows):
-            nc.scalar.copy(walk_packed(packed, 4), walk_rows(rows, 4))
-
-        g_codes = {}
-        g_scales = {}
-
-        def quantise_g(packed, s, lo, hi, buffer=None):
-            codes = keep.tile([P, hi - lo], U32, name=f"gc{s}_{lo}", align_bytes=64)
-            if buffer == "a3t01":
-                scales = placed.tile([P, hi - lo], U8, name="gs_last", align_bytes=64, offset=A3_AT)
-            elif buffer == "gates_late":
-                at = LATE_SCALES_AT + C * s
-                scales = placed.tile([P, hi - lo], U8, name=f"gs{s}_{lo}", align_bytes=64, offset=at)
+        def gather(engine, rows, s, t, lo, hi):
+            window = dy[s, t].indirect(offsets[:, lo // 16 : hi // 16])
+            if engine == "v":
+                nc.vector.tensor_copy(rows[:, t, lo:hi], window)
             else:
-                scales = keep.tile([P, hi - lo], U8, name=buffer or f"gs{s}_{lo}", align_bytes=64)
+                nc.scalar.activation(rows[:, t, lo:hi], window, COPY)
+
+        g_packed = {}
+
+        def gate_and_pack(rows, s, e):
+            packed = keep.tile([P, C, 4], BF16, name=f"gp{s}{e}", align_bytes=64)
+            cols = slice(C * e, C * (e + 1))
+            weights = gates[:, cols].rearrange("p (c r) -> p c r", r=2).unsqueeze(2).to_broadcast([P, C // 2, 4, 2])
+            nc.vector.tensor_tensor(walk_packed(packed[:], 2), walk_rows(rows[:, :, cols], 2), weights, MULT)
+            g_packed[s, e] = packed
+
+        g_mx = {}
+
+        def quantise_g(s, e):
+            codes = keep.tile([P, C], U32, name=f"gc{s}{e}", align_bytes=64)
+            scales = keep.tile([P, C], U8, name=f"gs{s}{e}", align_bytes=64)
             nc.vector.quantize_mx(
-                out=codes[:].bitcast(FP8X4), scales=scales[:], in_=packed.rearrange("p j t -> p (j t)")
+                out=codes[:].bitcast(FP8X4), scales=scales[:], in_=g_packed[s, e][:].rearrange("p j t -> p (j t)")
             )
-            for first in range(lo, hi, P):
-                g_codes[s, first] = codes[:, first - lo : first - lo + P]
-                g_scales[s, first] = scales[:, first - lo : first - lo + P]
+            g_mx[s, e] = (codes, scales)
 
         bank = {}
-        last = NP - 1
 
-        def first_product(s, e, a, halves=(0, 1)):
-            for h in halves:
-                if s == 0:
-                    b = psum.tile([P, 512], F32, name=f"bank{e}{a}{h}")
-                    bank[e, a, h] = b
-                nc.tensor.matmul_mx(
-                    out=bank[e, a, h][:],
-                    lhsT=g_codes[s, C * e + P * a].bitcast(FP8X4),
-                    lhsT_scale=g_scales[s, C * e + P * a],
-                    rhs=w2t[e, s][:, 1024 * h : 1024 * (h + 1)].bitcast(FP4X4),
-                    rhs_scale=w2s[e][:, s, 512 * h : 512 * (h + 1)],
-                    start=(s == 0),
-                    stop=(s == last),
-                )
+        def first_product(s, e):
+            codes, scales = g_mx[s, e]
+            for h in range(HP):
+                for a in range(AT):
+                    if s == 0:
+                        b = psum.tile([P, 512], F32, name=f"bank{e}{a}{h}")
+                        bank[e, a, h] = b
+                    nc.tensor.matmul_mx(
+                        out=bank[e, a, h][:],
+                        lhsT=codes[:, P * a : P * (a + 1)].bitcast(FP8X4),
+                        lhsT_scale=scales[:, P * a : P * (a + 1)],
+                        rhs=w2t[e, s][:, 1024 * h : 1024 * (h + 1)].bitcast(FP4X4),
+                        rhs_scale=w2s[e][:, s, 512 * h : 512 * (h + 1)],
+                        start=(s == 0),
+                        stop=(s == NP - 1),
+                    )
 
-        def turn(e, a, h, buffer=None, into=None):
-            if buffer is None:
-                own = dpool.tile([P, 4, P], F32, name="sorted_dh")
-                sorted_dh = own[:]
-            elif isinstance(buffer, str):
-                own = keep.tile([P, 4, P], F32, name=buffer, align_bytes=64)
-                sorted_dh = own[:]
-            else:
-                sorted_dh = buffer
-            nc.scalar.copy(sorted_dh, bank[e, a, h][:].rearrange("p (m t) -> p t m", t=4))
-            b = psum.tile([P, 4, P], F32, name=into or f"bank{e}{a}{h}")
+        def turn(e, a, h):
+            sorted_dh = keep.tile([P, 4, P], F32, name=f"sorted{a}{h}", align_bytes=64)
+            nc.scalar.copy(sorted_dh[:], bank[e, a, h][:].rearrange("p (m t) -> p t m", t=4))
+            b = psum.tile([P, 4, P], F32, name=f"bank0{a}{h}")
             for t in range(4):
                 nc.tensor.transpose(b[:, t, :], sorted_dh[:, t, :], ident[:])
             bank[e, a, h] = b
 
+        masked = {}
+
+        def mask_dh(e, a, h):
+            if a == 0:
+                m = keep.tile([P, 4, C], F32, name=f"masked{h}", align_bytes=64)
+                masked[e, h] = m
+            cols = slice(P * a, P * (a + 1))
+            nc.vector.scalar_tensor_tensor(
+                masked[e, h][:, :, cols], at[0, e, h][:, :, cols], 0.0, bank[e, a, h][:], IS_GT, MULT
+            )
+
         da = {}
 
-        def new_da(e, a, buffer):
-            if buffer == "half1":
-                packed = placed.tile([P, 2, HP, P, 4], BF16, name=f"da{e}{a}", align_bytes=64, offset=DA_AT)
-            else:
-                packed = keep.tile([P, 2, HP, P, 4], BF16, name=buffer, align_bytes=64)
-            da[e, a] = packed
-
-        def make_da1(e, a, h):
+        def product(e, h, w, lo=0, hi=C):
+            d = keep.tile([P, hi - lo, 4], BF16, name=f"da{e}{h}{w}_{lo}", align_bytes=64)
+            da[e, h, w, lo] = d
             nc.vector.tensor_tensor(
-                walk_packed(da[e, a][:, 0, h], 2),
-                walk_rows(bank[e, a, h][:], 2),
-                walk_rows(a3t[e, h][:, :, P * a : P * (a + 1)], 2),
+                walk_packed(d[:], 2),
+                walk_rows(masked[e, h][:, :, lo:hi], 2),
+                walk_rows(at[1 - w, e, h][:, :, lo:hi], 2),
                 MULT,
             )
 
-        def make_da3(e, a, h):
-            nc.vector.tensor_tensor(
-                da[e, a][:, 1, h], bank[e, a, h][:].rearrange("p t j -> p j t"), relu1[e, a, h], MULT
-            )
+        da_mx = {}
 
-        def product_rows(into, e, a, h, rows):
-            nc.vector.tensor_tensor(walk_packed(into, 2), walk_rows(bank[e, a, h][:], 2), walk_rows(rows, 2), MULT)
-
-        parked = {}
-
-        def park(e, a, h, buffer):
-            dh = keep.tile([P, P, 4], F32, name=buffer, align_bytes=64)
-            nc.scalar.copy(dh[:], bank[e, a, h][:].rearrange("p t j -> p j t"))
-            parked[h] = dh
-
-        def make_da1_gpsimd(e, a, h):
-            a3_packed = a3t[e, h][:, :, P * a : P * (a + 1)].rearrange("p t j -> p j t")
-            nc.gpsimd.tensor_tensor(da[e, a][:, 0, h], parked[h][:], a3_packed, MULT)
-
-        def make_da3_gpsimd(e, a, h):
-            nc.gpsimd.tensor_tensor(da[e, a][:, 1, h], parked[h][:], relu1[e, a, h], MULT)
-
-        def apply_mask(e, a):
-            da1 = da[e, a][:, 0]
-            nc.vector.tensor_tensor(da1, da1, mask[e, a][:], MULT)
-
-        da_codes = {}
-
-        def quantise_da_by_w(e, a):
-            codes = keep.tile([P, 2 * HP * P], U32, name=f"dc{e}{a}", align_bytes=64)
-            scales = dpool.tile([P, 2 * HP * P], U8, name="ds", align_bytes=64)
-            for w in (1, 0):
-                both = slice(HP * P * w, HP * P * (w + 1))
-                nc.vector.quantize_mx(
-                    out=codes[:, both].bitcast(FP8X4),
-                    scales=scales[:, both],
-                    in_=da[e, a][:, w].rearrange("p h j t -> p (h j t)"),
-                )
-                for h in range(HP):
-                    cols = slice(P * (HP * w + h), P * (HP * w + h + 1))
-                    da_codes[e, a, w, h] = (codes[:, cols], scales[:, cols])
-
-        def quantise_da(e, a):
-            codes = keep.tile([P, 2 * HP * P], U32, name=f"dc{e}{a}", align_bytes=64)
-            scales = dpool.tile([P, 2 * HP * P], U8, name="ds", align_bytes=64)
+        def quantise_da(e, h, w, lo=0, hi=C):
+            codes = keep.tile([P, hi - lo], U32, name=f"dc{e}{h}{w}_{lo}", align_bytes=64)
+            scales = keep.tile([P, hi - lo], U8, name=f"ds{e}{h}{w}_{lo}", align_bytes=64)
             nc.vector.quantize_mx(
-                out=codes[:].bitcast(FP8X4),
-                scales=scales[:],
-                in_=da[e, a][:].rearrange("p w h j t -> p (w h j t)"),
+                out=codes[:].bitcast(FP8X4), scales=scales[:], in_=da[e, h, w, lo][:].rearrange("p j t -> p (j t)")
             )
-            for w in range(2):
-                for h in range(HP):
-                    cols = slice(P * (HP * w + h), P * (HP * w + h + 1))
-                    da_codes[e, a, w, h] = (codes[:, cols], scales[:, cols])
-
-        def quantise_da_half(e, a, h, half, codes, scales):
-            both = slice(2 * P * h, 2 * P * (h + 1))
-            nc.vector.quantize_mx(
-                out=codes[:, both].bitcast(FP8X4), scales=scales[:, both], in_=half[:].rearrange("p w j t -> p (w j t)")
-            )
-            for w in range(2):
-                cols = slice(P * (2 * h + w), P * (2 * h + w + 1))
-                da_codes[e, a, w, h] = (codes[:, cols], scales[:, cols])
-
-        def second_product(e, a, banks, first_kt=0, count=KT):
-            per_bank = count // len(banks)
-            if e == 0:
-                passes = [(w, h) for h in range(HP) for w in range(2)]
-            else:
-                passes = [(w, h) for w in (1, 0) for h in range(HP)]
-            sums = []
-            for number, name in enumerate(banks):
-                b = psum.tile([P, per_bank, P], F32, name=name)
-                sums.append(b)
-                for within in range(per_bank):
-                    kt = first_kt + per_bank * number + within
-                    for w, h in passes:
-                        codes, scales = da_codes[e, a, w, h]
-                        nc.tensor.matmul_mx(
-                            out=b[:, within],
-                            lhsT=w13[e, w][:, h, 2 * P * kt : 2 * P * (kt + 1)].bitcast(FP4X4),
-                            lhsT_scale=w13s[:, e * HP + h, w, P * kt : P * (kt + 1)],
-                            rhs=codes.bitcast(FP8X4),
-                            rhs_scale=scales,
-                            start=((w, h) == passes[0]),
-                            stop=((w, h) == passes[-1]),
-                        )
-            return sums
+            if hi - lo == C:
+                da_mx[e, h, w, 0, C] = (codes[:], scales[:])
+            for first in range(lo, hi, P):
+                cols = slice(first - lo, first - lo + P)
+                da_mx[e, h, w, first, first + P] = (codes[:, cols], scales[:, cols])
 
         dx = {}
 
-        def copy_dx(e, a, first_kt, bank_tile, buffer):
-            count = bank_tile.shape[1]
-            d = keep.tile([P, count, P], F32, name=buffer, align_bytes=64)
-            nc.scalar.copy(d[:], bank_tile[:])
-            for within in range(count):
-                dx[e, a, first_kt + within] = d[:, within]
+        def second_product(e, kts, name, buffer, lo=0, hi=C, engine="s"):
+            b = psum.tile([P, len(kts), hi - lo], F32, name=name)
+            passes = [(w, h) for w in (1, 0) for h in range(HP)]
+            for within, kt in enumerate(kts):
+                for w, h in passes:
+                    codes, scales = da_mx[e, h, w, lo, hi]
+                    nc.tensor.matmul_mx(
+                        out=b[:, within],
+                        lhsT=w13[e, w][:, h, 2 * P * kt : 2 * P * (kt + 1)].bitcast(FP4X4),
+                        lhsT_scale=w13s[:, e * HP + h, w, P * kt : P * (kt + 1)],
+                        rhs=codes.bitcast(FP8X4),
+                        rhs_scale=scales,
+                        start=((w, h) == passes[0]),
+                        stop=((w, h) == passes[-1]),
+                    )
+            d = keep.tile([P, len(kts), hi - lo], F32, name=buffer, align_bytes=64)
+            if engine == "v":
+                nc.vector.tensor_copy(d[:], b[:])
+            else:
+                nc.scalar.copy(d[:], b[:])
+            for within, kt in enumerate(kts):
+                dx[e, kt, lo, hi] = d[:, within]
 
-        def scatter(e, a, kt):
-            lo = (C * e + P * a) // 16
-            nc.vector.tensor_copy(outs[kt][:].indirect(offsets[:, lo : lo + P // 16]), dx[e, a, kt])
+        def scatter(engine, e, kt, lo, hi):
+            window = outs[kt][:].indirect(offsets[:, (C * e + lo) // 16 : (C * e + hi) // 16])
+            if engine == "v":
+                nc.vector.tensor_copy(window, dx[e, kt, lo, hi])
+            else:
+                nc.scalar.activation(window, dx[e, kt, lo, hi], COPY)
 
-        gates_early = keep.tile([P, P], F32, name="gates_early", align_bytes=64)
-        nc.scalar.copy(gates_early[:], gates[:, 0:P])
-        gates_late = placed.tile([P, P], F32, name="gates_late", align_bytes=64, offset=GATES_AT)
-        nc.scalar.copy(gates_late[:], gates[:, 0:P])
-        relu_and_mask(0, 0, 0)
-        relu_and_mask_rows(0, 1, 0)
-        g_packed = {}
+        vector_gathers = [(0, 1, 0), (0, 1, 1), (0, 3, 0), (0, 3, 1), (1, 3, 0), (1, 3, 1), (2, 3, 1)]
+        last = NP - 1
         for s in range(last):
-            rows = gpool.tile([P, 4, S], F32, name="g_rows")
+            rows = keep.tile([P, 4, S], F32, name=f"rows{s}", align_bytes=64)
             for t in range(4):
-                if (s, t) == (0, 0):
-                    gather(rows[:, t, 0:P], s, t, 0, P, gates[:, 0:P])
-                    gather(rows[:, t, P:S], s, t, P, S, gates[:, P:S])
+                if (s, t, 1) in vector_gathers:
+                    for e in range(E):
+                        gather("v" if (s, t, e) in vector_gathers else "s", rows, s, t, C * e, C * (e + 1))
                 else:
-                    gather(rows[:, t], s, t, 0, S, gates[:])
-                if t == 2 and s > 0:
-                    quantise_g(g_packed[s - 1][:, 0:C], s - 1, 0, C, "dy21" if s == 2 else None)
-                    for a in range(AT):
-                        first_product(s - 1, 0, a)
-            if s < 2:
-                g_packed[s] = new_packed(S, "g_packed", 2)
-                pack(g_packed[s][:], rows[:])
-            if s == 0:
-                relu_and_mask(0, 0, 1)
-                relu_and_mask_rows(0, 1, 1)
-        packed20 = new_packed(C, "packed20", 1)
-        pack(packed20[:], rows[:, :, 0:C])
+                    gather("s", rows, s, t, 0, S)
+            for e in range(E):
+                gate_and_pack(rows[:], s, e)
+            for e in range(E):
+                quantise_g(s, e)
+            first_product(s, 0)
+        rows = keep.tile([P, 4, S], F32, name="rows3", align_bytes=64)
+        for e in range(E):
+            for t in range(4):
+                gather("s", rows, last, t, C * e, C * (e + 1))
+            gate_and_pack(rows[:], last, e)
+            quantise_g(last, e)
+        first_product(last, 0)
 
-        rows300 = keep.tile([P, 4, P], F32, name="rows3", align_bytes=64)
-        rows301 = keep.tile([P, 4, P], F32, name="rows301", align_bytes=64)
-        for t in range(2):
-            gather(rows300[:, t], last, t, 0, P, gates[:, 0:P])
-            gather(rows301[:, t], last, t, P, C, gates[:, P:C])
-        gather(rows300[:, 2], last, 2, 0, P, gates_early[:])
-        gather(rows301[:, 2], last, 2, P, C, gates[:, P:C])
-        quantise_g(packed20[:], 2, 0, C, "gates_early")
-        for a in range(AT):
-            first_product(2, 0, a)
-        gather(rows300[:, 3], last, 3, 0, P, gates_late[:])
-        gather(rows301[:, 3], last, 3, P, C, gates[:, P:C])
-        packed30 = new_packed(C, "packed30", 1)
-        pack(packed30[:, 0:P], rows300[:])
-        pack(packed30[:, P:C], rows301[:])
-        packed21 = keep.tile([P, C, 4], BF16, name="rows301", align_bytes=64)
-        pack(packed21[:], rows[:, :, C:S])
-        quantise_g(packed30[:, 0:P], last, 0, P)
-        first_product(last, 0, 0)
-        quantise_g(packed30[:, P:C], last, P, C)
-        first_product(last, 0, 1)
-        quantise_g(g_packed[0][:, C:S], 0, C, S, "gates_late")
-        quantise_g(g_packed[1][:, C:S], 1, C, S, "gates_late")
-        rows31 = keep.tile([P, 4, C], F32, name="rows3", align_bytes=64)
-        for t in range(4):
-            gather(rows31[:, t], last, t, C, S, gates[:, C:S])
-        quantise_g(packed21[:], 2, C, S, "dy32")
-        masked_a3 = keep.tile([P, HP, 4, P], F32, name="dy33", align_bytes=64)
-        for h in range(HP):
-            nc.gpsimd.tensor_tensor(masked_a3[:, h], a3t[0, h][:, :, P:C], mask[0, 1, h][:], MULT)
-        turn(0, 0, 0)
-        turn(0, 0, 1)
-        turn(0, 1, 0, "last_turn0")
-        turn(0, 1, 1)
-        packed31 = keep.tile([P, C, 4], BF16, name="last_turn0", align_bytes=64)
-        pack(packed31[:], rows31[:])
-        relu_late = keep.tile([P, AT, P, 4], F32, name="rows3", align_bytes=64)
-        relu_and_mask(1, 1, 1, relu_late[:, 1])
-        relu_and_mask(1, 0, 1, relu_late[:, 0])
-        for s in range(last):
-            for a in (1, 0):
-                first_product(s, 1, a)
+        def turns(e):
+            for h in range(HP):
+                for a in range(AT):
+                    turn(e, a, h)
 
-        new_da(0, 0, "da00")
-        make_da3(0, 0, 0)
-        make_da1(0, 0, 0)
-        make_da3(0, 0, 1)
-        make_da1(0, 0, 1)
-        half0 = keep.tile([P, 2, P, 4], BF16, name="relu001", align_bytes=64)
-        product_rows(half0[:, 1], 0, 1, 0, relu1[0, 1, 0])
-        product_rows(half0[:, 0], 0, 1, 0, masked_a3[:, 0])
-        apply_mask(0, 0)
-        quantise_g(packed31[:], last, C, S, "a3t01")
-        half1 = placed.tile([P, 2, P, 4], BF16, name="half1", align_bytes=64, offset=DA_AT)
-        quantise_da(0, 0)
-        product_rows(half1[:, 1], 0, 1, 1, relu1[0, 1, 1])
-        product_rows(half1[:, 0], 0, 1, 1, masked_a3[:, 1])
-        codes01 = keep.tile([P, 2 * HP * P], U32, name="dc01", align_bytes=64)
-        scales01 = dpool.tile([P, 2 * HP * P], U8, name="ds", align_bytes=64)
-        quantise_da_half(0, 1, 0, half0, codes01, scales01)
-        quantise_da_half(0, 1, 1, half1, codes01, scales01)
+        def products(e):
+            for h in range(HP):
+                for a in range(AT):
+                    mask_dh(e, a, h)
+            product(e, 0, 1)
+            product(e, 1, 1)
+            quantise_da(e, 0, 1)
+            product(e, 0, 0)
+            quantise_da(e, 1, 1)
+            if e == 0:
+                product(e, 1, 0)
+                quantise_da(e, 0, 0)
+                quantise_da(e, 1, 0)
+            else:
+                product(e, 1, 0, 0, P)
+                quantise_da(e, 0, 0)
+                product(e, 1, 0, P, C)
+                quantise_da(e, 1, 0, 0, P)
+                quantise_da(e, 1, 0, P, C)
 
-        first_product(last, 1, 1, (1, 0))
-        sums000 = second_product(0, 0, ("bank001",), 0, 1)
-        copy_dx(0, 0, 0, sums000[0], "dx000")
-        turn(1, 1, 1, None, "bank000")
-        sums001 = second_product(0, 0, ("bank010",), 1, KT - 1)
-        turn(1, 1, 0, "turn110", "bank111")
-        park(1, 1, 1, "park1")
-        copy_dx(0, 0, 1, sums001[0], "dx001")
-        park(1, 1, 0, "dc00")
-        scatter(0, 0, 0)
-        scatter(0, 0, 1)
-        sums01 = second_product(0, 1, ("bank110",))
+        turns(0)
+        products(0)
+        for s in range(NP):
+            first_product(s, 1)
+        turns(1)
+        second_product(0, (0, 1), "bank111", "sorted11")
+        second_product(0, (2,), "bank101", "sorted01")
         for kt in range(KT):
-            copy_dx(0, 1, kt, sums01[0][:, kt : kt + 1], f"dx01{kt}")
-        relu_last = keep.tile([P, AT, P, 4], F32, name="dc01", align_bytes=64)
-        make_relu(1, 1, 0, relu_last[:, 1])
-        first_product(last, 1, 0, (1, 0))
-        sorted10 = keep.tile([P, HP, 4, P], F32, name="turn110", align_bytes=64)
-        turn(1, 0, 1, sorted10[:, 1])
-        turn(1, 0, 0, sorted10[:, 0])
-        make_relu(1, 0, 0, relu_last[:, 0])
-        for a in range(AT):
-            make_mask(1, a, 0)
-
-        new_da(1, 1, "half1")
-        make_da3_gpsimd(1, 1, 1)
-        make_da1_gpsimd(1, 1, 1)
-        make_da1_gpsimd(1, 1, 0)
-        make_da3_gpsimd(1, 1, 0)
-        scatter(0, 0, 2)
+            scatter("s", 0, kt, 0, C)
+        products(1)
         for kt in range(KT):
-            scatter(0, 1, kt)
-        new_da(1, 0, "dx010")
-        make_da1(1, 0, 1)
-        make_da3(1, 0, 1)
-        make_da1(1, 0, 0)
-        make_da3(1, 0, 0)
-        apply_mask(1, 0)
-        quantise_da_by_w(1, 0)
-        sums10 = second_product(1, 0, ("bank001", "bank010", "bank011"))
-        apply_mask(1, 1)
-        quantise_da_by_w(1, 1)
+            second_product(1, (kt,), ("bank100", "bank110", "bank000")[kt], f"dx10{kt}", 0, P)
         for kt in range(KT):
-            copy_dx(1, 0, kt, sums10[kt], f"dx10{kt}")
-        sums11 = second_product(1, 1, ("bank000", "bank111", "bank101"))
+            second_product(1, (kt,), ("bank010", "bank001", "bank011")[kt], f"dx11{kt}", P, C, "v")
         for kt in range(KT):
-            copy_dx(1, 1, kt, sums11[kt], f"dx11{kt}")
-        for kt in range(KT):
-            scatter(1, 0, kt)
-        for kt in range(KT):
-            scatter(1, 1, kt)
+            scatter("s", 1, kt, 0, P)
+            scatter("v", 1, kt, P, C)
             nc.sync.dma_start(out[P * kt : P * (kt + 1), :], outs[kt][:])

@@ -24,6 +24,8 @@ FP8X4 = mybir.dt.float8_e4m3fn_x4
 FP4X4 = mybir.dt.float4_e2m1fn_x4
 MULT = mybir.AluOpType.mult
 IS_GT = mybir.AluOpType.is_gt
+RELU = mybir.ActivationFunctionType.Relu
+SIGN = mybir.ActivationFunctionType.Sign
 COPY = mybir.ActivationFunctionType.Copy
 
 
@@ -116,7 +118,7 @@ def tile_moe_bdx_glu_relu_kernel(
         for s in range(NP - 1):
             for t in range(4):
                 load_dy(s, t)
-                if (s, t) == (0, 2):
+                if (s, t) == (0, 3):
                     nc.sync.dma_start(gates[:], gate[0:P, :])
         load_dy_pass(NP - 1)
         load_w2s(0)
@@ -188,7 +190,7 @@ def tile_moe_bdx_glu_relu_kernel(
         def turn(e, a, h):
             sorted_dh = keep.tile([P, 4, P], F32, name=f"sorted{a}{h}", align_bytes=64)
             nc.scalar.copy(sorted_dh[:], bank[e, a, h][:].rearrange("p (m t) -> p t m", t=4))
-            b = psum.tile([P, 4, P], F32, name=f"bank0{a}{h}")
+            b = psum.tile([P, 4, P], F32, name=f"bank{e}{a}{h}")
             for t in range(4):
                 nc.tensor.transpose(b[:, t, :], sorted_dh[:, t, :], ident[:])
             bank[e, a, h] = b
@@ -232,21 +234,19 @@ def tile_moe_bdx_glu_relu_kernel(
 
         dx = {}
 
-        def second_product(e, kts, name, buffer, lo=0, hi=C, engine="s"):
-            b = psum.tile([P, len(kts), hi - lo], F32, name=name)
-            passes = [(w, h) for w in (1, 0) for h in range(HP)]
-            for within, kt in enumerate(kts):
-                for w, h in passes:
-                    codes, scales = da_mx[e, h, w, lo, hi]
-                    nc.tensor.matmul_mx(
-                        out=b[:, within],
-                        lhsT=w13[e, w][:, h, 2 * P * kt : 2 * P * (kt + 1)].bitcast(FP4X4),
-                        lhsT_scale=w13s[:, e * HP + h, w, P * kt : P * (kt + 1)],
-                        rhs=codes.bitcast(FP8X4),
-                        rhs_scale=scales,
-                        start=((w, h) == passes[0]),
-                        stop=((w, h) == passes[-1]),
-                    )
+        def second_pass(sums, e, kt, w, h, lo, hi, start, stop):
+            codes, scales = da_mx[e, h, w, lo, hi]
+            nc.tensor.matmul_mx(
+                out=sums,
+                lhsT=w13[e, w][:, h, 2 * P * kt : 2 * P * (kt + 1)].bitcast(FP4X4),
+                lhsT_scale=w13s[:, e * HP + h, w, P * kt : P * (kt + 1)],
+                rhs=codes.bitcast(FP8X4),
+                rhs_scale=scales,
+                start=start,
+                stop=stop,
+            )
+
+        def copy_dx(e, kts, b, buffer, lo, hi, engine):
             d = keep.tile([P, len(kts), hi - lo], F32, name=buffer, align_bytes=64)
             if engine == "v":
                 nc.vector.tensor_copy(d[:], b[:])
@@ -262,7 +262,7 @@ def tile_moe_bdx_glu_relu_kernel(
             else:
                 nc.scalar.activation(window, dx[e, kt, lo, hi], COPY)
 
-        vector_gathers = [(0, 1, 0), (0, 1, 1), (0, 3, 0), (0, 3, 1), (1, 3, 0), (1, 3, 1), (2, 3, 1)]
+        vector_gathers = [(0, t, 1) for t in range(4)] + [(1, 3, 0), (1, 3, 1), (2, 3, 0), (2, 3, 1)]
         last = NP - 1
         for s in range(last):
             rows = keep.tile([P, 4, S], F32, name=f"rows{s}", align_bytes=64)
@@ -290,41 +290,79 @@ def tile_moe_bdx_glu_relu_kernel(
                 for a in range(AT):
                     turn(e, a, h)
 
-        def products(e):
+        def masks(e):
             for h in range(HP):
                 for a in range(AT):
                     mask_dh(e, a, h)
-            product(e, 0, 1)
-            product(e, 1, 1)
-            quantise_da(e, 0, 1)
-            product(e, 0, 0)
-            quantise_da(e, 1, 1)
-            if e == 0:
-                product(e, 1, 0)
-                quantise_da(e, 0, 0)
-                quantise_da(e, 1, 0)
-            else:
-                product(e, 1, 0, 0, P)
-                quantise_da(e, 0, 0)
-                product(e, 1, 0, P, C)
-                quantise_da(e, 1, 0, 0, P)
-                quantise_da(e, 1, 0, P, C)
+
+        def bank_products(h, w, factor):
+            d = keep.tile([P, C, 4], BF16, name=f"da0{h}{w}_0", align_bytes=64)
+            da[0, h, w, 0] = d
+            for a in range(AT):
+                cols = slice(P * a, P * (a + 1))
+                nc.vector.tensor_tensor(
+                    walk_packed(d[:, cols], 2), walk_rows(bank[0, a, h][:], 2), walk_rows(factor[:, :, cols], 2), MULT
+                )
 
         turns(0)
-        products(0)
+        relu1 = keep.tile([P, 4, C], F32, name="relu1", align_bytes=64)
+        nc.scalar.activation(relu1[:], at[0, 0, 1][:], RELU)
+        mask = keep.tile([P, C, 4], BF16, name="mask", align_bytes=64)
+        nc.scalar.activation(walk_packed(mask[:], 4), walk_rows(relu1[:], 4), SIGN)
+        mask_dh(0, 0, 0)
+        mask_dh(0, 1, 0)
+        bank_products(1, 1, relu1[:])
+        product(0, 0, 1)
+        quantise_da(0, 1, 1)
+        product(0, 0, 0)
+        quantise_da(0, 0, 1)
+        bank_products(1, 0, at[1, 0, 1][:])
+        quantise_da(0, 0, 0)
+        nc.vector.tensor_tensor(da[0, 1, 0, 0][:], da[0, 1, 0, 0][:], mask[:], MULT)
+        quantise_da(0, 1, 0)
         for s in range(NP):
             first_product(s, 1)
         turns(1)
-        second_product(0, (0, 1), "bank111", "sorted11")
-        second_product(0, (2,), "bank101", "sorted01")
+        sums0 = []
+        for kt in range(KT):
+            b = psum.tile([P, 1, C], F32, name=("bank000", "bank010", "bank001")[kt])
+            sums0.append(b)
+        for w in (1, 0):
+            for kt in range(KT):
+                for h in range(HP):
+                    second_pass(sums0[kt][:, 0], 0, kt, w, h, 0, C, (w, h) == (1, 0), (w, h) == (0, 1))
+        for kt in range(KT):
+            copy_dx(0, (kt,), sums0[kt], ("sorted11", "sorted01", "sorted10")[kt], 0, C, "s")
         for kt in range(KT):
             scatter("s", 0, kt, 0, C)
-        products(1)
-        for kt in range(KT):
-            second_product(1, (kt,), ("bank100", "bank110", "bank000")[kt], f"dx10{kt}", 0, P)
-        for kt in range(KT):
-            second_product(1, (kt,), ("bank010", "bank001", "bank011")[kt], f"dx11{kt}", P, C, "v")
+        masks(1)
+        product(1, 0, 1)
+        product(1, 1, 1)
+        quantise_da(1, 0, 1)
+        product(1, 0, 0)
+        quantise_da(1, 1, 1)
+        product(1, 1, 0, 0, P)
+        quantise_da(1, 0, 0)
+        quantise_da(1, 1, 0, 0, P)
+        product(1, 1, 0, P, C)
+        quantise_da(1, 1, 0, P, C)
+        last_sums = []
+        for a in range(AT):
+            b = psum.tile([P, KT, P], F32, name=("bank100", "bank110")[a])
+            last_sums.append(b)
+        for w in (1, 0):
+            for a in range(AT):
+                for h in range(HP):
+                    for kt in range(KT):
+                        first = (w, h, kt) == (1, 0, 0)
+                        final = (w, h, kt) == (0, HP - 1, KT - 1)
+                        second_pass(last_sums[a][:, kt], 1, kt, w, h, P * a, P * (a + 1), first, final)
+        for a in range(AT):
+            copy_dx(1, range(KT), last_sums[a], f"dx1{a}", P * a, P * (a + 1), "sv"[a])
         for kt in range(KT):
             scatter("s", 1, kt, 0, P)
-            scatter("v", 1, kt, P, C)
+        scatter("v", 1, 0, P, C)
+        scatter("v", 1, 1, P, C)
+        scatter("v", 1, 2, P, C)
+        for kt in range(KT):
             nc.sync.dma_start(out[P * kt : P * (kt + 1), :], outs[kt][:])

@@ -76,7 +76,8 @@ def tile_moe_bdx_glu_relu_kernel(
         w2t = {}
         w13 = {}
         at = {}
-        gates = keep.tile([P, S], F32, name="gates", align_bytes=64)
+        gate_cols = keep.tile([P, 4], F32, name="gate_cols", align_bytes=64)
+        nc.scalar.dma_start(gate_cols[:], gate[0].rearrange("(j a) -> j a", a=4))
 
         def load_dy(s, t):
             d = keep.tile([P, T], F32, name=f"dy{s}{t}", align_bytes=64)
@@ -89,11 +90,11 @@ def tile_moe_bdx_glu_relu_kernel(
             for t in range(4):
                 dy[s, t] = d[:, t]
 
-        def load_w2(e, pair):
-            words = keep.tile([P, 2, 2 * H], U8, name=f"w2t{e}{pair}", align_bytes=64)
-            nc.sync.dma_start(words[:].bitcast(I32), w2_rows[e][:, 2 * pair : 2 * pair + 2])
-            for u in range(2):
-                w2t[e, 2 * pair + u] = words[:, u]
+        def load_w2(e, first, end):
+            words = keep.tile([P, end - first, 2 * H], U8, name=f"w2t{e}{first}", align_bytes=64)
+            nc.sync.dma_start(words[:].bitcast(I32), w2_rows[e][:, first:end])
+            for s in range(first, end):
+                w2t[e, s] = words[:, s - first]
 
         def load_w2s(e):
             for q in range(4):
@@ -118,17 +119,15 @@ def tile_moe_bdx_glu_relu_kernel(
         for s in range(NP - 1):
             for t in range(4):
                 load_dy(s, t)
-                if (s, t) == (0, 3):
-                    nc.sync.dma_start(gates[:], gate[0:P, :])
         load_dy_pass(NP - 1)
         load_w2s(0)
-        load_w2(0, 0)
-        load_w2(0, 1)
+        for s in range(NP):
+            load_w2(0, s, s + 1)
         load_a(0, 0, 0)
         load_a(0, 0, 1)
         load_w2s(1)
-        load_w2(1, 0)
-        load_w2(1, 1)
+        load_w2(1, 0, 2)
+        load_w2(1, 2, 4)
         load_a(1, 0, 0)
         load_a(1, 0, 1)
         load_a(0, 1, 0)
@@ -148,6 +147,11 @@ def tile_moe_bdx_glu_relu_kernel(
                 nc.vector.tensor_copy(rows[:, t, lo:hi], window)
             else:
                 nc.scalar.activation(rows[:, t, lo:hi], window, COPY)
+
+        gates_psum = psum.tile([P, P, 4], F32, name="bank111")
+        for a in range(4):
+            nc.tensor.transpose(gates_psum[:, :, a], gate_cols[:, a : a + 1].to_broadcast([P, P]), ident[:])
+        gates = gates_psum[:].rearrange("p j a -> p (j a)")
 
         g_packed = {}
 
@@ -262,7 +266,7 @@ def tile_moe_bdx_glu_relu_kernel(
             else:
                 nc.scalar.activation(window, dx[e, kt, lo, hi], COPY)
 
-        vector_gathers = [(0, t, 1) for t in range(4)] + [(1, 3, 0), (1, 3, 1), (2, 3, 0), (2, 3, 1)]
+        vector_gathers = [(0, t, 1) for t in range(4)] + [(1, 0, 0), (1, 0, 1), (2, 3, 0), (2, 3, 1)]
         last = NP - 1
         for s in range(last):
             rows = keep.tile([P, 4, S], F32, name=f"rows{s}", align_bytes=64)

@@ -128,12 +128,12 @@ def tile_moe_bdx_glu_relu_kernel(
         load_w2s(1)
         load_w2(1, 0, 2)
         load_w2(1, 2, 4)
+        load_w13s(1)
         load_a(1, 0, 0)
         load_a(1, 0, 1)
         load_a(0, 1, 0)
         load_a(0, 1, 1)
         load_w13s(0)
-        load_w13s(1)
         load_w13(0, 1)
         load_w13(0, 0)
         load_a(1, 1, 0)

from contextlib import ExitStack

import concourse.mybir as mybir
from concourse.masks import make_identity

E, C, T, K, H, N = 2, 256, 640, 384, 1024, 2048
S = E * C
P = 128
NP = N // 512
HP = H // 512
KT = K // P
AT = C // P

FLOPS = 2 * S * N * H + 2 * 2 * S * H * K
BYTES = 4 * (N * T + 2 * H * S + P * S + K * T) + E * (N * H + 2 * H * K) * 17 // 32 + 2 * S * 8

F32 = mybir.dt.float32
BF16 = mybir.dt.bfloat16
I32 = mybir.dt.int32
U32 = mybir.dt.uint32
U16 = mybir.dt.uint16
U8 = mybir.dt.uint8
FP8X4 = mybir.dt.float8_e4m3fn_x4
FP4X4 = mybir.dt.float4_e2m1fn_x4
MULT = mybir.AluOpType.mult
IS_GT = mybir.AluOpType.is_gt
RELU = mybir.ActivationFunctionType.Relu
SIGN = mybir.ActivationFunctionType.Sign
COPY = mybir.ActivationFunctionType.Copy


def walk_rows(rows, run):
    return rows.rearrange("p t (c r) -> p c t r", r=run)


def walk_packed(packed, run):
    return packed.rearrange("p (c r) t -> p c t r", r=run)


def tile_moe_bdx_glu_relu_kernel(
    tc, dyT, a1, a3, w2_words, w2_scales, w1_words, w1_scales, w3_words, w3_scales, gate, offs, out
):
    nc = tc.nc
    with ExitStack() as ctx:
        keep = ctx.enter_context(tc.tile_pool(name="keep", bufs=1))
        psum = ctx.enter_context(tc.psum_pool(name="psum", bufs=1))

        offsets = keep.tile([P, S // 16], U16, name="offsets")
        nc.sync.dma_start(offsets[:], offs)

        ident = keep.tile([P, P], F32, name="ident")
        make_identity(nc, ident[:])
        w2s = []
        for e in range(E):
            plane = keep.tile([P, NP, H], U8, name=f"w2s{e}", align_bytes=64)
            nc.gpsimd.memset(plane[:].bitcast(I32), 0)
            w2s.append(plane)
        w13s = keep.tile([P, E * HP, 2, K], U8, name="w13s", align_bytes=64)
        nc.gpsimd.memset(w13s[:].bitcast(I32), 0)
        outs = []
        for kt in range(KT):
            o = keep.tile([P, T], F32, name=f"out{kt}")
            if kt == 0:
                nc.vector.memset(o[:], 0.0)
            elif kt == 1:
                nc.scalar.activation(o[:], outs[0][:], COPY)
            else:
                nc.gpsimd.memset(o[:], 0.0)
            outs.append(o)

        dy_rows = dyT.rearrange("(s p t) u -> s t p u", s=NP, p=P, t=4)
        a_rows = [x.rearrange("(s p t) j -> s p t j", s=HP, p=P, t=4) for x in (a1, a3)]
        w2s_rows = w2_scales.bitcast(I32).rearrange("e s (q r) i -> r q e s i", r=4)
        w2_rows = w2_words.bitcast(I32).rearrange("e s p x -> e p s x")
        dy = {}
        w2t = {}
        w13 = {}
        at = {}
        gate_cols = keep.tile([P, 4], F32, name="gate_cols", align_bytes=64)
        nc.scalar.dma_start(gate_cols[:], gate[0].rearrange("(j a) -> j a", a=4))

        def load_dy(s, t):
            d = keep.tile([P, T], F32, name=f"dy{s}{t}", align_bytes=64)
            nc.sync.dma_start(d[:], dy_rows[s, t])
            dy[s, t] = d[:]

        def load_dy_pass(s):
            d = keep.tile([P, 4, T], F32, name=f"dy{s}", align_bytes=64)
            nc.sync.dma_start(d[:], dyT.rearrange("(s p t) u -> s p t u", s=NP, p=P, t=4)[s])
            for t in range(4):
                dy[s, t] = d[:, t]

        def load_w2(e, first, end):
            words = keep.tile([P, end - first, 2 * H], U8, name=f"w2t{e}{first}", align_bytes=64)
            nc.sync.dma_start(words[:].bitcast(I32), w2_rows[e][:, first:end])
            for s in range(first, end):
                w2t[e, s] = words[:, s - first]

        def load_w2s(e):
            for q in range(4):
                nc.sync.dma_start(w2s[e][q:P:32].bitcast(I32), w2s_rows[q, :, e])

        def load_w13(e, w):
            words = keep.tile([P, HP, 2 * K], U8, name=f"w13_{e}{w}", align_bytes=64)
            source = (w1_words, w3_words)[w].bitcast(I32).rearrange("e s p x -> e p s x")
            nc.sync.dma_start(words[:].bitcast(I32), source[e])
            w13[e, w] = words

        def load_w13s(w):
            scale_rows = (w1_scales, w3_scales)[w].bitcast(I32).rearrange("e s (q r) k -> r q (e s) k", r=4)
            for q in range(4):
                nc.sync.dma_start(w13s[q:P:32, :, w].bitcast(I32), scale_rows[q])

        def load_a(w, e, h):
            rows = keep.tile([P, 4, C], F32, name=f"a{w}{e}{h}", align_bytes=64)
            nc.sync.dma_start(rows[:], a_rows[w][h][:, :, C * e : C * (e + 1)])
            at[w, e, h] = rows

        for s in range(NP - 1):
            for t in range(4):
                load_dy(s, t)
        load_dy_pass(NP - 1)
        load_w2s(0)
        for s in range(NP):
            load_w2(0, s, s + 1)
        load_a(0, 0, 0)
        load_a(0, 0, 1)
        load_w2s(1)
        load_w2(1, 0, 2)
        load_w2(1, 2, 4)
        load_w13s(1)
        load_a(1, 0, 0)
        load_a(1, 0, 1)
        load_a(0, 1, 0)
        load_a(0, 1, 1)
        load_w13s(0)
        load_w13(0, 1)
        load_w13(0, 0)
        load_a(1, 1, 0)
        load_a(1, 1, 1)
        load_w13(1, 1)
        load_w13(1, 0)

        def gather(engine, rows, s, t, lo, hi):
            window = dy[s, t].indirect(offsets[:, lo // 16 : hi // 16])
            if engine == "v":
                nc.vector.tensor_copy(rows[:, t, lo:hi], window)
            else:
                nc.scalar.activation(rows[:, t, lo:hi], window, COPY)

        gates_psum = psum.tile([P, P, 4], F32, name="bank111")
        for a in range(4):
            nc.tensor.transpose(gates_psum[:, :, a], gate_cols[:, a : a + 1].to_broadcast([P, P]), ident[:])
        gates = gates_psum[:].rearrange("p j a -> p (j a)")

        g_packed = {}

        def gate_and_pack(rows, s, e):
            packed = keep.tile([P, C, 4], BF16, name=f"gp{s}{e}", align_bytes=64)
            cols = slice(C * e, C * (e + 1))
            weights = gates[:, cols].rearrange("p (c r) -> p c r", r=2).unsqueeze(2).to_broadcast([P, C // 2, 4, 2])
            nc.vector.tensor_tensor(walk_packed(packed[:], 2), walk_rows(rows[:, :, cols], 2), weights, MULT)
            g_packed[s, e] = packed

        g_mx = {}

        def quantise_g(s, e):
            codes = keep.tile([P, C], U32, name=f"gc{s}{e}", align_bytes=64)
            scales = keep.tile([P, C], U8, name=f"gs{s}{e}", align_bytes=64)
            nc.vector.quantize_mx(
                out=codes[:].bitcast(FP8X4), scales=scales[:], in_=g_packed[s, e][:].rearrange("p j t -> p (j t)")
            )
            g_mx[s, e] = (codes, scales)

        bank = {}

        def first_product(s, e):
            codes, scales = g_mx[s, e]
            for h in range(HP):
                for a in range(AT):
                    if s == 0:
                        b = psum.tile([P, 512], F32, name=f"bank{e}{a}{h}")
                        bank[e, a, h] = b
                    nc.tensor.matmul_mx(
                        out=bank[e, a, h][:],
                        lhsT=codes[:, P * a : P * (a + 1)].bitcast(FP8X4),
                        lhsT_scale=scales[:, P * a : P * (a + 1)],
                        rhs=w2t[e, s][:, 1024 * h : 1024 * (h + 1)].bitcast(FP4X4),
                        rhs_scale=w2s[e][:, s, 512 * h : 512 * (h + 1)],
                        start=(s == 0),
                        stop=(s == NP - 1),
                    )

        def turn(e, a, h):
            sorted_dh = keep.tile([P, 4, P], F32, name=f"sorted{a}{h}", align_bytes=64)
            nc.scalar.copy(sorted_dh[:], bank[e, a, h][:].rearrange("p (m t) -> p t m", t=4))
            b = psum.tile([P, 4, P], F32, name=f"bank{e}{a}{h}")
            for t in range(4):
                nc.tensor.transpose(b[:, t, :], sorted_dh[:, t, :], ident[:])
            bank[e, a, h] = b

        masked = {}

        def mask_dh(e, a, h):
            if a == 0:
                m = keep.tile([P, 4, C], F32, name=f"masked{h}", align_bytes=64)
                masked[e, h] = m
            cols = slice(P * a, P * (a + 1))
            nc.vector.scalar_tensor_tensor(
                masked[e, h][:, :, cols], at[0, e, h][:, :, cols], 0.0, bank[e, a, h][:], IS_GT, MULT
            )

        da = {}

        def product(e, h, w, lo=0, hi=C):
            d = keep.tile([P, hi - lo, 4], BF16, name=f"da{e}{h}{w}_{lo}", align_bytes=64)
            da[e, h, w, lo] = d
            nc.vector.tensor_tensor(
                walk_packed(d[:], 2),
                walk_rows(masked[e, h][:, :, lo:hi], 2),
                walk_rows(at[1 - w, e, h][:, :, lo:hi], 2),
                MULT,
            )

        da_mx = {}

        def quantise_da(e, h, w, lo=0, hi=C):
            codes = keep.tile([P, hi - lo], U32, name=f"dc{e}{h}{w}_{lo}", align_bytes=64)
            scales = keep.tile([P, hi - lo], U8, name=f"ds{e}{h}{w}_{lo}", align_bytes=64)
            nc.vector.quantize_mx(
                out=codes[:].bitcast(FP8X4), scales=scales[:], in_=da[e, h, w, lo][:].rearrange("p j t -> p (j t)")
            )
            if hi - lo == C:
                da_mx[e, h, w, 0, C] = (codes[:], scales[:])
            for first in range(lo, hi, P):
                cols = slice(first - lo, first - lo + P)
                da_mx[e, h, w, first, first + P] = (codes[:, cols], scales[:, cols])

        dx = {}

        def second_pass(sums, e, kt, w, h, lo, hi, start, stop):
            codes, scales = da_mx[e, h, w, lo, hi]
            nc.tensor.matmul_mx(
                out=sums,
                lhsT=w13[e, w][:, h, 2 * P * kt : 2 * P * (kt + 1)].bitcast(FP4X4),
                lhsT_scale=w13s[:, e * HP + h, w, P * kt : P * (kt + 1)],
                rhs=codes.bitcast(FP8X4),
                rhs_scale=scales,
                start=start,
                stop=stop,
            )

        def copy_dx(e, kts, b, buffer, lo, hi, engine):
            d = keep.tile([P, len(kts), hi - lo], F32, name=buffer, align_bytes=64)
            if engine == "v":
                nc.vector.tensor_copy(d[:], b[:])
            else:
                nc.scalar.copy(d[:], b[:])
            for within, kt in enumerate(kts):
                dx[e, kt, lo, hi] = d[:, within]

        def scatter(engine, e, kt, lo, hi):
            window = outs[kt][:].indirect(offsets[:, (C * e + lo) // 16 : (C * e + hi) // 16])
            if engine == "v":
                nc.vector.tensor_copy(window, dx[e, kt, lo, hi])
            else:
                nc.scalar.activation(window, dx[e, kt, lo, hi], COPY)

        vector_gathers = [(0, t, 1) for t in range(4)] + [(1, 0, 0), (1, 0, 1), (2, 3, 0), (2, 3, 1)]
        last = NP - 1
        for s in range(last):
            rows = keep.tile([P, 4, S], F32, name=f"rows{s}", align_bytes=64)
            for t in range(4):
                if (s, t, 1) in vector_gathers:
                    for e in range(E):
                        gather("v" if (s, t, e) in vector_gathers else "s", rows, s, t, C * e, C * (e + 1))
                else:
                    gather("s", rows, s, t, 0, S)
            for e in range(E):
                gate_and_pack(rows[:], s, e)
            for e in range(E):
                quantise_g(s, e)
            first_product(s, 0)
        rows = keep.tile([P, 4, S], F32, name="rows3", align_bytes=64)
        for e in range(E):
            for t in range(4):
                gather("s", rows, last, t, C * e, C * (e + 1))
            gate_and_pack(rows[:], last, e)
            quantise_g(last, e)
        first_product(last, 0)

        def turns(e):
            for h in range(HP):
                for a in range(AT):
                    turn(e, a, h)

        def masks(e):
            for h in range(HP):
                for a in range(AT):
                    mask_dh(e, a, h)

        def bank_products(h, w, factor):
            d = keep.tile([P, C, 4], BF16, name=f"da0{h}{w}_0", align_bytes=64)
            da[0, h, w, 0] = d
            for a in range(AT):
                cols = slice(P * a, P * (a + 1))
                nc.vector.tensor_tensor(
                    walk_packed(d[:, cols], 2), walk_rows(bank[0, a, h][:], 2), walk_rows(factor[:, :, cols], 2), MULT
                )

        turns(0)
        relu1 = keep.tile([P, 4, C], F32, name="relu1", align_bytes=64)
        nc.scalar.activation(relu1[:], at[0, 0, 1][:], RELU)
        mask = keep.tile([P, C, 4], BF16, name="mask", align_bytes=64)
        nc.scalar.activation(walk_packed(mask[:], 4), walk_rows(relu1[:], 4), SIGN)
        mask_dh(0, 0, 0)
        mask_dh(0, 1, 0)
        bank_products(1, 1, relu1[:])
        product(0, 0, 1)
        quantise_da(0, 1, 1)
        product(0, 0, 0)
        quantise_da(0, 0, 1)
        bank_products(1, 0, at[1, 0, 1][:])
        quantise_da(0, 0, 0)
        nc.vector.tensor_tensor(da[0, 1, 0, 0][:], da[0, 1, 0, 0][:], mask[:], MULT)
        quantise_da(0, 1, 0)
        for s in range(NP):
            first_product(s, 1)
        turns(1)
        sums0 = []
        for kt in range(KT):
            b = psum.tile([P, 1, C], F32, name=("bank000", "bank010", "bank001")[kt])
            sums0.append(b)
        for w in (1, 0):
            for kt in range(KT):
                for h in range(HP):
                    second_pass(sums0[kt][:, 0], 0, kt, w, h, 0, C, (w, h) == (1, 0), (w, h) == (0, 1))
        for kt in range(KT):
            copy_dx(0, (kt,), sums0[kt], ("sorted11", "sorted01", "sorted10")[kt], 0, C, "s")
        for kt in range(KT):
            scatter("s", 0, kt, 0, C)
        masks(1)
        product(1, 0, 1)
        product(1, 1, 1)
        quantise_da(1, 0, 1)
        product(1, 0, 0)
        quantise_da(1, 1, 1)
        product(1, 1, 0, 0, P)
        quantise_da(1, 0, 0)
        quantise_da(1, 1, 0, 0, P)
        product(1, 1, 0, P, C)
        quantise_da(1, 1, 0, P, C)
        last_sums = []
        for a in range(AT):
            b = psum.tile([P, KT, P], F32, name=("bank100", "bank110")[a])
            last_sums.append(b)
        for w in (1, 0):
            for a in range(AT):
                for h in range(HP):
                    for kt in range(KT):
                        first = (w, h, kt) == (1, 0, 0)
                        final = (w, h, kt) == (0, HP - 1, KT - 1)
                        second_pass(last_sums[a][:, kt], 1, kt, w, h, P * a, P * (a + 1), first, final)
        for a in range(AT):
            copy_dx(1, range(KT), last_sums[a], f"dx1{a}", P * a, P * (a + 1), "sv"[a])
        for kt in range(KT):
            scatter("s", 1, kt, 0, P)
        scatter("v", 1, 0, P, C)
        scatter("v", 1, 1, P, C)
        scatter("v", 1, 2, P, C)
        for kt in range(KT):
            nc.sync.dma_start(out[P * kt : P * (kt + 1), :], outs[kt][:])
